import numpy as np
import ml_dtypes


def mxq(x, axis, fmt="e4m3"):
    dtype, down = {"e4m3": (ml_dtypes.float8_e4m3fn, 7), "e5m2": (ml_dtypes.float8_e5m2, 14)}[fmt]
    v = np.moveaxis(np.asarray(x, np.float32).astype(ml_dtypes.bfloat16).astype(np.float64), axis, -1)
    blocks = v.reshape(v.shape[:-1] + (-1, 32))
    amax = np.abs(blocks).max(-1, keepdims=True)
    byte = np.maximum(np.where(amax > 0, np.frexp(amax)[1] - 1 + 127, 0) - down, 1)
    scale = np.exp2(byte - 127.0)
    codes = (blocks / scale).astype(np.float32).astype(dtype).astype(np.float64)
    return np.moveaxis((codes * scale).reshape(v.shape), -1, axis)


WIDE = False


def mx_kscale(k):
    if not WIDE:
        return np.ones(k)
    levels = np.array([10, -10, 5, -5, 0])
    if k % 512:
        return np.exp2(np.random.permutation(np.resize(levels, k // 32))).repeat(32)
    a = np.empty((k // 512, 16))
    for p in range(k // 512):
        a[p, :8] = np.random.permutation(np.resize(levels, 8))
        for g in range(8):
            far = levels[np.abs(levels - a[p, g]) >= 10]
            a[p, g + 8] = far[np.random.randint(len(far))]
    return np.exp2(a.ravel()).repeat(32)


BF16 = ml_dtypes.bfloat16


def bf(x):
    return np.asarray(x, np.float32).astype(BF16)


def f64(x):
    return np.asarray(x).astype(np.float64)


E, K, D, C, NB = 256, 16, 512, 128, 8
NBC = NB * C


def silu(v):
    return v / (1.0 + np.exp(-v))


def draw0():
    s = mx_kscale(D)
    t = mx_kscale(NBC)
    m_kj = bf(np.random.standard_normal((E, K, D)) * s)
    m_ji = bf(np.random.standard_normal((E, D)))
    sbf = bf(np.random.standard_normal((E, K, NB)))
    w_down = bf(np.random.standard_normal((D, C)) / np.sqrt(D) / s[:, None])
    gain = bf((1.0 + 0.1 * np.random.standard_normal(NBC)) * t)
    w_bil = bf(np.random.standard_normal((NBC, D)) * 2.0 / np.sqrt(NBC) / t[:, None])
    return {"m_kj": m_kj, "m_ji": m_ji, "sbf": sbf, "w_down": w_down, "gain": gain, "w_bil": w_bil}


def core(m_kj, m_ji, sbf, w_down, gain, w_bil):
    m_kj, m_ji, sbf, w_down, gain, w_bil = f64(m_kj), f64(m_ji), f64(sbf), f64(w_down), f64(gain), f64(w_bil)
    e, k, _ = m_kj.shape
    nbc = gain.shape[0]
    x = silu(mxq(m_kj, 2, "e4m3") @ mxq(w_down, 0, "e4m3"))
    q = (sbf[:, :, :, None] * x[:, :, None, :]).reshape(e, k, nbc)
    p = q * gain
    t = silu(mxq(p, 2, "e4m3") @ mxq(w_bil, 0, "e4m3"))
    agg = np.sum(t, axis=1) / np.sqrt(k)
    return m_ji + agg


def e4m3fn_bytes(y):
    return np.clip(np.asarray(y, np.float64), -448.0, 448.0).astype(np.float32).astype(ml_dtypes.float8_e4m3fn).view(np.uint8)


def e4m3fn_values(b):
    return np.asarray(b, np.uint8).view(ml_dtypes.float8_e4m3fn).astype(np.float64)


def setup_inputs():
    d = draw0()
    x0 = np.asarray(d['m_kj']).astype(np.float64)
    s = (np.max(np.abs(x0), axis=(0, 1), keepdims=True) / 448.0).astype(np.float32)
    out = {}
    for k, v in d.items():
        if k == 'm_kj':
            out['m_kj_bytes'] = e4m3fn_bytes(x0 / s.astype(np.float64))
            out['m_kj_scale'] = s
        else:
            out[k] = v
    return out


def reference(m_kj_bytes, m_kj_scale, m_ji, sbf, w_down, gain, w_bil):
    return core(e4m3fn_values(m_kj_bytes) * m_kj_scale.astype(np.float64), m_ji, sbf, w_down, gain, w_bil)

@@ -1,0 +1,403 @@
+from contextlib import ExitStack
+
+import concourse.mybir as mybir
+from concourse.masks import make_identity
+
+E, K, D, C, NB = 256, 16, 512, 128, 8
+NBC = NB * C
+P = 128
+FLOPS = 2 * E * K * D * C + 2 * E * K * NBC * D
+
+F32 = mybir.dt.float32
+BF16 = mybir.dt.bfloat16
+U32 = mybir.dt.uint32
+U8 = mybir.dt.uint8
+FP8 = mybir.dt.float8_e4m3fn
+FP8X4 = mybir.dt.float8_e4m3fn_x4
+MULT = mybir.AluOpType.mult
+ADD = mybir.AluOpType.add
+SILU = mybir.ActivationFunctionType.Silu
+
+TILES = 32
+HALF = 16
+M_CHUNKS = [[0], [1]] + [[t, t + 1] for t in range(2, TILES, 2)]
+P_CHUNKS = [[t, t + 1] for t in range(0, TILES - 2, 2)] + [[TILES - 2], [TILES - 1]]
+OFFLOAD = [t for t in range(10, TILES, 2)]
+LOADS = [(0, 2), (2, 4), (4, 8), (8, 12), (12, 16), (16, 20), (20, 24), (24, 28), (28, 32)]
+
+
+def tile_dimenettripletbilinear_kernel(tc, m_kj_bytes, m_kj_scale, m_ji, sbf, w_down, gain, w_bil, out):
+    nc = tc.nc
+    with ExitStack() as ctx:
+        const = ctx.enter_context(tc.tile_pool(name="const", bufs=1))
+        work = ctx.enter_context(tc.tile_pool(name="work", bufs=2))
+        psum = ctx.enter_context(tc.psum_pool(name="psum", bufs=1))
+        ctx.enter_context(tc.manual_schedule())
+
+        mbytes = {}
+
+        def load_bytes(t0, t1):
+            t_t = const.tile([P, (t1 - t0) * D], U8, name="mbytes%d" % t0, align_bytes=64)
+            h = t0 // HALF
+            nc.sync.dma_start(
+                out=t_t[:], in_=m_kj_bytes[h * P:(h + 1) * P, t0 - h * HALF:t1 - h * HALF, :].rearrange("e k d -> e (k d)")
+            )
+            for t in range(t0, t1):
+                mbytes[t] = t_t[:, (t - t0) * D:(t - t0 + 1) * D]
+
+        g_raw = const.tile([1, NBC], BF16, name="g_raw", align_bytes=64)
+        nc.sync.dma_start(out=g_raw[:], in_=gain.unsqueeze(0))
+        scale_bc = const.tile([P, D], F32, name="scale_bc", align_bytes=64)
+        nc.sync.dma_start(out=scale_bc[:], in_=m_kj_scale.rearrange("a b k -> (a b k)").partition_broadcast(P))
+        load_bytes(*LOADS[0])
+        wd_raw = const.tile([P, 4, C], BF16, name="wd_raw", align_bytes=64)
+        nc.sync.dma_start(out=wd_raw[:], in_=w_down.rearrange("(p j) c -> p j c", j=4))
+        sbf_raw = const.tile([P, 2, K * NB], BF16, name="sbf_raw", align_bytes=64)
+        nc.sync.dma_start(out=sbf_raw[:], in_=sbf.rearrange("(h e) k n -> e h (k n)", e=P))
+        load_bytes(*LOADS[1])
+        wb_raw = const.tile([P, 2, 4, D], BF16, name="wb_raw", align_bytes=64)
+        wb_hbm = w_bil.rearrange("(g p j) d -> g p j d", g=2, j=4)
+        for g in range(2):
+            nc.sync.dma_start(out=wb_raw[:, g], in_=wb_hbm[g])
+        for t0, t1 in LOADS[2:]:
+            load_bytes(t0, t1)
+        mji = const.tile([P, 2, D], BF16, name="mji", align_bytes=64)
+        nc.sync.dma_start(out=mji[:], in_=m_ji.rearrange("(h e) d -> e h d", e=P))
+
+        warm = const.tile([P, 1], F32, name="warm")
+        nc.vector.memset(warm[:], 0.0)
+        warm2 = const.tile([P, 1], F32, name="warm2")
+        nc.scalar.activation(out=warm2[:], in_=warm[:], func=SILU)
+        ident = const.tile([P, P], F32, name="ident", align_bytes=64)
+        make_identity(nc, ident[:])
+        ones = const.tile([P, 512], BF16, name="ones", align_bytes=64)
+        nc.gpsimd.memset(ones[:], 1.0)
+        g_zero = const.tile([P, NBC], BF16, name="g_zero", align_bytes=64)
+        nc.gpsimd.memset(g_zero[:], 0.0)
+        for u in range(2):
+            nc.scalar.copy(
+                out=g_zero[0:1, :].rearrange("o (n u i e) -> o u n i e", u=2, i=32, e=2)[:, u],
+                in_=g_raw[:].rearrange("o (n i u e) -> o u n i e", u=2, i=32, e=2)[:, u],
+            )
+        sbf_f = const.tile([P, 2 * K * NB], F32, name="sbf_f", align_bytes=64)
+        nc.scalar.copy(out=sbf_f[:], in_=sbf_raw[:].rearrange("p h k -> p (h k)"))
+
+        wd_grp = const.tile([P, C, 4], BF16, name="wd_grp", align_bytes=64)
+        wd_codes = const.tile([P, C], U32, name="wd_codes", align_bytes=64)
+        wd_sc = const.tile([P, C], U8, name="wd_sc", align_bytes=64)
+
+        def wd_prepare():
+            for u in range(2):
+                nc.vector.tensor_copy(
+                    out=wd_grp[:].rearrange("p (u i e) j -> p u i e j", u=2, e=2)[:, u],
+                    in_=wd_raw[:].rearrange("p j (i u e) -> p u i e j", u=2, e=2)[:, u],
+                )
+            nc.vector.quantize_mx(out=wd_codes[:].bitcast(FP8X4), scales=wd_sc[:], in_=wd_grp[:].rearrange("p c j -> p (c j)"))
+
+        wb_grp = const.tile([P, 2, D, 4], BF16, name="wb_grp", align_bytes=64)
+        wb_codes = const.tile([P, 2, D], U32, name="wb_codes", align_bytes=64)
+        wb_sc = const.tile([P, 2, D], U8, name="wb_sc", align_bytes=64)
+
+        def wb_interleave(a):
+            g, part = a // 4, a % 4
+            d = slice(part * 128, part * 128 + 128)
+            nc.scalar.copy(out=wb_grp[:, g, d, :], in_=wb_raw[:, g, :, d].rearrange("p j d -> p d j"))
+
+        def wb_quantise(g):
+            nc.vector.quantize_mx(out=wb_codes[:, g, :].bitcast(FP8X4), scales=wb_sc[:, g, :], in_=wb_grp[:, g].rearrange("p d j -> p (d j)"))
+
+        gain_ps = psum.tile([P, NBC], BF16, name="gain_ps")
+
+        def gain_spread():
+            for a in range(2):
+                nc.tensor.matmul(out=gain_ps[:, a * 512:(a + 1) * 512], lhsT=ones[:, 0:P], rhs=g_zero[:, a * 512:(a + 1) * 512], start=True, stop=True)
+
+        def warm_tensor(n):
+            w_t = psum.tile([P, 4 * P], F32, name="mm", bufs=2)
+            for a in range(n):
+                nc.tensor.matmul(out=w_t[:], lhsT=ones[:, 0:P], rhs=ones[:], start=True, stop=True)
+
+        mw, mtr, mq, mcode, yps, xs, pts, ptr, pqs, pcode, mm, tts, aggs = {}, {}, {}, {}, {}, {}, {}, {}, {}, {}, {}, {}, {}
+
+        def product(t):
+            mw_t = work.tile([P, D], BF16, name="mw", bufs=8, align_bytes=64)
+            nc.vector.tensor_tensor(out=mw_t[:], in0=mbytes[t].bitcast(FP8), in1=scale_bc[:], op=MULT)
+            mw[t] = mw_t
+
+        casts = {}
+
+        def product_cast(t):
+            c_t = work.tile([P, D], BF16, name="cast", bufs=3, align_bytes=64)
+            nc.scalar.copy(out=c_t[:], in_=mbytes[t].bitcast(FP8))
+            casts[t] = c_t
+
+        def product_gpsimd(t, half, codes):
+            if half == 0:
+                mw_t = work.tile([P, D], BF16, name="mw", bufs=8, align_bytes=64)
+                mw[t] = mw_t
+            mark = work.tile([P, 1], U32, name="mark", bufs=2)
+            nc.gpsimd.tensor_copy(out=mark[:], in_=codes[:, 0:1])
+            nc.gpsimd.tensor_tensor(
+                out=mw[t][:, half * 256:half * 256 + 256].rearrange("p (w e) -> p w e", e=2),
+                in0=casts[t][:].rearrange("p (w u e) -> p u w e", u=2, e=2)[:, half],
+                in1=scale_bc[:].rearrange("p (w u e) -> p u w e", u=2, e=2)[:, half], op=MULT,
+            )
+
+        def m_transpose(c):
+            tr_t = psum.tile([P, 2, 2, P], F32, name="tr", bufs=3)
+            for j, t in enumerate(M_CHUNKS[c]):
+                words = mw[t][:].bitcast(F32)
+                for u in range(2):
+                    cols = slice(u * P, u * P + P) if t in OFFLOAD else slice(u, 256, 2)
+                    nc.tensor.transpose(tr_t[:, j, u, :], words[:, cols], ident[:])
+            mtr[c] = tr_t
+
+        def m_copy(c):
+            n = len(M_CHUNKS[c])
+            mq_t = work.tile([P, 2 * P * 4], BF16, name="mq", bufs=4, align_bytes=64)
+            dst = mq_t[:].bitcast(F32)[:, 0:n * 256].rearrange("p (j r u) -> p j r u", j=n, u=2)
+            nc.scalar.copy(out=dst, in_=mtr[c][:, 0:n].rearrange("p j u r -> p j r u"))
+            mq[c] = mq_t
+
+        def m_quant(c):
+            n = len(M_CHUNKS[c])
+            mc_t = work.tile([P, 2 * P], U32, name="mc", bufs=3, align_bytes=64)
+            ms_t = work.tile([P, 2 * P], U8, name="ms", bufs=3, align_bytes=64)
+            nc.vector.quantize_mx(out=mc_t[:, 0:n * P].bitcast(FP8X4), scales=ms_t[:, 0:n * P], in_=mq[c][:, 0:n * P * 4])
+            mcode[c] = (mc_t, ms_t)
+
+        def stage1(c):
+            y_t = psum.tile([P, 2, C], F32, name="y", bufs=1)
+            mc_t, ms_t = mcode[c]
+            for j in range(len(M_CHUNKS[c])):
+                cols = slice(j * P, (j + 1) * P)
+                nc.tensor.matmul_mx(
+                    out=y_t[:, j, :], lhsT=mc_t[:, cols].bitcast(FP8X4), lhsT_scale=ms_t[:, cols],
+                    rhs=wd_codes[:].bitcast(FP8X4), rhs_scale=wd_sc[:], start=True, stop=True,
+                )
+            yps[c] = y_t
+
+        def silu1(c):
+            n = len(M_CHUNKS[c])
+            x_t = work.tile([P, 2, C], F32, name="x", bufs=3, align_bytes=64)
+            nc.scalar.activation(out=x_t[:, 0:n], in_=yps[c][:, 0:n], func=SILU)
+            for j, t in enumerate(M_CHUNKS[c]):
+                xs[t] = x_t[:, j, :].rearrange("p (u w) -> p u w", u=2)
+
+        def p_ops(t, n0, n1):
+            if n0 == 0:
+                p_t = work.tile([P, NBC], BF16, name="pt", bufs=3, align_bytes=64)
+                pts[t] = p_t
+            view = pts[t][:].rearrange("p (g u n w) -> p g u n w", g=2, u=2, n=4)
+            for n in range(n0, n1):
+                col = t * NB + n
+                nc.vector.scalar_tensor_tensor(
+                    out=view[:, n // 4, :, n % 4, :], in0=xs[t], scalar=sbf_f[:, col:col + 1],
+                    in1=gain_ps[:, n * C:(n + 1) * C].rearrange("p (u w) -> p u w", u=2), op0=MULT, op1=MULT,
+                )
+
+        p_place = {}
+        for c, tiles in enumerate(P_CHUNKS):
+            for j, t in enumerate(tiles):
+                p_place[t] = (c, j)
+
+        def p_transpose(t, passes=(0, 1)):
+            words = pts[t][:].bitcast(F32)
+            tr_t = psum.tile([P, 4, P], F32, name="tr", bufs=3)
+            for g in passes:
+                for a in (2 * g, 2 * g + 1):
+                    nc.tensor.transpose(tr_t[:, a, :], words[:, a * P:(a + 1) * P], ident[:])
+                ptr[t, g] = tr_t
+
+        def p_copy(t, passes=(0, 1)):
+            c, j = p_place[t]
+            n = len(P_CHUNKS[c])
+            if j == 0 and passes[0] == 0:
+                pq_t = work.tile([P, 2 * NBC], BF16, name="pq", bufs=3, align_bytes=64)
+                pqs[c] = pq_t
+            g0, g1 = passes[0], passes[-1] + 1
+            dst = pqs[c][:].bitcast(F32)[:, 0:n * 512].rearrange("p (g j r u) -> p g j r u", g=2, j=n, u=2)[:, g0:g1, j]
+            nc.scalar.copy(out=dst, in_=ptr[t, g0][:].rearrange("p (g u) r -> p g r u", g=2)[:, g0:g1])
+
+        def p_quant(c, passes=(0, 1)):
+            n = len(P_CHUNKS[c])
+            if passes[0] == 0:
+                pc_t = work.tile([P, 4 * P], U32, name="pc", bufs=3, align_bytes=64)
+                ps_t = work.tile([P, 4 * P], U8, name="ps", bufs=3, align_bytes=64)
+                pcode[c] = (pc_t, ps_t)
+            words = slice(passes[0] * n * P, (passes[-1] + 1) * n * P)
+            values = slice(passes[0] * n * 512, (passes[-1] + 1) * n * 512)
+            nc.vector.quantize_mx(out=pcode[c][0][:, words].bitcast(FP8X4), scales=pcode[c][1][:, words], in_=pqs[c][:, values])
+
+        def bank_dims(c, b):
+            per = 2 if c == 16 else 4 // len(P_CHUNKS[c])
+            return list(range(b * per, (b + 1) * per))
+
+        def stage2(c, b):
+            n = len(P_CHUNKS[c])
+            if c < 15:
+                mm_t = psum.tile([P, 4 * P], F32, name="mm", bufs=2)
+            else:
+                mm_t = psum.tile([P, 4 * P], F32, name="tr", bufs=3)
+            pc_t, ps_t = pcode[c]
+            if c < 12:
+                nc.tensor.matmul_mx(
+                    out=mm_t[:, 0:128], lhsT=wb_codes[:, 0, 0:P].bitcast(FP8X4), lhsT_scale=wb_sc[:, 0, 0:P],
+                    rhs=wb_codes[:, 1, 0:128].bitcast(FP8X4), rhs_scale=wb_sc[:, 1, 0:128], start=True, stop=True,
+                )
+            for i, d in enumerate(bank_dims(c, b)):
+                cols = slice(d * P, (d + 1) * P)
+                for g in range(2):
+                    toks = slice(g * n * P, (g + 1) * n * P)
+                    nc.tensor.matmul_mx(
+                        out=mm_t[:, i * n * P:(i + 1) * n * P], lhsT=wb_codes[:, g, cols].bitcast(FP8X4), lhsT_scale=wb_sc[:, g, cols],
+                        rhs=pc_t[:, toks].bitcast(FP8X4), rhs_scale=ps_t[:, toks], start=(g == 0), stop=(g == 1),
+                    )
+            mm[c, b] = mm_t
+
+        def silu2(c, b):
+            t_t = work.tile([P, 4 * P], F32, name="tt", bufs=6, align_bytes=64)
+            w = len(bank_dims(c, b)) * len(P_CHUNKS[c]) * P
+            nc.scalar.activation(out=t_t[:, 0:w], in_=mm[c, b][:, 0:w], func=SILU)
+            tts[c, b] = t_t
+
+        def k_sum(c, b):
+            tiles = P_CHUNKS[c]
+            n = len(tiles)
+            h = tiles[0] // HALF
+            dims = bank_dims(c, b)
+            first = tiles[0] % HALF == 0 and dims[0] == 0
+            last = tiles[-1] % HALF == HALF - 1 and dims[-1] == 3
+            if first:
+                agg_t = psum.tile([P, D], F32, name="agg", bufs=1)
+                aggs[h] = agg_t
+            for i, d in enumerate(dims):
+                for j in range(n):
+                    nc.tensor.matmul(
+                        out=aggs[h][:, d * P:(d + 1) * P], lhsT=tts[c, b][:, (i * n + j) * P:(i * n + j + 1) * P], rhs=ident[:],
+                        is_transpose=True, start=(first and i == 0 and j == 0), stop=(last and d == 3 and j == n - 1),
+                    )
+            return last
+
+        def finish(h):
+            o_t = work.tile([P, D], F32, name="o", bufs=2, align_bytes=64)
+            nc.vector.scalar_tensor_tensor(out=o_t[:], in0=aggs[h][:], scalar=0.25, in1=mji[:, h, :], op0=MULT, op1=ADD)
+            nc.sync.dma_start(out=out[h * P:(h + 1) * P, :], in_=o_t[:])
+
+        def at(chunks, q, lead):
+            return [c for c, tiles in enumerate(chunks) if tiles[0] - lead == q]
+
+        warm_tensor(3)
+        product(0)
+        m_transpose(0)
+        m_copy(0)
+        product(1)
+        m_transpose(1)
+        gain_spread()
+        m_copy(1)
+        wd_prepare()
+        m_quant(0)
+        stage1(0)
+        silu1(0)
+        product(2)
+        m_quant(1)
+        stage1(1)
+        silu1(1)
+        product(3)
+        m_transpose(2)
+        warm_tensor(3)
+        wb_interleave(0)
+        wb_interleave(1)
+        m_copy(2)
+        wb_interleave(2)
+        p_ops(0, 0, 8)
+        product(4)
+        m_quant(2)
+        stage1(2)
+        silu1(2)
+        product(5)
+        m_transpose(3)
+        m_copy(3)
+        to_silu, to_sum = [], []
+        for q in range(1, TILES):
+            p_transpose(q - 1)
+            done = [P_CHUNKS[cb[0]][0] // HALF for cb in to_sum if k_sum(*cb)]
+            to_sum = to_silu
+            if q >= 40:
+                p_copy(q - 1)
+            for cb in to_silu:
+                silu2(*cb)
+            to_silu = []
+            if q < 40:
+                p_copy(q - 1)
+            if q == 1:
+                p_ops(q, 0, 8)
+            if q + 5 < TILES and q + 5 not in OFFLOAD:
+                product(q + 5)
+            for c in at(P_CHUNKS, q, -3):
+                if c < 14:
+                    p_quant(c)
+                    codes = pcode[c][0]
+            for c in at(M_CHUNKS, q, 2):
+                m_quant(c)
+                codes = mcode[c][0]
+            for half in range(2):
+                if q + 7 - half in OFFLOAD:
+                    product_gpsimd(q + 7 - half, half, codes)
+            if 1 < q < TILES - 1:
+                p_ops(q, 0, 8)
+            if q == TILES - 2:
+                p_quant(14)
+            for h in done:
+                finish(h)
+            if q == 3:
+                wb_quantise(0)
+                wb_quantise(1)
+            if q > 1:
+                for c in at(M_CHUNKS, q, 1):
+                    silu1(c)
+            if q + 8 in OFFLOAD:
+                product_cast(q + 8)
+            for c in at(M_CHUNKS, q, 4):
+                if c > 3:
+                    m_transpose(c)
+                    m_copy(c)
+            for c in range(14):
+                for b in range(2):
+                    if q == P_CHUNKS[c][0] + 4 + b - (1 if c == 13 else 0):
+                        stage2(c, b)
+                        to_silu.append((c, b))
+            for c in at(M_CHUNKS, q, 2):
+                stage1(c)
+            if q < 4:
+                warm_tensor(3)
+            if q < 3:
+                for a in range(3 * q, min(3 * q + 3, 8)):
+                    wb_interleave(a)
+        last = TILES - 1
+        p_ops(last, 0, 4)
+        stage2(14, 0)
+        p_transpose(last, (0,))
+        p_copy(last, (0,))
+        p_ops(last, 4, 8)
+        p_quant(15)
+        p_transpose(last, (1,))
+        p_copy(last, (1,))
+        p_quant(16)
+        silu2(14, 0)
+        stage2(14, 1)
+        stage2(15, 0)
+        for cb in to_sum:
+            k_sum(*cb)
+        silu2(14, 1)
+        silu2(15, 0)
+        stage2(16, 0)
+        stage2(16, 1)
+        silu2(16, 0)
+        k_sum(14, 0)
+        silu2(16, 1)
+        k_sum(14, 1)
+        k_sum(15, 0)
+        k_sum(16, 0)
+        k_sum(16, 1)
+        finish(1)

@@ -15,15 +15,14 @@ U8 = mybir.dt.uint8
 FP8 = mybir.dt.float8_e4m3fn
 FP8X4 = mybir.dt.float8_e4m3fn_x4
 MULT = mybir.AluOpType.mult
-ADD = mybir.AluOpType.add
 SILU = mybir.ActivationFunctionType.Silu
+COPY = mybir.ActivationFunctionType.Copy
 
 TILES = 32
+PAIRS = 16
 HALF = 16
-M_CHUNKS = [[0], [1]] + [[t, t + 1] for t in range(2, TILES, 2)]
-P_CHUNKS = [[t, t + 1] for t in range(0, TILES - 2, 2)] + [[TILES - 2], [TILES - 1]]
-OFFLOAD = [t for t in range(10, TILES, 2)]
-LOADS = [(0, 2), (2, 4), (4, 8), (8, 12), (12, 16), (16, 20), (20, 24), (24, 28), (28, 32)]
+FIRST_GPSIMD_PAIR = 2
+LOADS = [(0, 2), (2, 6), (6, 10), (10, 16), (16, 24), (24, 32)]
 
 
 def tile_dimenettripletbilinear_kernel(tc, m_kj_bytes, m_kj_scale, m_ji, sbf, w_down, gain, w_bil, out):
@@ -43,146 +42,176 @@ def tile_dimenettripletbilinear_kernel(tc, m_kj_bytes, m_kj_scale, m_ji, sbf, w_
                 out=t_t[:], in_=m_kj_bytes[h * P:(h + 1) * P, t0 - h * HALF:t1 - h * HALF, :].rearrange("e k d -> e (k d)")
             )
             for t in range(t0, t1):
-                mbytes[t] = t_t[:, (t - t0) * D:(t - t0 + 1) * D]
+                mbytes[t] = t_t[:, (t - t0) * D:(t - t0 + 1) * D].bitcast(FP8)
 
-        g_raw = const.tile([1, NBC], BF16, name="g_raw", align_bytes=64)
-        nc.sync.dma_start(out=g_raw[:], in_=gain.unsqueeze(0))
-        scale_bc = const.tile([P, D], F32, name="scale_bc", align_bytes=64)
-        nc.sync.dma_start(out=scale_bc[:], in_=m_kj_scale.rearrange("a b k -> (a b k)").partition_broadcast(P))
         load_bytes(*LOADS[0])
+        scale4 = const.tile([P, 4], F32, name="scale4", align_bytes=64)
+        nc.scalar.dma_start(out=scale4[:], in_=m_kj_scale.rearrange("a b (p j) -> p (a b j)", j=4))
         wd_raw = const.tile([P, 4, C], BF16, name="wd_raw", align_bytes=64)
         nc.sync.dma_start(out=wd_raw[:], in_=w_down.rearrange("(p j) c -> p j c", j=4))
-        sbf_raw = const.tile([P, 2, K * NB], BF16, name="sbf_raw", align_bytes=64)
-        nc.sync.dma_start(out=sbf_raw[:], in_=sbf.rearrange("(h e) k n -> e h (k n)", e=P))
-        load_bytes(*LOADS[1])
-        wb_raw = const.tile([P, 2, 4, D], BF16, name="wb_raw", align_bytes=64)
+        gain8 = const.tile([P, 8], BF16, name="gain8", align_bytes=64)
+        nc.scalar.dma_start(out=gain8[:], in_=gain.rearrange("(p j) -> p j", j=8))
+        sbf_sb = const.tile([P, 2, K * NB], BF16, name="sbf_sb", align_bytes=64)
+        nc.scalar.dma_start(out=sbf_sb[:], in_=sbf.rearrange("(h e) k n -> e h (k n)", e=P))
         wb_hbm = w_bil.rearrange("(g p j) d -> g p j d", g=2, j=4)
-        for g in range(2):
-            nc.sync.dma_start(out=wb_raw[:, g], in_=wb_hbm[g])
-        for t0, t1 in LOADS[2:]:
-            load_bytes(t0, t1)
+        wb_raw = {}
+
+        def load_wb(g, b):
+            wb_t = const.tile([P, 4, 256], BF16, name="wb_raw%d%d" % (g, b), align_bytes=64)
+            nc.sync.dma_start(out=wb_t[:], in_=wb_hbm[g][:, :, b * 256:(b + 1) * 256])
+            wb_raw[g, b] = wb_t
+
+        load_wb(0, 0)
+        load_bytes(*LOADS[1])
+        load_wb(1, 0)
+        load_wb(0, 1)
+        load_wb(1, 1)
+        load_bytes(*LOADS[2])
         mji = const.tile([P, 2, D], BF16, name="mji", align_bytes=64)
         nc.sync.dma_start(out=mji[:], in_=m_ji.rearrange("(h e) d -> e h d", e=P))
+        for t0, t1 in LOADS[3:]:
+            load_bytes(t0, t1)
 
-        warm = const.tile([P, 1], F32, name="warm")
-        nc.vector.memset(warm[:], 0.0)
-        warm2 = const.tile([P, 1], F32, name="warm2")
-        nc.scalar.activation(out=warm2[:], in_=warm[:], func=SILU)
         ident = const.tile([P, P], F32, name="ident", align_bytes=64)
         make_identity(nc, ident[:])
-        ones = const.tile([P, 512], BF16, name="ones", align_bytes=64)
-        nc.gpsimd.memset(ones[:], 1.0)
-        g_zero = const.tile([P, NBC], BF16, name="g_zero", align_bytes=64)
-        nc.gpsimd.memset(g_zero[:], 0.0)
-        for u in range(2):
-            nc.scalar.copy(
-                out=g_zero[0:1, :].rearrange("o (n u i e) -> o u n i e", u=2, i=32, e=2)[:, u],
-                in_=g_raw[:].rearrange("o (n i u e) -> o u n i e", u=2, i=32, e=2)[:, u],
-            )
-        sbf_f = const.tile([P, 2 * K * NB], F32, name="sbf_f", align_bytes=64)
-        nc.scalar.copy(out=sbf_f[:], in_=sbf_raw[:].rearrange("p h k -> p (h k)"))
+        one = const.tile([P, 1], F32, name="one")
+        nc.vector.memset(one[:], 1.0)
+        ident4 = const.tile([P, P], BF16, name="ident4", align_bytes=64)
+        nc.vector.tensor_scalar(out=ident4[:], in0=ident[:], scalar1=4.0, scalar2=None, op0=MULT)
+
+        def bank():
+            bank_t = psum.tile([P, 512], F32, name="bank", bufs=6)
+            return bank_t
+
+        scale_pair = const.tile([P, 2 * D], F32, name="scale_pair", align_bytes=64)
+
+        def scale_spread():
+            b_t = bank()
+            for j in range(4):
+                nc.tensor.transpose(b_t[:, j * P:(j + 1) * P], scale4[:, j:j + 1].to_broadcast([P, P]), ident[:])
+            return b_t
+
+        def scale_copy_plain(b_t):
+            nc.scalar.copy(out=scale_pair[:, 0:D].rearrange("q (p j) -> q p j", j=4), in_=b_t[:].rearrange("q (j p) -> q p j", j=4))
+
+        def scale_copy_split(b_t):
+            nc.scalar.copy(out=scale_pair[:, D:2 * D].rearrange("q (u p e) -> q u p e", u=2, e=2), in_=b_t[:].rearrange("q (u e p) -> q u p e", u=2, e=2))
+
+        gain_ps = psum.tile([P, 512], F32, name="gain_ps")
+
+        def gain_spread():
+            words = gain8[:].bitcast(F32)
+            place = gain_ps[:].rearrange("q (n u r a) -> q u a n r", n=NB, u=2, a=2)
+            for j in range(4):
+                nc.tensor.transpose(place[:, j % 2, j // 2], words[:, j:j + 1].to_broadcast([P, P]), ident[:])
 
         wd_grp = const.tile([P, C, 4], BF16, name="wd_grp", align_bytes=64)
         wd_codes = const.tile([P, C], U32, name="wd_codes", align_bytes=64)
         wd_sc = const.tile([P, C], U8, name="wd_sc", align_bytes=64)
 
-        def wd_prepare():
+        def wd_interleave():
             for u in range(2):
                 nc.vector.tensor_copy(
                     out=wd_grp[:].rearrange("p (u i e) j -> p u i e j", u=2, e=2)[:, u],
                     in_=wd_raw[:].rearrange("p j (i u e) -> p u i e j", u=2, e=2)[:, u],
                 )
+
+        def wd_quantise():
             nc.vector.quantize_mx(out=wd_codes[:].bitcast(FP8X4), scales=wd_sc[:], in_=wd_grp[:].rearrange("p c j -> p (c j)"))
 
-        wb_grp = const.tile([P, 2, D, 4], BF16, name="wb_grp", align_bytes=64)
-        wb_codes = const.tile([P, 2, D], U32, name="wb_codes", align_bytes=64)
-        wb_sc = const.tile([P, 2, D], U8, name="wb_sc", align_bytes=64)
+        wb_grp, wb_codes, wb_sc = {}, {}, {}
 
-        def wb_interleave(a):
-            g, part = a // 4, a % 4
-            d = slice(part * 128, part * 128 + 128)
-            nc.scalar.copy(out=wb_grp[:, g, d, :], in_=wb_raw[:, g, :, d].rearrange("p j d -> p d j"))
-
-        def wb_quantise(g):
-            nc.vector.quantize_mx(out=wb_codes[:, g, :].bitcast(FP8X4), scales=wb_sc[:, g, :], in_=wb_grp[:, g].rearrange("p d j -> p (d j)"))
-
-        gain_ps = psum.tile([P, NBC], BF16, name="gain_ps")
-
-        def gain_spread():
-            for a in range(2):
-                nc.tensor.matmul(out=gain_ps[:, a * 512:(a + 1) * 512], lhsT=ones[:, 0:P], rhs=g_zero[:, a * 512:(a + 1) * 512], start=True, stop=True)
-
-        def warm_tensor(n):
-            w_t = psum.tile([P, 4 * P], F32, name="mm", bufs=2)
-            for a in range(n):
-                nc.tensor.matmul(out=w_t[:], lhsT=ones[:, 0:P], rhs=ones[:], start=True, stop=True)
-
-        mw, mtr, mq, mcode, yps, xs, pts, ptr, pqs, pcode, mm, tts, aggs = {}, {}, {}, {}, {}, {}, {}, {}, {}, {}, {}, {}, {}
-
-        def product(t):
-            mw_t = work.tile([P, D], BF16, name="mw", bufs=8, align_bytes=64)
-            nc.vector.tensor_tensor(out=mw_t[:], in0=mbytes[t].bitcast(FP8), in1=scale_bc[:], op=MULT)
-            mw[t] = mw_t
-
-        casts = {}
-
-        def product_cast(t):
-            c_t = work.tile([P, D], BF16, name="cast", bufs=3, align_bytes=64)
-            nc.scalar.copy(out=c_t[:], in_=mbytes[t].bitcast(FP8))
-            casts[t] = c_t
-
-        def product_gpsimd(t, half, codes):
-            if half == 0:
-                mw_t = work.tile([P, D], BF16, name="mw", bufs=8, align_bytes=64)
-                mw[t] = mw_t
-            mark = work.tile([P, 1], U32, name="mark", bufs=2)
-            nc.gpsimd.tensor_copy(out=mark[:], in_=codes[:, 0:1])
-            nc.gpsimd.tensor_tensor(
-                out=mw[t][:, half * 256:half * 256 + 256].rearrange("p (w e) -> p w e", e=2),
-                in0=casts[t][:].rearrange("p (w u e) -> p u w e", u=2, e=2)[:, half],
-                in1=scale_bc[:].rearrange("p (w u e) -> p u w e", u=2, e=2)[:, half], op=MULT,
+        def wb_interleave(g, b):
+            grp_t = const.tile([P, 256, 4], BF16, name="wb_grp%d%d" % (g, b), align_bytes=64)
+            nc.scalar.copy(
+                out=grp_t[:].rearrange("p (c i) j -> p c j i", i=4),
+                in_=wb_raw[g, b][:].rearrange("p j (c i) -> p c j i", i=4),
             )
+            wb_grp[g, b] = grp_t
 
-        def m_transpose(c):
-            tr_t = psum.tile([P, 2, 2, P], F32, name="tr", bufs=3)
-            for j, t in enumerate(M_CHUNKS[c]):
-                words = mw[t][:].bitcast(F32)
-                for u in range(2):
-                    cols = slice(u * P, u * P + P) if t in OFFLOAD else slice(u, 256, 2)
-                    nc.tensor.transpose(tr_t[:, j, u, :], words[:, cols], ident[:])
-            mtr[c] = tr_t
+        def wb_quantise(g, b):
+            codes_t = const.tile([P, 256], U32, name="wb_codes%d%d" % (g, b), align_bytes=64)
+            sc_t = const.tile([P, 256], U8, name="wb_sc%d%d" % (g, b), align_bytes=64)
+            nc.vector.quantize_mx(out=codes_t[:].bitcast(FP8X4), scales=sc_t[:], in_=wb_grp[g, b][:].rearrange("p d j -> p (d j)"))
+            wb_codes[g, b], wb_sc[g, b] = codes_t, sc_t
 
-        def m_copy(c):
-            n = len(M_CHUNKS[c])
-            mq_t = work.tile([P, 2 * P * 4], BF16, name="mq", bufs=4, align_bytes=64)
-            dst = mq_t[:].bitcast(F32)[:, 0:n * 256].rearrange("p (j r u) -> p j r u", j=n, u=2)
-            nc.scalar.copy(out=dst, in_=mtr[c][:, 0:n].rearrange("p j u r -> p j r u"))
-            mq[c] = mq_t
+        casts, mw, mtr, mq, mcode, yps, xs, pts, ptr, pqs, pcode, mm, tts, aggs = ({} for a in range(14))
 
-        def m_quant(c):
-            n = len(M_CHUNKS[c])
-            mc_t = work.tile([P, 2 * P], U32, name="mc", bufs=3, align_bytes=64)
-            ms_t = work.tile([P, 2 * P], U8, name="ms", bufs=3, align_bytes=64)
-            nc.vector.quantize_mx(out=mc_t[:, 0:n * P].bitcast(FP8X4), scales=ms_t[:, 0:n * P], in_=mq[c][:, 0:n * P * 4])
-            mcode[c] = (mc_t, ms_t)
+        split = {}
 
-        def stage1(c):
-            y_t = psum.tile([P, 2, C], F32, name="y", bufs=1)
-            mc_t, ms_t = mcode[c]
-            for j in range(len(M_CHUNKS[c])):
-                cols = slice(j * P, (j + 1) * P)
+        def cast_tile(t):
+            if t // 2 not in casts:
+                c_t = work.tile([P, 2 * D], BF16, name="cast", bufs=3, align_bytes=64)
+                casts[t // 2] = c_t
+            return casts[t // 2][:, t % 2 * D:(t % 2 + 1) * D]
+
+        def cast_vector(t):
+            nc.vector.tensor_scalar(
+                out=cast_tile(t).rearrange("p (u w e) -> p w u e", u=2, e=2), in0=mbytes[t].rearrange("p (w u e) -> p w u e", u=2, e=2),
+                scalar1=one[:], scalar2=None, op0=MULT,
+            )
+            split[t] = True
+
+        def cast_scalar(t):
+            nc.scalar.copy(out=cast_tile(t), in_=mbytes[t])
+            split[t] = False
+
+        def product_gpsimd(j):
+            mw_t = work.tile([P, 2 * D], BF16, name="mw", bufs=2, align_bytes=64)
+            if split[2 * j]:
+                nc.gpsimd.tensor_tensor(
+                    out=mw_t[:].rearrange("p (a k) -> p a k", a=2), in0=casts[j][:].rearrange("p (a k) -> p a k", a=2),
+                    in1=scale_pair[:, D:2 * D].unsqueeze(1).to_broadcast([P, 2, D]), op=MULT,
+                )
+            else:
+                nc.gpsimd.tensor_tensor(out=mw_t[:], in0=casts[j][:], in1=scale_pair[:], op=MULT)
+            mw[j] = mw_t
+
+        def tile_transpose(b_t, col, source, t):
+            words = source[:, t % 2 * D:(t % 2 + 1) * D].bitcast(F32)
+            for u in range(2):
+                half = words[:, u * P:(u + 1) * P] if split[t] else words[:, u:256:2]
+                nc.tensor.transpose(b_t[:, col + u * P:col + (u + 1) * P], half, ident[:])
+
+        def m_transpose(j):
+            b_t = bank()
+            for a in range(2):
+                tile_transpose(b_t, a * 256, mw[j], 2 * j + a)
+            mtr[j] = b_t
+
+        def m_copy(j):
+            mq_t = work.tile([P, 2 * D], BF16, name="mq", bufs=3, align_bytes=64)
+            nc.scalar.copy(out=mq_t[:].bitcast(F32).rearrange("p (a r u) -> p a r u", a=2, u=2), in_=mtr[j][:].rearrange("p (a u r) -> p a r u", a=2, u=2))
+            mq[j] = mq_t
+
+        def m_quant(j, a0, a1):
+            if a0 == 0:
+                mc_t = work.tile([P, 2 * P], U32, name="mc", bufs=2, align_bytes=64)
+                ms_t = work.tile([P, 2 * P], U8, name="ms", bufs=2, align_bytes=64)
+                mcode[j] = (mc_t, ms_t)
+            cols = slice(a0 * P, a1 * P)
+            nc.vector.quantize_mx(out=mcode[j][0][:, cols].bitcast(FP8X4), scales=mcode[j][1][:, cols], in_=mq[j][:, a0 * D:a1 * D])
+
+        def stage1(j, a0, a1):
+            y_t = bank()
+            mc_t, ms_t = mcode[j]
+            for a in range(a0, a1):
+                cols = slice(a * P, (a + 1) * P)
                 nc.tensor.matmul_mx(
-                    out=y_t[:, j, :], lhsT=mc_t[:, cols].bitcast(FP8X4), lhsT_scale=ms_t[:, cols],
+                    out=y_t[:, cols], lhsT=mc_t[:, cols].bitcast(FP8X4), lhsT_scale=ms_t[:, cols],
                     rhs=wd_codes[:].bitcast(FP8X4), rhs_scale=wd_sc[:], start=True, stop=True,
                 )
-            yps[c] = y_t
+            yps[j] = y_t
 
-        def silu1(c):
-            n = len(M_CHUNKS[c])
-            x_t = work.tile([P, 2, C], F32, name="x", bufs=3, align_bytes=64)
-            nc.scalar.activation(out=x_t[:, 0:n], in_=yps[c][:, 0:n], func=SILU)
-            for j, t in enumerate(M_CHUNKS[c]):
-                xs[t] = x_t[:, j, :].rearrange("p (u w) -> p u w", u=2)
+        def silu1(j, a0, a1):
+            x_t = work.tile([P, 2 * C], F32, name="x", bufs=3, align_bytes=64)
+            cols = slice(a0 * P, a1 * P)
+            nc.scalar.activation(out=x_t[:, cols], in_=yps[j][:, cols], func=SILU)
+            for a in range(a0, a1):
+                xs[2 * j + a] = x_t[:, a * P:(a + 1) * P].rearrange("p (u w) -> p u w", u=2)
+
+        gain_bf = gain_ps[:].bitcast(BF16)
+        sbf_cols = sbf_sb[:].rearrange("p h k -> p (h k)")
 
         def p_ops(t, n0, n1):
             if n0 == 0:
@@ -192,212 +221,241 @@ def tile_dimenettripletbilinear_kernel(tc, m_kj_bytes, m_kj_scale, m_ji, sbf, w_
             for n in range(n0, n1):
                 col = t * NB + n
                 nc.vector.scalar_tensor_tensor(
-                    out=view[:, n // 4, :, n % 4, :], in0=xs[t], scalar=sbf_f[:, col:col + 1],
-                    in1=gain_ps[:, n * C:(n + 1) * C].rearrange("p (u w) -> p u w", u=2), op0=MULT, op1=MULT,
+                    out=view[:, n // 4, :, n % 4, :], in0=xs[t], scalar=sbf_cols[:, col:col + 1],
+                    in1=gain_bf[:, n * C:(n + 1) * C].rearrange("p (u w) -> p u w", u=2), op0=MULT, op1=MULT,
                 )
 
-        p_place = {}
-        for c, tiles in enumerate(P_CHUNKS):
-            for j, t in enumerate(tiles):
-                p_place[t] = (c, j)
-
-        def p_transpose(t, passes=(0, 1)):
+        def p_transpose(t, g0, g1):
             words = pts[t][:].bitcast(F32)
-            tr_t = psum.tile([P, 4, P], F32, name="tr", bufs=3)
-            for g in passes:
-                for a in (2 * g, 2 * g + 1):
-                    nc.tensor.transpose(tr_t[:, a, :], words[:, a * P:(a + 1) * P], ident[:])
-                ptr[t, g] = tr_t
+            b_t = bank()
+            for a in range(2 * g0, 2 * g1):
+                nc.tensor.transpose(b_t[:, a * P:(a + 1) * P], words[:, a * P:(a + 1) * P], ident[:])
+            ptr[t] = b_t
 
-        def p_copy(t, passes=(0, 1)):
-            c, j = p_place[t]
-            n = len(P_CHUNKS[c])
-            if j == 0 and passes[0] == 0:
+        def p_copy(t):
+            c, a = t // 2, t % 2
+            if a == 0:
                 pq_t = work.tile([P, 2 * NBC], BF16, name="pq", bufs=3, align_bytes=64)
                 pqs[c] = pq_t
-            g0, g1 = passes[0], passes[-1] + 1
-            dst = pqs[c][:].bitcast(F32)[:, 0:n * 512].rearrange("p (g j r u) -> p g j r u", g=2, j=n, u=2)[:, g0:g1, j]
-            nc.scalar.copy(out=dst, in_=ptr[t, g0][:].rearrange("p (g u) r -> p g r u", g=2)[:, g0:g1])
+            dst = pqs[c][:].bitcast(F32).rearrange("p (g a r u) -> p g a r u", g=2, a=2, u=2)[:, :, a]
+            nc.scalar.copy(out=dst, in_=ptr[t][:].rearrange("p (g u r) -> p g r u", g=2, u=2))
 
-        def p_quant(c, passes=(0, 1)):
-            n = len(P_CHUNKS[c])
-            if passes[0] == 0:
-                pc_t = work.tile([P, 4 * P], U32, name="pc", bufs=3, align_bytes=64)
-                ps_t = work.tile([P, 4 * P], U8, name="ps", bufs=3, align_bytes=64)
-                pcode[c] = (pc_t, ps_t)
-            words = slice(passes[0] * n * P, (passes[-1] + 1) * n * P)
-            values = slice(passes[0] * n * 512, (passes[-1] + 1) * n * 512)
-            nc.vector.quantize_mx(out=pcode[c][0][:, words].bitcast(FP8X4), scales=pcode[c][1][:, words], in_=pqs[c][:, values])
-
-        def bank_dims(c, b):
-            per = 2 if c == 16 else 4 // len(P_CHUNKS[c])
-            return list(range(b * per, (b + 1) * per))
+        def p_quant(c):
+            pc_t = work.tile([P, 4 * P], U32, name="pc", bufs=3, align_bytes=64)
+            ps_t = work.tile([P, 4 * P], U8, name="ps", bufs=3, align_bytes=64)
+            nc.vector.quantize_mx(out=pc_t[:].bitcast(FP8X4), scales=ps_t[:], in_=pqs[c][:])
+            pcode[c] = (pc_t, ps_t)
 
         def stage2(c, b):
-            n = len(P_CHUNKS[c])
-            if c < 15:
-                mm_t = psum.tile([P, 4 * P], F32, name="mm", bufs=2)
-            else:
-                mm_t = psum.tile([P, 4 * P], F32, name="tr", bufs=3)
+            mm_t = bank()
             pc_t, ps_t = pcode[c]
-            if c < 12:
-                nc.tensor.matmul_mx(
-                    out=mm_t[:, 0:128], lhsT=wb_codes[:, 0, 0:P].bitcast(FP8X4), lhsT_scale=wb_sc[:, 0, 0:P],
-                    rhs=wb_codes[:, 1, 0:128].bitcast(FP8X4), rhs_scale=wb_sc[:, 1, 0:128], start=True, stop=True,
-                )
-            for i, d in enumerate(bank_dims(c, b)):
-                cols = slice(d * P, (d + 1) * P)
+            for i in range(2):
+                cols = slice(i * P, (i + 1) * P)
                 for g in range(2):
-                    toks = slice(g * n * P, (g + 1) * n * P)
+                    toks = slice(g * 256, (g + 1) * 256)
                     nc.tensor.matmul_mx(
-                        out=mm_t[:, i * n * P:(i + 1) * n * P], lhsT=wb_codes[:, g, cols].bitcast(FP8X4), lhsT_scale=wb_sc[:, g, cols],
+                        out=mm_t[:, i * 256:(i + 1) * 256], lhsT=wb_codes[g, b][:, cols].bitcast(FP8X4), lhsT_scale=wb_sc[g, b][:, cols],
                         rhs=pc_t[:, toks].bitcast(FP8X4), rhs_scale=ps_t[:, toks], start=(g == 0), stop=(g == 1),
                     )
             mm[c, b] = mm_t
 
-        def silu2(c, b):
-            t_t = work.tile([P, 4 * P], F32, name="tt", bufs=6, align_bytes=64)
-            w = len(bank_dims(c, b)) * len(P_CHUNKS[c]) * P
-            nc.scalar.activation(out=t_t[:, 0:w], in_=mm[c, b][:, 0:w], func=SILU)
-            tts[c, b] = t_t
+        def silu2(key, width):
+            t_t = work.tile([P, 4 * P], F32, name="tt", bufs=5, align_bytes=64)
+            nc.scalar.activation(out=t_t[:, 0:width], in_=mm[key][:, 0:width], func=SILU)
+            tts[key] = t_t
 
-        def k_sum(c, b):
-            tiles = P_CHUNKS[c]
-            n = len(tiles)
-            h = tiles[0] // HALF
-            dims = bank_dims(c, b)
-            first = tiles[0] % HALF == 0 and dims[0] == 0
-            last = tiles[-1] % HALF == HALF - 1 and dims[-1] == 3
-            if first:
-                agg_t = psum.tile([P, D], F32, name="agg", bufs=1)
-                aggs[h] = agg_t
+        def agg_open(h):
+            agg_t = psum.tile([P, D], F32, name="agg")
+            nc.tensor.matmul(out=agg_t[:], lhsT=ident4[:], rhs=mji[:, h, :], start=True, stop=False)
+            aggs[h] = agg_t
+
+        def k_sum(key, h, dims, last):
             for i, d in enumerate(dims):
-                for j in range(n):
-                    nc.tensor.matmul(
-                        out=aggs[h][:, d * P:(d + 1) * P], lhsT=tts[c, b][:, (i * n + j) * P:(i * n + j + 1) * P], rhs=ident[:],
-                        is_transpose=True, start=(first and i == 0 and j == 0), stop=(last and d == 3 and j == n - 1),
-                    )
-            return last
+                nc.tensor.matmul(
+                    out=aggs[h][:, d * P:(d + 1) * P], lhsT=tts[key][:, i * P:(i + 1) * P], rhs=ident[:],
+                    is_transpose=True, start=False, stop=(last and i == len(dims) - 1),
+                )
+
+        def k_sum_pair(c, b):
+            if c % 8 == 0 and b == 0:
+                agg_open(c // 8)
+            k_sum((c, b), c // 8, [2 * b, 2 * b, 2 * b + 1, 2 * b + 1], c == 7 and b == 1)
 
         def finish(h):
             o_t = work.tile([P, D], F32, name="o", bufs=2, align_bytes=64)
-            nc.vector.scalar_tensor_tensor(out=o_t[:], in0=aggs[h][:], scalar=0.25, in1=mji[:, h, :], op0=MULT, op1=ADD)
+            nc.scalar.activation(out=o_t[:], in_=aggs[h][:], func=COPY, scale=0.25)
             nc.sync.dma_start(out=out[h * P:(h + 1) * P, :], in_=o_t[:])
 
-        def at(chunks, q, lead):
-            return [c for c, tiles in enumerate(chunks) if tiles[0] - lead == q]
+        head = {}
 
-        warm_tensor(3)
-        product(0)
-        m_transpose(0)
-        m_copy(0)
-        product(1)
-        m_transpose(1)
+        def head_transpose(t):
+            b_t = bank()
+            tile_transpose(b_t, 0, casts[t // 2], t)
+            head[t] = b_t
+
+        def head_product(t):
+            if t % 2 == 0:
+                mq_t = work.tile([P, 2 * D], BF16, name="mq", bufs=3, align_bytes=64)
+                mq[t // 2] = mq_t
+            nc.vector.tensor_tensor(
+                out=mq[t // 2][:, t % 2 * D:(t % 2 + 1) * D].rearrange("p (r u e) -> p r u e", u=2, e=2),
+                in0=head[t][:, 0:256].bitcast(BF16).rearrange("p (u r e) -> p r u e", u=2, e=2),
+                in1=scale4[:].rearrange("p (u e) -> p u e", u=2).unsqueeze(1).to_broadcast([P, P, 2, 2]), op=MULT,
+            )
+
+        cast_vector(0)
+        scale_bank = scale_spread()
+        head_transpose(0)
+        cast_vector(1)
+        head_transpose(1)
         gain_spread()
-        m_copy(1)
-        wd_prepare()
-        m_quant(0)
-        stage1(0)
-        silu1(0)
-        product(2)
-        m_quant(1)
-        stage1(1)
-        silu1(1)
-        product(3)
-        m_transpose(2)
-        warm_tensor(3)
-        wb_interleave(0)
-        wb_interleave(1)
-        m_copy(2)
-        wb_interleave(2)
-        p_ops(0, 0, 8)
-        product(4)
-        m_quant(2)
-        stage1(2)
-        silu1(2)
-        product(5)
-        m_transpose(3)
-        m_copy(3)
-        to_silu, to_sum = [], []
-        for q in range(1, TILES):
-            p_transpose(q - 1)
-            done = [P_CHUNKS[cb[0]][0] // HALF for cb in to_sum if k_sum(*cb)]
-            to_sum = to_silu
-            if q >= 40:
-                p_copy(q - 1)
-            for cb in to_silu:
-                silu2(*cb)
-            to_silu = []
-            if q < 40:
-                p_copy(q - 1)
-            if q == 1:
-                p_ops(q, 0, 8)
-            if q + 5 < TILES and q + 5 not in OFFLOAD:
-                product(q + 5)
-            for c in at(P_CHUNKS, q, -3):
-                if c < 14:
-                    p_quant(c)
-                    codes = pcode[c][0]
-            for c in at(M_CHUNKS, q, 2):
-                m_quant(c)
-                codes = mcode[c][0]
-            for half in range(2):
-                if q + 7 - half in OFFLOAD:
-                    product_gpsimd(q + 7 - half, half, codes)
-            if 1 < q < TILES - 1:
-                p_ops(q, 0, 8)
-            if q == TILES - 2:
-                p_quant(14)
-            for h in done:
-                finish(h)
-            if q == 3:
-                wb_quantise(0)
-                wb_quantise(1)
-            if q > 1:
-                for c in at(M_CHUNKS, q, 1):
-                    silu1(c)
-            if q + 8 in OFFLOAD:
-                product_cast(q + 8)
-            for c in at(M_CHUNKS, q, 4):
-                if c > 3:
-                    m_transpose(c)
-                    m_copy(c)
-            for c in range(14):
-                for b in range(2):
-                    if q == P_CHUNKS[c][0] + 4 + b - (1 if c == 13 else 0):
-                        stage2(c, b)
-                        to_silu.append((c, b))
-            for c in at(M_CHUNKS, q, 2):
-                stage1(c)
-            if q < 4:
-                warm_tensor(3)
-            if q < 3:
-                for a in range(3 * q, min(3 * q + 3, 8)):
-                    wb_interleave(a)
-        last = TILES - 1
-        p_ops(last, 0, 4)
-        stage2(14, 0)
-        p_transpose(last, (0,))
-        p_copy(last, (0,))
-        p_ops(last, 4, 8)
-        p_quant(15)
-        p_transpose(last, (1,))
-        p_copy(last, (1,))
-        p_quant(16)
-        silu2(14, 0)
-        stage2(14, 1)
-        stage2(15, 0)
-        for cb in to_sum:
-            k_sum(*cb)
-        silu2(14, 1)
-        silu2(15, 0)
-        stage2(16, 0)
-        stage2(16, 1)
-        silu2(16, 0)
-        k_sum(14, 0)
-        silu2(16, 1)
-        k_sum(14, 1)
-        k_sum(15, 0)
-        k_sum(16, 0)
-        k_sum(16, 1)
+        wd_interleave()
+        wb_interleave(0, 0)
+        scale_copy_split(scale_bank)
+        head_product(0)
+        wd_quantise()
+        cast_vector(2)
+        m_quant(0, 0, 1)
+        stage1(0, 0, 1)
+        silu1(0, 0, 1)
+        head_product(1)
+        scale_copy_plain(scale_bank)
+        cast_vector(3)
+        cast_vector(4)
+        head_transpose(2)
+        m_quant(0, 1, 2)
+        head_transpose(3)
+        stage1(0, 1, 2)
+        wb_interleave(1, 0)
+        silu1(0, 1, 2)
+        cast_vector(5)
+        product_gpsimd(2)
+        p_ops(0, 0, NB)
+        head_product(2)
+        head_product(3)
+        wb_interleave(0, 1)
+        p_transpose(0, 0, 2)
+        cast_scalar(6)
+        p_copy(0)
+
+        for j in range(1, PAIRS - 1):
+            if j == 1:
+                wb_quantise(0, 0)
+            m_quant(j, 0, 2)
+            if j == 1:
+                wb_quantise(1, 0)
+            if j == 2:
+                wb_quantise(0, 1)
+                wb_quantise(1, 1)
+            if j >= 2:
+                p_quant(j - 2)
+            if j + 2 < PAIRS:
+                cast_vector(2 * j + 5)
+                product_gpsimd(j + 2)
+            stage1(j, 0, 2)
+            silu1(j, 0, 2)
+            if j >= 2:
+                stage2(j - 2, 0)
+                silu2((j - 2, 0), 512)
+            if j == 1:
+                wb_interleave(1, 1)
+            p_ops(2 * j - 1, 0, NB)
+            m_transpose(j + 1)
+            m_copy(j + 1)
+            p_transpose(2 * j - 1, 0, 2)
+            p_copy(2 * j - 1)
+            if j >= 3:
+                k_sum_pair(j - 3, 1)
+            if j == 10:
+                finish(0)
+            if j + 3 < PAIRS:
+                cast_scalar(2 * j + 6)
+            if j >= 2:
+                stage2(j - 2, 1)
+                silu2((j - 2, 1), 512)
+            p_ops(2 * j, 0, NB)
+            if j >= 2:
+                k_sum_pair(j - 2, 0)
+            if j < PAIRS - 2:
+                p_transpose(2 * j, 0, 2)
+                p_copy(2 * j)
+
+        def single_copy(engine, t, g0, g1):
+            if g0 == 0:
+                pq_t = work.tile([P, 2 * NBC], BF16, name="pq", bufs=3, align_bytes=64)
+                pqs[t] = pq_t
+            dst = pqs[t][:, 0:NBC].bitcast(F32).rearrange("p (g r u) -> p g r u", g=2, u=2)[:, g0:g1]
+            engine(out=dst, in_=ptr[t, g0][:].rearrange("p (g u r) -> p g r u", g=2, u=2)[:, g0:g1])
+
+        def single_transpose(t, g0, g1):
+            p_transpose(t, g0, g1)
+            ptr[t, g0] = ptr[t]
+
+        def single_quant(t, g0, g1):
+            if g0 == 0:
+                pc_t = work.tile([P, 4 * P], U32, name="pc", bufs=3, align_bytes=64)
+                ps_t = work.tile([P, 4 * P], U8, name="ps", bufs=3, align_bytes=64)
+                pcode[t] = (pc_t, ps_t)
+            cols = slice(g0 * P, g1 * P)
+            nc.vector.quantize_mx(out=pcode[t][0][:, cols].bitcast(FP8X4), scales=pcode[t][1][:, cols], in_=pqs[t][:, g0 * D:g1 * D])
+
+        def single_pass(t, key, slot, d, g, start, stop):
+            b, cols, toks = d // 2, slice(d % 2 * P, (d % 2 + 1) * P), slice(g * P, (g + 1) * P)
+            nc.tensor.matmul_mx(
+                out=mm[key][:, slot * P:(slot + 1) * P], lhsT=wb_codes[g, b][:, cols].bitcast(FP8X4), lhsT_scale=wb_sc[g, b][:, cols],
+                rhs=pcode[t][0][:, toks].bitcast(FP8X4), rhs_scale=pcode[t][1][:, toks], start=start, stop=stop,
+            )
+
+        def single_stage2(t):
+            mm[t] = bank()
+            for d in range(4):
+                for g in range(2):
+                    single_pass(t, t, d, d, g, g == 0, g == 1)
+            silu2(t, 512)
+
+        single_transpose(28, 0, 2)
+        single_copy(nc.scalar.copy, 28, 0, 2)
+        m_quant(15, 0, 2)
+        p_quant(13)
+        stage1(15, 0, 2)
+        silu1(15, 0, 2)
+        stage2(13, 0)
+        silu2((13, 0), 512)
+        p_ops(29, 0, NB)
+        k_sum_pair(12, 1)
+        single_transpose(29, 0, 2)
+        single_copy(nc.scalar.copy, 29, 0, 2)
+        single_quant(28, 0, 2)
+        stage2(13, 1)
+        silu2((13, 1), 512)
+        single_stage2(28)
+        p_ops(30, 0, NB)
+        k_sum_pair(13, 0)
+        single_transpose(30, 0, 2)
+        single_copy(nc.scalar.copy, 30, 0, 2)
+        single_quant(29, 0, 2)
+        single_stage2(29)
+        p_ops(31, 0, NB)
+        k_sum_pair(13, 1)
+        single_transpose(31, 0, 1)
+        k_sum(28, 1, [0, 1, 2, 3], False)
+        single_transpose(31, 1, 2)
+        single_copy(nc.vector.tensor_copy, 31, 0, 1)
+        single_quant(30, 0, 2)
+        single_copy(nc.vector.tensor_copy, 31, 1, 2)
+        single_quant(31, 0, 1)
+        single_quant(31, 1, 2)
+        single_stage2(30)
+        for b in range(2):
+            mm[31, b] = bank()
+        for g in range(2):
+            for b in range(2):
+                for i in range(2):
+                    single_pass(31, (31, b), i, 2 * b + i, g, g == 0 and i == 0, g == 1 and i == 1)
+        for b in range(2):
+            silu2((31, b), 256)
+        k_sum(29, 1, [0, 1, 2, 3], False)
+        k_sum(30, 1, [0, 1, 2, 3], False)
+        k_sum((31, 0), 1, [0, 1], False)
+        k_sum((31, 1), 1, [2, 3], True)
         finish(1)

@@ -80,10 +80,10 @@ def tile_dimenettripletbilinear_kernel(tc, m_kj_bytes, m_kj_scale, m_ji, sbf, w_
         nc.vector.tensor_scalar(out=ident4[:], in0=ident[:], scalar1=4.0, scalar2=None, op0=MULT)
 
         def bank():
-            bank_t = psum.tile([P, 512], F32, name="bank", bufs=6)
+            bank_t = psum.tile([P, 512], F32, name="bank", bufs=5)
             return bank_t
 
-        scale_pair = const.tile([P, 2 * D], F32, name="scale_pair", align_bytes=64)
+        scale_split = const.tile([P, D], F32, name="scale_split", align_bytes=64)
 
         def scale_spread():
             b_t = bank()
@@ -91,11 +91,8 @@ def tile_dimenettripletbilinear_kernel(tc, m_kj_bytes, m_kj_scale, m_ji, sbf, w_
                 nc.tensor.transpose(b_t[:, j * P:(j + 1) * P], scale4[:, j:j + 1].to_broadcast([P, P]), ident[:])
             return b_t
 
-        def scale_copy_plain(b_t):
-            nc.scalar.copy(out=scale_pair[:, 0:D].rearrange("q (p j) -> q p j", j=4), in_=b_t[:].rearrange("q (j p) -> q p j", j=4))
-
         def scale_copy_split(b_t):
-            nc.scalar.copy(out=scale_pair[:, D:2 * D].rearrange("q (u p e) -> q u p e", u=2, e=2), in_=b_t[:].rearrange("q (u e p) -> q u p e", u=2, e=2))
+            nc.scalar.copy(out=scale_split[:].rearrange("q (u p e) -> q u p e", u=2, e=2), in_=b_t[:].rearrange("q (u e p) -> q u p e", u=2, e=2))
 
         gain_ps = psum.tile([P, 512], F32, name="gain_ps")
 
@@ -137,46 +134,36 @@ def tile_dimenettripletbilinear_kernel(tc, m_kj_bytes, m_kj_scale, m_ji, sbf, w_
 
         casts, mw, mtr, mq, mcode, yps, xs, pts, ptr, pqs, pcode, mm, tts, aggs = ({} for a in range(14))
 
-        split = {}
-
         def cast_tile(t):
             if t // 2 not in casts:
                 c_t = work.tile([P, 2 * D], BF16, name="cast", bufs=3, align_bytes=64)
                 casts[t // 2] = c_t
             return casts[t // 2][:, t % 2 * D:(t % 2 + 1) * D]
 
-        def cast_vector(t):
+        def cast_split(t):
             nc.vector.tensor_scalar(
                 out=cast_tile(t).rearrange("p (u w e) -> p w u e", u=2, e=2), in0=mbytes[t].rearrange("p (w u e) -> p w u e", u=2, e=2),
                 scalar1=one[:], scalar2=None, op0=MULT,
             )
-            split[t] = True
 
-        def cast_scalar(t):
-            nc.scalar.copy(out=cast_tile(t), in_=mbytes[t])
-            split[t] = False
+        def cast_plain(engine, t):
+            engine(out=cast_tile(t), in_=mbytes[t])
 
         def product_gpsimd(j):
             mw_t = work.tile([P, 2 * D], BF16, name="mw", bufs=2, align_bytes=64)
-            if split[2 * j]:
-                nc.gpsimd.tensor_tensor(
-                    out=mw_t[:].rearrange("p (a k) -> p a k", a=2), in0=casts[j][:].rearrange("p (a k) -> p a k", a=2),
-                    in1=scale_pair[:, D:2 * D].unsqueeze(1).to_broadcast([P, 2, D]), op=MULT,
-                )
-            else:
-                nc.gpsimd.tensor_tensor(out=mw_t[:], in0=casts[j][:], in1=scale_pair[:], op=MULT)
+            nc.gpsimd.tensor_tensor(
+                out=mw_t[:].rearrange("p (u a w e) -> p u a w e", u=2, a=2, e=2),
+                in0=casts[j][:].rearrange("p (a w u e) -> p u a w e", a=2, u=2, e=2),
+                in1=scale_split[:].rearrange("p (u w e) -> p u w e", u=2, e=2).unsqueeze(2).to_broadcast([P, 2, 2, P, 2]), op=MULT,
+            )
             mw[j] = mw_t
-
-        def tile_transpose(b_t, col, source, t):
-            words = source[:, t % 2 * D:(t % 2 + 1) * D].bitcast(F32)
-            for u in range(2):
-                half = words[:, u * P:(u + 1) * P] if split[t] else words[:, u:256:2]
-                nc.tensor.transpose(b_t[:, col + u * P:col + (u + 1) * P], half, ident[:])
 
         def m_transpose(j):
             b_t = bank()
+            words = mw[j][:].bitcast(F32)
             for a in range(2):
-                tile_transpose(b_t, a * 256, mw[j], 2 * j + a)
+                for u in range(2):
+                    nc.tensor.transpose(b_t[:, (2 * a + u) * P:(2 * a + u + 1) * P], words[:, (2 * u + a) * P:(2 * u + a + 1) * P], ident[:])
             mtr[j] = b_t
 
         def m_copy(j):
@@ -231,6 +218,7 @@ def tile_dimenettripletbilinear_kernel(tc, m_kj_bytes, m_kj_scale, m_ji, sbf, w_
             for a in range(2 * g0, 2 * g1):
                 nc.tensor.transpose(b_t[:, a * P:(a + 1) * P], words[:, a * P:(a + 1) * P], ident[:])
             ptr[t] = b_t
+            ptr[t, g0] = b_t
 
         def p_copy(t):
             c, a = t // 2, t % 2
@@ -260,12 +248,12 @@ def tile_dimenettripletbilinear_kernel(tc, m_kj_bytes, m_kj_scale, m_ji, sbf, w_
             mm[c, b] = mm_t
 
         def silu2(key, width):
-            t_t = work.tile([P, 4 * P], F32, name="tt", bufs=5, align_bytes=64)
+            t_t = work.tile([P, 4 * P], F32, name="tt", bufs=8, align_bytes=64)
             nc.scalar.activation(out=t_t[:, 0:width], in_=mm[key][:, 0:width], func=SILU)
             tts[key] = t_t
 
         def agg_open(h):
-            agg_t = psum.tile([P, D], F32, name="agg")
+            agg_t = psum.tile([P, D], F32, name="agg", bufs=2)
             nc.tensor.matmul(out=agg_t[:], lhsT=ident4[:], rhs=mji[:, h, :], start=True, stop=False)
             aggs[h] = agg_t
 
@@ -277,8 +265,6 @@ def tile_dimenettripletbilinear_kernel(tc, m_kj_bytes, m_kj_scale, m_ji, sbf, w_
                 )
 
         def k_sum_pair(c, b):
-            if c % 8 == 0 and b == 0:
-                agg_open(c // 8)
             k_sum((c, b), c // 8, [2 * b, 2 * b, 2 * b + 1, 2 * b + 1], c == 7 and b == 1)
 
         def finish(h):
@@ -290,7 +276,9 @@ def tile_dimenettripletbilinear_kernel(tc, m_kj_bytes, m_kj_scale, m_ji, sbf, w_
 
         def head_transpose(t):
             b_t = bank()
-            tile_transpose(b_t, 0, casts[t // 2], t)
+            words = cast_tile(t).bitcast(F32)
+            for u in range(2):
+                nc.tensor.transpose(b_t[:, u * P:(u + 1) * P], words[:, u * P:(u + 1) * P], ident[:])
             head[t] = b_t
 
         def head_product(t):
@@ -303,10 +291,10 @@ def tile_dimenettripletbilinear_kernel(tc, m_kj_bytes, m_kj_scale, m_ji, sbf, w_
                 in1=scale4[:].rearrange("p (u e) -> p u e", u=2).unsqueeze(1).to_broadcast([P, P, 2, 2]), op=MULT,
             )
 
-        cast_vector(0)
+        cast_split(0)
         scale_bank = scale_spread()
         head_transpose(0)
-        cast_vector(1)
+        cast_split(1)
         head_transpose(1)
         gain_spread()
         wd_interleave()
@@ -314,71 +302,26 @@ def tile_dimenettripletbilinear_kernel(tc, m_kj_bytes, m_kj_scale, m_ji, sbf, w_
         scale_copy_split(scale_bank)
         head_product(0)
         wd_quantise()
-        cast_vector(2)
+        cast_split(2)
         m_quant(0, 0, 1)
         stage1(0, 0, 1)
         silu1(0, 0, 1)
         head_product(1)
-        scale_copy_plain(scale_bank)
-        cast_vector(3)
-        cast_vector(4)
+        cast_split(3)
+        cast_plain(nc.vector.tensor_copy, 4)
         head_transpose(2)
         m_quant(0, 1, 2)
         head_transpose(3)
         stage1(0, 1, 2)
         wb_interleave(1, 0)
         silu1(0, 1, 2)
-        cast_vector(5)
+        cast_plain(nc.vector.tensor_copy, 5)
         product_gpsimd(2)
         p_ops(0, 0, NB)
         head_product(2)
         head_product(3)
         wb_interleave(0, 1)
-        p_transpose(0, 0, 2)
-        cast_scalar(6)
-        p_copy(0)
-
-        for j in range(1, PAIRS - 1):
-            if j == 1:
-                wb_quantise(0, 0)
-            m_quant(j, 0, 2)
-            if j == 1:
-                wb_quantise(1, 0)
-            if j == 2:
-                wb_quantise(0, 1)
-                wb_quantise(1, 1)
-            if j >= 2:
-                p_quant(j - 2)
-            if j + 2 < PAIRS:
-                cast_vector(2 * j + 5)
-                product_gpsimd(j + 2)
-            stage1(j, 0, 2)
-            silu1(j, 0, 2)
-            if j >= 2:
-                stage2(j - 2, 0)
-                silu2((j - 2, 0), 512)
-            if j == 1:
-                wb_interleave(1, 1)
-            p_ops(2 * j - 1, 0, NB)
-            m_transpose(j + 1)
-            m_copy(j + 1)
-            p_transpose(2 * j - 1, 0, 2)
-            p_copy(2 * j - 1)
-            if j >= 3:
-                k_sum_pair(j - 3, 1)
-            if j == 10:
-                finish(0)
-            if j + 3 < PAIRS:
-                cast_scalar(2 * j + 6)
-            if j >= 2:
-                stage2(j - 2, 1)
-                silu2((j - 2, 1), 512)
-            p_ops(2 * j, 0, NB)
-            if j >= 2:
-                k_sum_pair(j - 2, 0)
-            if j < PAIRS - 2:
-                p_transpose(2 * j, 0, 2)
-                p_copy(2 * j)
+        cast_plain(nc.scalar.copy, 6)
 
         def single_copy(engine, t, g0, g1):
             if g0 == 0:
@@ -386,10 +329,6 @@ def tile_dimenettripletbilinear_kernel(tc, m_kj_bytes, m_kj_scale, m_ji, sbf, w_
                 pqs[t] = pq_t
             dst = pqs[t][:, 0:NBC].bitcast(F32).rearrange("p (g r u) -> p g r u", g=2, u=2)[:, g0:g1]
             engine(out=dst, in_=ptr[t, g0][:].rearrange("p (g u r) -> p g r u", g=2, u=2)[:, g0:g1])
-
-        def single_transpose(t, g0, g1):
-            p_transpose(t, g0, g1)
-            ptr[t, g0] = ptr[t]
 
         def single_quant(t, g0, g1):
             if g0 == 0:
@@ -413,35 +352,79 @@ def tile_dimenettripletbilinear_kernel(tc, m_kj_bytes, m_kj_scale, m_ji, sbf, w_
                     single_pass(t, t, d, d, g, g == 0, g == 1)
             silu2(t, 512)
 
-        single_transpose(28, 0, 2)
-        single_copy(nc.scalar.copy, 28, 0, 2)
+        for j in range(1, PAIRS - 1):
+            if j == 1:
+                wb_quantise(0, 0)
+            m_quant(j, 0, 2)
+            if j == 2:
+                wb_quantise(0, 1)
+                wb_quantise(1, 1)
+            if j + 2 < PAIRS:
+                cast_plain(nc.vector.tensor_copy, 2 * j + 5)
+                product_gpsimd(j + 2)
+            if j == 1:
+                wb_quantise(1, 0)
+            if j >= 2:
+                p_quant(j - 2)
+            if j >= 3:
+                k_sum_pair(j - 3, 0)
+                silu2((j - 3, 1), 512)
+            if j + 3 < PAIRS:
+                cast_plain(nc.scalar.copy, 2 * j + 6)
+            p_transpose(2 * j - 2, 0, 2)
+            p_copy(2 * j - 2)
+            m_transpose(j + 1)
+            stage1(j, 0, 2)
+            silu1(j, 0, 2)
+            m_copy(j + 1)
+            if j == 1:
+                wb_interleave(1, 1)
+                agg_open(0)
+                agg_open(1)
+            if j >= 2:
+                stage2(j - 2, 0)
+                silu2((j - 2, 0), 512)
+            p_ops(2 * j - 1, 0, NB)
+            if j >= 3:
+                k_sum_pair(j - 3, 1)
+            p_transpose(2 * j - 1, 0, 2)
+            p_copy(2 * j - 1)
+            if j >= 2:
+                stage2(j - 2, 1)
+            p_ops(2 * j, 0, NB)
+
         m_quant(15, 0, 2)
         p_quant(13)
+        k_sum_pair(12, 0)
+        silu2((12, 1), 512)
+        p_transpose(28, 0, 2)
+        single_copy(nc.scalar.copy, 28, 0, 2)
         stage1(15, 0, 2)
         silu1(15, 0, 2)
         stage2(13, 0)
+        stage2(13, 1)
         silu2((13, 0), 512)
         p_ops(29, 0, NB)
+        p_transpose(29, 0, 2)
         k_sum_pair(12, 1)
-        single_transpose(29, 0, 2)
         single_copy(nc.scalar.copy, 29, 0, 2)
-        single_quant(28, 0, 2)
-        stage2(13, 1)
         silu2((13, 1), 512)
+        single_quant(28, 0, 2)
         single_stage2(28)
         p_ops(30, 0, NB)
         k_sum_pair(13, 0)
-        single_transpose(30, 0, 2)
+        p_transpose(30, 0, 2)
         single_copy(nc.scalar.copy, 30, 0, 2)
+        k_sum_pair(13, 1)
         single_quant(29, 0, 2)
         single_stage2(29)
+        finish(0)
         p_ops(31, 0, NB)
-        k_sum_pair(13, 1)
-        single_transpose(31, 0, 1)
+        p_transpose(31, 0, 1)
+        p_transpose(31, 1, 2)
         k_sum(28, 1, [0, 1, 2, 3], False)
-        single_transpose(31, 1, 2)
-        single_copy(nc.vector.tensor_copy, 31, 0, 1)
         single_quant(30, 0, 2)
+        single_copy(nc.vector.tensor_copy, 31, 0, 1)
         single_copy(nc.vector.tensor_copy, 31, 1, 2)
         single_quant(31, 0, 1)
         single_quant(31, 1, 2)
@@ -454,8 +437,8 @@ def tile_dimenettripletbilinear_kernel(tc, m_kj_bytes, m_kj_scale, m_ji, sbf, w_
                     single_pass(31, (31, b), i, 2 * b + i, g, g == 0 and i == 0, g == 1 and i == 1)
         for b in range(2):
             silu2((31, b), 256)
-        k_sum(29, 1, [0, 1, 2, 3], False)
-        k_sum(30, 1, [0, 1, 2, 3], False)
+        for t in range(29, 31):
+            k_sum(t, 1, [0, 1, 2, 3], False)
         k_sum((31, 0), 1, [0, 1], False)
         k_sum((31, 1), 1, [2, 3], True)
         finish(1)

@@ -76,6 +76,8 @@ def tile_dimenettripletbilinear_kernel(tc, m_kj_bytes, m_kj_scale, m_ji, sbf, w_
         make_identity(nc, ident[:])
         one = const.tile([P, 1], F32, name="one")
         nc.vector.memset(one[:], 1.0)
+        warm = const.tile([P, 1], F32, name="warm")
+        nc.scalar.activation(out=warm[:], in_=one[:], func=SILU)
         ident4 = const.tile([P, P], BF16, name="ident4", align_bytes=64)
         nc.vector.tensor_scalar(out=ident4[:], in0=ident[:], scalar1=4.0, scalar2=None, op0=MULT)
 

@@ -61,8 +61,8 @@ def tile_dimenettripletbilinear_kernel(tc, m_kj_bytes, m_kj_scale, m_ji, sbf, w_
             nc.sync.dma_start(out=wb_t[:], in_=wb_hbm[g][:, :, b * 256:(b + 1) * 256])
             wb_raw[g, b] = wb_t
 
-        load_wb(0, 0)
         load_bytes(*LOADS[1])
+        load_wb(0, 0)
         load_wb(1, 0)
         load_wb(0, 1)
         load_wb(1, 1)
@@ -82,7 +82,7 @@ def tile_dimenettripletbilinear_kernel(tc, m_kj_bytes, m_kj_scale, m_ji, sbf, w_
         nc.vector.tensor_scalar(out=ident4[:], in0=ident[:], scalar1=4.0, scalar2=None, op0=MULT)
 
         def bank():
-            bank_t = psum.tile([P, 512], F32, name="bank", bufs=5)
+            bank_t = psum.tile([P, 512], F32, name="bank", bufs=4)
             return bank_t
 
         scale_split = const.tile([P, D], F32, name="scale_split", align_bytes=64)
@@ -110,7 +110,7 @@ def tile_dimenettripletbilinear_kernel(tc, m_kj_bytes, m_kj_scale, m_ji, sbf, w_
 
         def wd_interleave():
             for u in range(2):
-                nc.vector.tensor_copy(
+                nc.scalar.copy(
                     out=wd_grp[:].rearrange("p (u i e) j -> p u i e j", u=2, e=2)[:, u],
                     in_=wd_raw[:].rearrange("p j (i u e) -> p u i e j", u=2, e=2)[:, u],
                 )
@@ -254,25 +254,33 @@ def tile_dimenettripletbilinear_kernel(tc, m_kj_bytes, m_kj_scale, m_ji, sbf, w_
             nc.scalar.activation(out=t_t[:, 0:width], in_=mm[key][:, 0:width], func=SILU)
             tts[key] = t_t
 
-        def agg_open(h):
-            agg_t = psum.tile([P, D], F32, name="agg", bufs=2)
-            nc.tensor.matmul(out=agg_t[:], lhsT=ident4[:], rhs=mji[:, h, :], start=True, stop=False)
-            aggs[h] = agg_t
+        def agg_open(h, d0, d1):
+            agg_t = psum.tile([P, D], F32, name="agg", bufs=3)
+            nc.tensor.matmul(out=agg_t[:, d0 * P:d1 * P], lhsT=ident4[:], rhs=mji[:, h, d0 * P:d1 * P], start=True, stop=False)
+            for d in range(d0, d1):
+                aggs[h, d] = agg_t
 
         def k_sum(key, h, dims, last):
             for i, d in enumerate(dims):
                 nc.tensor.matmul(
-                    out=aggs[h][:, d * P:(d + 1) * P], lhsT=tts[key][:, i * P:(i + 1) * P], rhs=ident[:],
+                    out=aggs[h, d][:, d * P:(d + 1) * P], lhsT=tts[key][:, i * P:(i + 1) * P], rhs=ident[:],
                     is_transpose=True, start=False, stop=(last and i == len(dims) - 1),
                 )
 
         def k_sum_pair(c, b):
             k_sum((c, b), c // 8, [2 * b, 2 * b, 2 * b + 1, 2 * b + 1], c == 7 and b == 1)
 
-        def finish(h):
-            o_t = work.tile([P, D], F32, name="o", bufs=2, align_bytes=64)
-            nc.scalar.activation(out=o_t[:], in_=aggs[h][:], func=COPY, scale=0.25)
-            nc.sync.dma_start(out=out[h * P:(h + 1) * P, :], in_=o_t[:])
+        def finish_scalar(h, d0, d1):
+            cols = slice(d0 * P, d1 * P)
+            o_t = const.tile([P, D], F32, name="o%d%d" % (h, d0), align_bytes=64)
+            nc.scalar.activation(out=o_t[:, cols], in_=aggs[h, d0][:, cols], func=COPY, scale=0.25)
+            nc.sync.dma_start(out=out[h * P:(h + 1) * P, cols], in_=o_t[:, cols])
+
+        def finish_vector(h, d0, d1):
+            cols = slice(d0 * P, d1 * P)
+            o_t = const.tile([P, D], F32, name="o%d%d" % (h, d0), align_bytes=64)
+            nc.vector.tensor_scalar(out=o_t[:, cols], in0=aggs[h, d0][:, cols], scalar1=0.25, scalar2=None, op0=MULT)
+            nc.sync.dma_start(out=out[h * P:(h + 1) * P, cols], in_=o_t[:, cols])
 
         head = {}
 
@@ -294,31 +302,31 @@ def tile_dimenettripletbilinear_kernel(tc, m_kj_bytes, m_kj_scale, m_ji, sbf, w_
             )
 
         cast_split(0)
-        scale_bank = scale_spread()
         head_transpose(0)
+        scale_bank = scale_spread()
         cast_split(1)
         head_transpose(1)
         gain_spread()
         wd_interleave()
+        cast_split(2)
+        cast_plain(nc.scalar.copy, 4)
         wb_interleave(0, 0)
         scale_copy_split(scale_bank)
         head_product(0)
         wd_quantise()
-        cast_split(2)
         m_quant(0, 0, 1)
         stage1(0, 0, 1)
         silu1(0, 0, 1)
         head_product(1)
         cast_split(3)
-        cast_plain(nc.vector.tensor_copy, 4)
         head_transpose(2)
+        cast_plain(nc.vector.tensor_copy, 5)
+        product_gpsimd(2)
         m_quant(0, 1, 2)
         head_transpose(3)
         stage1(0, 1, 2)
         wb_interleave(1, 0)
         silu1(0, 1, 2)
-        cast_plain(nc.vector.tensor_copy, 5)
-        product_gpsimd(2)
         p_ops(0, 0, NB)
         head_product(2)
         head_product(3)
@@ -381,8 +389,6 @@ def tile_dimenettripletbilinear_kernel(tc, m_kj_bytes, m_kj_scale, m_ji, sbf, w_
             m_copy(j + 1)
             if j == 1:
                 wb_interleave(1, 1)
-                agg_open(0)
-                agg_open(1)
             if j >= 2:
                 stage2(j - 2, 0)
                 silu2((j - 2, 0), 512)
@@ -391,6 +397,10 @@ def tile_dimenettripletbilinear_kernel(tc, m_kj_bytes, m_kj_scale, m_ji, sbf, w_
                 k_sum_pair(j - 3, 1)
             p_transpose(2 * j - 1, 0, 2)
             p_copy(2 * j - 1)
+            if j == 1:
+                agg_open(0, 0, 4)
+                agg_open(1, 0, 2)
+                agg_open(1, 2, 4)
             if j >= 2:
                 stage2(j - 2, 1)
             p_ops(2 * j, 0, NB)
@@ -414,13 +424,13 @@ def tile_dimenettripletbilinear_kernel(tc, m_kj_bytes, m_kj_scale, m_ji, sbf, w_
         single_quant(28, 0, 2)
         single_stage2(28)
         p_ops(30, 0, NB)
-        k_sum_pair(13, 0)
         p_transpose(30, 0, 2)
+        k_sum_pair(13, 0)
         single_copy(nc.scalar.copy, 30, 0, 2)
         k_sum_pair(13, 1)
         single_quant(29, 0, 2)
         single_stage2(29)
-        finish(0)
+        finish_scalar(0, 0, 4)
         p_ops(31, 0, NB)
         p_transpose(31, 0, 1)
         p_transpose(31, 1, 2)
@@ -441,6 +451,7 @@ def tile_dimenettripletbilinear_kernel(tc, m_kj_bytes, m_kj_scale, m_ji, sbf, w_
             silu2((31, b), 256)
         for t in range(29, 31):
             k_sum(t, 1, [0, 1, 2, 3], False)
-        k_sum((31, 0), 1, [0, 1], False)
+        k_sum((31, 0), 1, [0, 1], True)
+        finish_vector(1, 0, 2)
         k_sum((31, 1), 1, [2, 3], True)
-        finish(1)
+        finish_scalar(1, 2, 4)

@@ -21,7 +21,7 @@ COPY = mybir.ActivationFunctionType.Copy
 TILES = 32
 PAIRS = 16
 HALF = 16
-FIRST_GPSIMD_PAIR = 2
+SCALAR_CAST = 384
 LOADS = [(0, 2), (2, 6), (6, 10), (10, 16), (16, 24), (24, 32)]
 
 
@@ -41,8 +41,8 @@ def tile_dimenettripletbilinear_kernel(tc, m_kj_bytes, m_kj_scale, m_ji, sbf, w_
             nc.sync.dma_start(
                 out=t_t[:], in_=m_kj_bytes[h * P:(h + 1) * P, t0 - h * HALF:t1 - h * HALF, :].rearrange("e k d -> e (k d)")
             )
-            for t in range(t0, t1):
-                mbytes[t] = t_t[:, (t - t0) * D:(t - t0 + 1) * D].bitcast(FP8)
+            for t in range(t0, t1, 2):
+                mbytes[t // 2] = t_t[:, (t - t0) * D:(t - t0 + 2) * D].bitcast(FP8)
 
         load_bytes(*LOADS[0])
         scale4 = const.tile([P, 4], F32, name="scale4", align_bytes=64)
@@ -110,7 +110,7 @@ def tile_dimenettripletbilinear_kernel(tc, m_kj_bytes, m_kj_scale, m_ji, sbf, w_
 
         def wd_interleave():
             for u in range(2):
-                nc.scalar.copy(
+                nc.vector.tensor_copy(
                     out=wd_grp[:].rearrange("p (u i e) j -> p u i e j", u=2, e=2)[:, u],
                     in_=wd_raw[:].rearrange("p j (i u e) -> p u i e j", u=2, e=2)[:, u],
                 )
@@ -136,20 +136,24 @@ def tile_dimenettripletbilinear_kernel(tc, m_kj_bytes, m_kj_scale, m_ji, sbf, w_
 
         casts, mw, mtr, mq, mcode, yps, xs, pts, ptr, pqs, pcode, mm, tts, aggs = ({} for a in range(14))
 
-        def cast_tile(t):
-            if t // 2 not in casts:
+        def cast_tile(j):
+            if j not in casts:
                 c_t = work.tile([P, 2 * D], BF16, name="cast", bufs=3, align_bytes=64)
-                casts[t // 2] = c_t
-            return casts[t // 2][:, t % 2 * D:(t % 2 + 1) * D]
+                casts[j] = c_t
+            return casts[j]
 
         def cast_split(t):
+            cols = slice(t % 2 * D, (t % 2 + 1) * D)
             nc.vector.tensor_scalar(
-                out=cast_tile(t).rearrange("p (u w e) -> p w u e", u=2, e=2), in0=mbytes[t].rearrange("p (w u e) -> p w u e", u=2, e=2),
-                scalar1=one[:], scalar2=None, op0=MULT,
+                out=cast_tile(t // 2)[:, cols].rearrange("p (u w e) -> p w u e", u=2, e=2),
+                in0=mbytes[t // 2][:, cols].rearrange("p (w u e) -> p w u e", u=2, e=2), scalar1=one[:], scalar2=None, op0=MULT,
             )
 
-        def cast_plain(engine, t):
-            engine(out=cast_tile(t), in_=mbytes[t])
+        def cast_scalar(j):
+            nc.scalar.copy(out=cast_tile(j)[:, 0:SCALAR_CAST], in_=mbytes[j][:, 0:SCALAR_CAST])
+
+        def cast_vector(j):
+            nc.vector.tensor_copy(out=cast_tile(j)[:, SCALAR_CAST:2 * D], in_=mbytes[j][:, SCALAR_CAST:2 * D])
 
         def product_gpsimd(j):
             mw_t = work.tile([P, 2 * D], BF16, name="mw", bufs=2, align_bytes=64)
@@ -286,7 +290,7 @@ def tile_dimenettripletbilinear_kernel(tc, m_kj_bytes, m_kj_scale, m_ji, sbf, w_
 
         def head_transpose(t):
             b_t = bank()
-            words = cast_tile(t).bitcast(F32)
+            words = casts[t // 2][:, t % 2 * D:(t % 2 + 1) * D].bitcast(F32)
             for u in range(2):
                 nc.tensor.transpose(b_t[:, u * P:(u + 1) * P], words[:, u * P:(u + 1) * P], ident[:])
             head[t] = b_t
@@ -309,7 +313,7 @@ def tile_dimenettripletbilinear_kernel(tc, m_kj_bytes, m_kj_scale, m_ji, sbf, w_
         gain_spread()
         wd_interleave()
         cast_split(2)
-        cast_plain(nc.scalar.copy, 4)
+        cast_scalar(2)
         wb_interleave(0, 0)
         scale_copy_split(scale_bank)
         head_product(0)
@@ -320,7 +324,7 @@ def tile_dimenettripletbilinear_kernel(tc, m_kj_bytes, m_kj_scale, m_ji, sbf, w_
         head_product(1)
         cast_split(3)
         head_transpose(2)
-        cast_plain(nc.vector.tensor_copy, 5)
+        cast_vector(2)
         product_gpsimd(2)
         m_quant(0, 1, 2)
         head_transpose(3)
@@ -331,7 +335,7 @@ def tile_dimenettripletbilinear_kernel(tc, m_kj_bytes, m_kj_scale, m_ji, sbf, w_
         head_product(2)
         head_product(3)
         wb_interleave(0, 1)
-        cast_plain(nc.scalar.copy, 6)
+        cast_scalar(3)
 
         def single_copy(engine, t, g0, g1):
             if g0 == 0:
@@ -370,7 +374,7 @@ def tile_dimenettripletbilinear_kernel(tc, m_kj_bytes, m_kj_scale, m_ji, sbf, w_
                 wb_quantise(0, 1)
                 wb_quantise(1, 1)
             if j + 2 < PAIRS:
-                cast_plain(nc.vector.tensor_copy, 2 * j + 5)
+                cast_vector(j + 2)
                 product_gpsimd(j + 2)
             if j == 1:
                 wb_quantise(1, 0)
@@ -380,7 +384,7 @@ def tile_dimenettripletbilinear_kernel(tc, m_kj_bytes, m_kj_scale, m_ji, sbf, w_
                 k_sum_pair(j - 3, 0)
                 silu2((j - 3, 1), 512)
             if j + 3 < PAIRS:
-                cast_plain(nc.scalar.copy, 2 * j + 6)
+                cast_scalar(j + 3)
             p_transpose(2 * j - 2, 0, 2)
             p_copy(2 * j - 2)
             m_transpose(j + 1)

@@ -21,7 +21,7 @@ COPY = mybir.ActivationFunctionType.Copy
 TILES = 32
 PAIRS = 16
 HALF = 16
-SCALAR_CAST = 384
+SCALAR_CAST = 512
 LOADS = [(0, 2), (2, 6), (6, 10), (10, 16), (16, 24), (24, 32)]
 
 
@@ -82,7 +82,7 @@ def tile_dimenettripletbilinear_kernel(tc, m_kj_bytes, m_kj_scale, m_ji, sbf, w_
         nc.vector.tensor_scalar(out=ident4[:], in0=ident[:], scalar1=4.0, scalar2=None, op0=MULT)
 
         def bank():
-            bank_t = psum.tile([P, 512], F32, name="bank", bufs=4)
+            bank_t = psum.tile([P, 512], F32, name="bank", bufs=5)
             return bank_t
 
         scale_split = const.tile([P, D], F32, name="scale_split", align_bytes=64)
@@ -110,7 +110,7 @@ def tile_dimenettripletbilinear_kernel(tc, m_kj_bytes, m_kj_scale, m_ji, sbf, w_
 
         def wd_interleave():
             for u in range(2):
-                nc.vector.tensor_copy(
+                nc.scalar.copy(
                     out=wd_grp[:].rearrange("p (u i e) j -> p u i e j", u=2, e=2)[:, u],
                     in_=wd_raw[:].rearrange("p j (i u e) -> p u i e j", u=2, e=2)[:, u],
                 )
@@ -259,7 +259,7 @@ def tile_dimenettripletbilinear_kernel(tc, m_kj_bytes, m_kj_scale, m_ji, sbf, w_
             tts[key] = t_t
 
         def agg_open(h, d0, d1):
-            agg_t = psum.tile([P, D], F32, name="agg", bufs=3)
+            agg_t = psum.tile([P, D], F32, name="agg", bufs=2)
             nc.tensor.matmul(out=agg_t[:, d0 * P:d1 * P], lhsT=ident4[:], rhs=mji[:, h, d0 * P:d1 * P], start=True, stop=False)
             for d in range(d0, d1):
                 aggs[h, d] = agg_t
@@ -369,6 +369,8 @@ def tile_dimenettripletbilinear_kernel(tc, m_kj_bytes, m_kj_scale, m_ji, sbf, w_
         for j in range(1, PAIRS - 1):
             if j == 1:
                 wb_quantise(0, 0)
+            if 2 <= j < PAIRS - 2:
+                cast_scalar(j + 2)
             m_quant(j, 0, 2)
             if j == 2:
                 wb_quantise(0, 1)
@@ -383,8 +385,6 @@ def tile_dimenettripletbilinear_kernel(tc, m_kj_bytes, m_kj_scale, m_ji, sbf, w_
             if j >= 3:
                 k_sum_pair(j - 3, 0)
                 silu2((j - 3, 1), 512)
-            if j + 3 < PAIRS:
-                cast_scalar(j + 3)
             p_transpose(2 * j - 2, 0, 2)
             p_copy(2 * j - 2)
             m_transpose(j + 1)
@@ -403,8 +403,7 @@ def tile_dimenettripletbilinear_kernel(tc, m_kj_bytes, m_kj_scale, m_ji, sbf, w_
             p_copy(2 * j - 1)
             if j == 1:
                 agg_open(0, 0, 4)
-                agg_open(1, 0, 2)
-                agg_open(1, 2, 4)
+                agg_open(1, 0, 4)
             if j >= 2:
                 stage2(j - 2, 1)
             p_ops(2 * j, 0, NB)
@@ -455,7 +454,7 @@ def tile_dimenettripletbilinear_kernel(tc, m_kj_bytes, m_kj_scale, m_ji, sbf, w_
             silu2((31, b), 256)
         for t in range(29, 31):
             k_sum(t, 1, [0, 1, 2, 3], False)
-        k_sum((31, 0), 1, [0, 1], True)
-        finish_vector(1, 0, 2)
+        k_sum((31, 0), 1, [0, 1], False)
         k_sum((31, 1), 1, [2, 3], True)
-        finish_scalar(1, 2, 4)
+        finish_vector(1, 0, 2)
+        finish_vector(1, 2, 4)

@@ -21,7 +21,7 @@ COPY = mybir.ActivationFunctionType.Copy
 TILES = 32
 PAIRS = 16
 HALF = 16
-SCALAR_CAST = 512
+SCALAR_CAST = 768
 LOADS = [(0, 2), (2, 6), (6, 10), (10, 16), (16, 24), (24, 32)]
 
 

@@ -15,13 +15,14 @@ U8 = mybir.dt.uint8
 FP8 = mybir.dt.float8_e4m3fn
 FP8X4 = mybir.dt.float8_e4m3fn_x4
 MULT = mybir.AluOpType.mult
+ADD = mybir.AluOpType.add
 SILU = mybir.ActivationFunctionType.Silu
 COPY = mybir.ActivationFunctionType.Copy
 
 TILES = 32
 PAIRS = 16
 HALF = 16
-SCALAR_CAST = 768
+SCALAR_CAST = 832
 LOADS = [(0, 2), (2, 6), (6, 10), (10, 16), (16, 24), (24, 32)]
 
 
@@ -110,7 +111,7 @@ def tile_dimenettripletbilinear_kernel(tc, m_kj_bytes, m_kj_scale, m_ji, sbf, w_
 
         def wd_interleave():
             for u in range(2):
-                nc.scalar.copy(
+                nc.vector.tensor_copy(
                     out=wd_grp[:].rearrange("p (u i e) j -> p u i e j", u=2, e=2)[:, u],
                     in_=wd_raw[:].rearrange("p j (i u e) -> p u i e j", u=2, e=2)[:, u],
                 )
@@ -120,12 +121,9 @@ def tile_dimenettripletbilinear_kernel(tc, m_kj_bytes, m_kj_scale, m_ji, sbf, w_
 
         wb_grp, wb_codes, wb_sc = {}, {}, {}
 
-        def wb_interleave(g, b):
+        def wb_interleave(engine, g, b):
             grp_t = const.tile([P, 256, 4], BF16, name="wb_grp%d%d" % (g, b), align_bytes=64)
-            nc.scalar.copy(
-                out=grp_t[:].rearrange("p (c i) j -> p c j i", i=4),
-                in_=wb_raw[g, b][:].rearrange("p j (c i) -> p c j i", i=4),
-            )
+            engine(out=grp_t[:], in_=wb_raw[g, b][:].rearrange("p j d -> p d j"))
             wb_grp[g, b] = grp_t
 
         def wb_quantise(g, b):
@@ -149,8 +147,8 @@ def tile_dimenettripletbilinear_kernel(tc, m_kj_bytes, m_kj_scale, m_ji, sbf, w_
                 in0=mbytes[t // 2][:, cols].rearrange("p (w u e) -> p w u e", u=2, e=2), scalar1=one[:], scalar2=None, op0=MULT,
             )
 
-        def cast_scalar(j):
-            nc.scalar.copy(out=cast_tile(j)[:, 0:SCALAR_CAST], in_=mbytes[j][:, 0:SCALAR_CAST])
+        def cast_scalar(j, width):
+            nc.scalar.copy(out=cast_tile(j)[:, 0:width], in_=mbytes[j][:, 0:width])
 
         def cast_vector(j):
             nc.vector.tensor_copy(out=cast_tile(j)[:, SCALAR_CAST:2 * D], in_=mbytes[j][:, SCALAR_CAST:2 * D])
@@ -292,7 +290,8 @@ def tile_dimenettripletbilinear_kernel(tc, m_kj_bytes, m_kj_scale, m_ji, sbf, w_
             b_t = bank()
             words = casts[t // 2][:, t % 2 * D:(t % 2 + 1) * D].bitcast(F32)
             for u in range(2):
-                nc.tensor.transpose(b_t[:, u * P:(u + 1) * P], words[:, u * P:(u + 1) * P], ident[:])
+                half = words[:, u * P:(u + 1) * P] if t < 2 else words[:, u:256:2]
+                nc.tensor.transpose(b_t[:, u * P:(u + 1) * P], half, ident[:])
             head[t] = b_t
 
         def head_product(t):
@@ -312,30 +311,29 @@ def tile_dimenettripletbilinear_kernel(tc, m_kj_bytes, m_kj_scale, m_ji, sbf, w_
         head_transpose(1)
         gain_spread()
         wd_interleave()
-        cast_split(2)
-        cast_scalar(2)
-        wb_interleave(0, 0)
+        cast_scalar(1, 2 * D)
         scale_copy_split(scale_bank)
+        cast_scalar(2, SCALAR_CAST)
         head_product(0)
         wd_quantise()
         m_quant(0, 0, 1)
         stage1(0, 0, 1)
         silu1(0, 0, 1)
         head_product(1)
-        cast_split(3)
         head_transpose(2)
+        wb_interleave(nc.vector.tensor_copy, 0, 0)
         cast_vector(2)
         product_gpsimd(2)
         m_quant(0, 1, 2)
         head_transpose(3)
         stage1(0, 1, 2)
-        wb_interleave(1, 0)
+        wb_interleave(nc.scalar.copy, 1, 0)
         silu1(0, 1, 2)
         p_ops(0, 0, NB)
         head_product(2)
         head_product(3)
-        wb_interleave(0, 1)
-        cast_scalar(3)
+        wb_interleave(nc.scalar.copy, 0, 1)
+        cast_scalar(3, SCALAR_CAST)
 
         def single_copy(engine, t, g0, g1):
             if g0 == 0:
@@ -370,7 +368,7 @@ def tile_dimenettripletbilinear_kernel(tc, m_kj_bytes, m_kj_scale, m_ji, sbf, w_
             if j == 1:
                 wb_quantise(0, 0)
             if 2 <= j < PAIRS - 2:
-                cast_scalar(j + 2)
+                cast_scalar(j + 2, SCALAR_CAST)
             m_quant(j, 0, 2)
             if j == 2:
                 wb_quantise(0, 1)
@@ -392,7 +390,7 @@ def tile_dimenettripletbilinear_kernel(tc, m_kj_bytes, m_kj_scale, m_ji, sbf, w_
             silu1(j, 0, 2)
             m_copy(j + 1)
             if j == 1:
-                wb_interleave(1, 1)
+                wb_interleave(nc.scalar.copy, 1, 1)
             if j >= 2:
                 stage2(j - 2, 0)
                 silu2((j - 2, 0), 512)
@@ -427,17 +425,16 @@ def tile_dimenettripletbilinear_kernel(tc, m_kj_bytes, m_kj_scale, m_ji, sbf, w_
         single_quant(28, 0, 2)
         single_stage2(28)
         p_ops(30, 0, NB)
-        p_transpose(30, 0, 2)
         k_sum_pair(13, 0)
+        p_transpose(30, 0, 2)
         single_copy(nc.scalar.copy, 30, 0, 2)
-        k_sum_pair(13, 1)
         single_quant(29, 0, 2)
         single_stage2(29)
         finish_scalar(0, 0, 4)
         p_ops(31, 0, NB)
         p_transpose(31, 0, 1)
         p_transpose(31, 1, 2)
-        k_sum(28, 1, [0, 1, 2, 3], False)
+        k_sum_pair(13, 1)
         single_quant(30, 0, 2)
         single_copy(nc.vector.tensor_copy, 31, 0, 1)
         single_copy(nc.vector.tensor_copy, 31, 1, 2)
@@ -452,8 +449,9 @@ def tile_dimenettripletbilinear_kernel(tc, m_kj_bytes, m_kj_scale, m_ji, sbf, w_
                     single_pass(31, (31, b), i, 2 * b + i, g, g == 0 and i == 0, g == 1 and i == 1)
         for b in range(2):
             silu2((31, b), 256)
-        for t in range(29, 31):
-            k_sum(t, 1, [0, 1, 2, 3], False)
+        nc.vector.tensor_tensor(out=tts[29][:], in0=tts[28][:], in1=tts[29][:], op=ADD)
+        k_sum(29, 1, [0, 1, 2, 3], False)
+        k_sum(30, 1, [0, 1, 2, 3], False)
         k_sum((31, 0), 1, [0, 1], False)
         k_sum((31, 1), 1, [2, 3], True)
         finish_vector(1, 0, 2)

@@ -83,7 +83,7 @@ def tile_dimenettripletbilinear_kernel(tc, m_kj_bytes, m_kj_scale, m_ji, sbf, w_
         nc.vector.tensor_scalar(out=ident4[:], in0=ident[:], scalar1=4.0, scalar2=None, op0=MULT)
 
         def bank():
-            bank_t = psum.tile([P, 512], F32, name="bank", bufs=5)
+            bank_t = psum.tile([P, 512], F32, name="bank", bufs=4)
             return bank_t
 
         scale_split = const.tile([P, D], F32, name="scale_split", align_bytes=64)
@@ -257,7 +257,7 @@ def tile_dimenettripletbilinear_kernel(tc, m_kj_bytes, m_kj_scale, m_ji, sbf, w_
             tts[key] = t_t
 
         def agg_open(h, d0, d1):
-            agg_t = psum.tile([P, D], F32, name="agg", bufs=2)
+            agg_t = psum.tile([P, D], F32, name="agg", bufs=3)
             nc.tensor.matmul(out=agg_t[:, d0 * P:d1 * P], lhsT=ident4[:], rhs=mji[:, h, d0 * P:d1 * P], start=True, stop=False)
             for d in range(d0, d1):
                 aggs[h, d] = agg_t
@@ -401,7 +401,8 @@ def tile_dimenettripletbilinear_kernel(tc, m_kj_bytes, m_kj_scale, m_ji, sbf, w_
             p_copy(2 * j - 1)
             if j == 1:
                 agg_open(0, 0, 4)
-                agg_open(1, 0, 4)
+                agg_open(1, 0, 2)
+                agg_open(1, 2, 4)
             if j >= 2:
                 stage2(j - 2, 1)
             p_ops(2 * j, 0, NB)
@@ -452,7 +453,7 @@ def tile_dimenettripletbilinear_kernel(tc, m_kj_bytes, m_kj_scale, m_ji, sbf, w_
         nc.vector.tensor_tensor(out=tts[29][:], in0=tts[28][:], in1=tts[29][:], op=ADD)
         k_sum(29, 1, [0, 1, 2, 3], False)
         k_sum(30, 1, [0, 1, 2, 3], False)
-        k_sum((31, 0), 1, [0, 1], False)
-        k_sum((31, 1), 1, [2, 3], True)
+        k_sum((31, 0), 1, [0, 1], True)
         finish_vector(1, 0, 2)
-        finish_vector(1, 2, 4)
+        k_sum((31, 1), 1, [2, 3], True)
+        finish_scalar(1, 2, 4)

@@ -50,8 +50,8 @@ def tile_dimenettripletbilinear_kernel(tc, m_kj_bytes, m_kj_scale, m_ji, sbf, w_
         nc.scalar.dma_start(out=scale4[:], in_=m_kj_scale.rearrange("a b (p j) -> p (a b j)", j=4))
         wd_raw = const.tile([P, 4, C], BF16, name="wd_raw", align_bytes=64)
         nc.sync.dma_start(out=wd_raw[:], in_=w_down.rearrange("(p j) c -> p j c", j=4))
-        gain8 = const.tile([P, 8], BF16, name="gain8", align_bytes=64)
-        nc.scalar.dma_start(out=gain8[:], in_=gain.rearrange("(p j) -> p j", j=8))
+        gain8 = const.tile([P, 2, 4], BF16, name="gain8", align_bytes=64)
+        nc.scalar.dma_start(out=gain8[:], in_=gain.rearrange("(g p j) -> p g j", g=2, j=4))
         sbf_sb = const.tile([P, 2, K * NB], BF16, name="sbf_sb", align_bytes=64)
         nc.scalar.dma_start(out=sbf_sb[:], in_=sbf.rearrange("(h e) k n -> e h (k n)", e=P))
         wb_hbm = w_bil.rearrange("(g p j) d -> g p j d", g=2, j=4)
@@ -100,10 +100,9 @@ def tile_dimenettripletbilinear_kernel(tc, m_kj_bytes, m_kj_scale, m_ji, sbf, w_
         gain_ps = psum.tile([P, 512], F32, name="gain_ps")
 
         def gain_spread():
-            words = gain8[:].bitcast(F32)
-            place = gain_ps[:].rearrange("q (n u r a) -> q u a n r", n=NB, u=2, a=2)
+            words = gain8[:].rearrange("p g j -> p (g j)").bitcast(F32)
             for j in range(4):
-                nc.tensor.transpose(place[:, j % 2, j // 2], words[:, j:j + 1].to_broadcast([P, P]), ident[:])
+                nc.tensor.transpose(gain_ps[:, j * P:(j + 1) * P], words[:, j:j + 1].to_broadcast([P, P]), ident[:])
 
         wd_grp = const.tile([P, C, 4], BF16, name="wd_grp", align_bytes=64)
         wd_codes = const.tile([P, C], U32, name="wd_codes", align_bytes=64)
@@ -201,7 +200,7 @@ def tile_dimenettripletbilinear_kernel(tc, m_kj_bytes, m_kj_scale, m_ji, sbf, w_
             for a in range(a0, a1):
                 xs[2 * j + a] = x_t[:, a * P:(a + 1) * P].rearrange("p (u w) -> p u w", u=2)
 
-        gain_bf = gain_ps[:].bitcast(BF16)
+        gain_bf = gain_ps[:].bitcast(BF16).rearrange("p (g u n w) -> p g u n w", g=2, u=2, n=4)
         sbf_cols = sbf_sb[:].rearrange("p h k -> p (h k)")
 
         def p_ops(t, n0, n1):
@@ -213,7 +212,7 @@ def tile_dimenettripletbilinear_kernel(tc, m_kj_bytes, m_kj_scale, m_ji, sbf, w_
                 col = t * NB + n
                 nc.vector.scalar_tensor_tensor(
                     out=view[:, n // 4, :, n % 4, :], in0=xs[t], scalar=sbf_cols[:, col:col + 1],
-                    in1=gain_bf[:, n * C:(n + 1) * C].rearrange("p (u w) -> p u w", u=2), op0=MULT, op1=MULT,
+                    in1=gain_bf[:, n // 4, :, n % 4, :], op0=MULT, op1=MULT,
                 )
 
         def p_transpose(t, g0, g1):
@@ -309,7 +308,6 @@ def tile_dimenettripletbilinear_kernel(tc, m_kj_bytes, m_kj_scale, m_ji, sbf, w_
         scale_bank = scale_spread()
         cast_split(1)
         head_transpose(1)
-        gain_spread()
         wd_interleave()
         cast_scalar(1, 2 * D)
         scale_copy_split(scale_bank)
@@ -318,6 +316,7 @@ def tile_dimenettripletbilinear_kernel(tc, m_kj_bytes, m_kj_scale, m_ji, sbf, w_
         wd_quantise()
         m_quant(0, 0, 1)
         stage1(0, 0, 1)
+        gain_spread()
         silu1(0, 0, 1)
         head_product(1)
         head_transpose(2)

@@ -22,7 +22,8 @@ COPY = mybir.ActivationFunctionType.Copy
 TILES = 32
 PAIRS = 16
 HALF = 16
-SCALAR_CAST = 832
+CAST_HEAD = 11264
+CAST_STEP = 512
 LOADS = [(0, 2), (2, 6), (6, 10), (10, 16), (16, 24), (24, 32)]
 
 
@@ -64,13 +65,14 @@ def tile_dimenettripletbilinear_kernel(tc, m_kj_bytes, m_kj_scale, m_ji, sbf, w_
 
         load_bytes(*LOADS[1])
         load_wb(0, 0)
+        load_bytes(*LOADS[2])
         load_wb(1, 0)
         load_wb(0, 1)
         load_wb(1, 1)
-        load_bytes(*LOADS[2])
+        load_bytes(*LOADS[3])
         mji = const.tile([P, 2, D], BF16, name="mji", align_bytes=64)
         nc.sync.dma_start(out=mji[:], in_=m_ji.rearrange("(h e) d -> e h d", e=P))
-        for t0, t1 in LOADS[3:]:
+        for t0, t1 in LOADS[4:]:
             load_bytes(t0, t1)
 
         ident = const.tile([P, P], F32, name="ident", align_bytes=64)
@@ -82,9 +84,13 @@ def tile_dimenettripletbilinear_kernel(tc, m_kj_bytes, m_kj_scale, m_ji, sbf, w_
         ident4 = const.tile([P, P], BF16, name="ident4", align_bytes=64)
         nc.vector.tensor_scalar(out=ident4[:], in0=ident[:], scalar1=4.0, scalar2=None, op0=MULT)
 
+        free = []
+        for i in range(7):
+            bank_t = psum.tile([P, 512], F32, name="bank%d" % i)
+            free.append(bank_t)
+
         def bank():
-            bank_t = psum.tile([P, 512], F32, name="bank", bufs=4)
-            return bank_t
+            return free.pop(0)
 
         scale_split = const.tile([P, D], F32, name="scale_split", align_bytes=64)
 
@@ -96,6 +102,7 @@ def tile_dimenettripletbilinear_kernel(tc, m_kj_bytes, m_kj_scale, m_ji, sbf, w_
 
         def scale_copy_split(b_t):
             nc.scalar.copy(out=scale_split[:].rearrange("q (u p e) -> q u p e", u=2, e=2), in_=b_t[:].rearrange("q (u e p) -> q u p e", u=2, e=2))
+            free.append(b_t)
 
         gain_ps = psum.tile([P, 512], F32, name="gain_ps")
 
@@ -118,7 +125,12 @@ def tile_dimenettripletbilinear_kernel(tc, m_kj_bytes, m_kj_scale, m_ji, sbf, w_
         def wd_quantise():
             nc.vector.quantize_mx(out=wd_codes[:].bitcast(FP8X4), scales=wd_sc[:], in_=wd_grp[:].rearrange("p c j -> p (c j)"))
 
-        wb_grp, wb_codes, wb_sc = {}, {}, {}
+        wb_grp, wb_codes, wb_sc = {}, [], []
+        for g in range(2):
+            codes_t = const.tile([P, D], U32, name="wb_codes%d" % g, align_bytes=64)
+            sc_t = const.tile([P, D], U8, name="wb_sc%d" % g, align_bytes=64)
+            wb_codes.append(codes_t)
+            wb_sc.append(sc_t)
 
         def wb_interleave(engine, g, b):
             grp_t = const.tile([P, 256, 4], BF16, name="wb_grp%d%d" % (g, b), align_bytes=64)
@@ -126,53 +138,49 @@ def tile_dimenettripletbilinear_kernel(tc, m_kj_bytes, m_kj_scale, m_ji, sbf, w_
             wb_grp[g, b] = grp_t
 
         def wb_quantise(g, b):
-            codes_t = const.tile([P, 256], U32, name="wb_codes%d%d" % (g, b), align_bytes=64)
-            sc_t = const.tile([P, 256], U8, name="wb_sc%d%d" % (g, b), align_bytes=64)
-            nc.vector.quantize_mx(out=codes_t[:].bitcast(FP8X4), scales=sc_t[:], in_=wb_grp[g, b][:].rearrange("p d j -> p (d j)"))
-            wb_codes[g, b], wb_sc[g, b] = codes_t, sc_t
+            cols = slice(b * 256, (b + 1) * 256)
+            nc.vector.quantize_mx(out=wb_codes[g][:, cols].bitcast(FP8X4), scales=wb_sc[g][:, cols], in_=wb_grp[g, b][:].rearrange("p d j -> p (d j)"))
 
-        casts, mw, mtr, mq, mcode, yps, xs, pts, ptr, pqs, pcode, mm, tts, aggs = ({} for a in range(14))
-
-        def cast_tile(j):
-            if j not in casts:
-                c_t = work.tile([P, 2 * D], BF16, name="cast", bufs=3, align_bytes=64)
-                casts[j] = c_t
-            return casts[j]
+        mtr, mcode, yps, xs, pts, ptr, pqs, pcode, mm, tts, aggs, head = ({} for a in range(12))
+        casts = []
+        for j in range(PAIRS):
+            cast_t = const.tile([P, 2 * D], BF16, name="cast%d" % j, align_bytes=64)
+            casts.append(cast_t)
+        ring = []
+        for i in range(3):
+            ring_t = const.tile([P, 2 * D], BF16, name="ring%d" % i, align_bytes=64)
+            ring.append(ring_t)
 
         def cast_split(t):
             cols = slice(t % 2 * D, (t % 2 + 1) * D)
             nc.vector.tensor_scalar(
-                out=cast_tile(t // 2)[:, cols].rearrange("p (u w e) -> p w u e", u=2, e=2),
+                out=casts[t // 2][:, cols].rearrange("p (u w e) -> p w u e", u=2, e=2),
                 in0=mbytes[t // 2][:, cols].rearrange("p (w u e) -> p w u e", u=2, e=2), scalar1=one[:], scalar2=None, op0=MULT,
             )
 
-        def cast_scalar(j, width):
-            nc.scalar.copy(out=cast_tile(j)[:, 0:width], in_=mbytes[j][:, 0:width])
-
-        def cast_vector(j):
-            nc.vector.tensor_copy(out=cast_tile(j)[:, SCALAR_CAST:2 * D], in_=mbytes[j][:, SCALAR_CAST:2 * D])
+        def cast_columns(c0, c1):
+            for j in range(c0 // (2 * D), PAIRS):
+                lo, hi = max(c0 - j * 2 * D, 0), min(c1 - j * 2 * D, 2 * D)
+                if lo < hi:
+                    nc.scalar.copy(out=casts[j][:, lo:hi], in_=mbytes[j][:, lo:hi])
 
         def product_gpsimd(j):
-            mw_t = work.tile([P, 2 * D], BF16, name="mw", bufs=2, align_bytes=64)
             nc.gpsimd.tensor_tensor(
-                out=mw_t[:].rearrange("p (u a w e) -> p u a w e", u=2, a=2, e=2),
+                out=ring[(j + 1) % 3][:].rearrange("p (u a w e) -> p u a w e", u=2, a=2, e=2),
                 in0=casts[j][:].rearrange("p (a w u e) -> p u a w e", a=2, u=2, e=2),
                 in1=scale_split[:].rearrange("p (u w e) -> p u w e", u=2, e=2).unsqueeze(2).to_broadcast([P, 2, 2, P, 2]), op=MULT,
             )
-            mw[j] = mw_t
 
         def m_transpose(j):
             b_t = bank()
-            words = mw[j][:].bitcast(F32)
-            for a in range(2):
-                for u in range(2):
-                    nc.tensor.transpose(b_t[:, (2 * a + u) * P:(2 * a + u + 1) * P], words[:, (2 * u + a) * P:(2 * u + a + 1) * P], ident[:])
+            words = ring[(j + 1) % 3][:].bitcast(F32)
+            for i in range(4):
+                nc.tensor.transpose(b_t[:, i * P:(i + 1) * P], words[:, i * P:(i + 1) * P], ident[:])
             mtr[j] = b_t
 
         def m_copy(j):
-            mq_t = work.tile([P, 2 * D], BF16, name="mq", bufs=3, align_bytes=64)
-            nc.scalar.copy(out=mq_t[:].bitcast(F32).rearrange("p (a r u) -> p a r u", a=2, u=2), in_=mtr[j][:].rearrange("p (a u r) -> p a r u", a=2, u=2))
-            mq[j] = mq_t
+            nc.scalar.copy(out=ring[j % 3][:].bitcast(F32).rearrange("p (r u) -> p r u", u=2), in_=mtr[j][:].rearrange("p (u r) -> p r u", u=2))
+            free.append(mtr[j])
 
         def m_quant(j, a0, a1):
             if a0 == 0:
@@ -180,7 +188,7 @@ def tile_dimenettripletbilinear_kernel(tc, m_kj_bytes, m_kj_scale, m_ji, sbf, w_
                 ms_t = work.tile([P, 2 * P], U8, name="ms", bufs=2, align_bytes=64)
                 mcode[j] = (mc_t, ms_t)
             cols = slice(a0 * P, a1 * P)
-            nc.vector.quantize_mx(out=mcode[j][0][:, cols].bitcast(FP8X4), scales=mcode[j][1][:, cols], in_=mq[j][:, a0 * D:a1 * D])
+            nc.vector.quantize_mx(out=mcode[j][0][:, cols].bitcast(FP8X4), scales=mcode[j][1][:, cols], in_=ring[j % 3][:, a0 * D:a1 * D])
 
         def stage1(j, a0, a1):
             y_t = bank()
@@ -197,18 +205,18 @@ def tile_dimenettripletbilinear_kernel(tc, m_kj_bytes, m_kj_scale, m_ji, sbf, w_
             x_t = work.tile([P, 2 * C], F32, name="x", bufs=3, align_bytes=64)
             cols = slice(a0 * P, a1 * P)
             nc.scalar.activation(out=x_t[:, cols], in_=yps[j][:, cols], func=SILU)
+            free.append(yps[j])
             for a in range(a0, a1):
                 xs[2 * j + a] = x_t[:, a * P:(a + 1) * P].rearrange("p (u w) -> p u w", u=2)
 
         gain_bf = gain_ps[:].bitcast(BF16).rearrange("p (g u n w) -> p g u n w", g=2, u=2, n=4)
         sbf_cols = sbf_sb[:].rearrange("p h k -> p (h k)")
 
-        def p_ops(t, n0, n1):
-            if n0 == 0:
-                p_t = work.tile([P, NBC], BF16, name="pt", bufs=3, align_bytes=64)
-                pts[t] = p_t
-            view = pts[t][:].rearrange("p (g u n w) -> p g u n w", g=2, u=2, n=4)
-            for n in range(n0, n1):
+        def p_ops(t):
+            p_t = work.tile([P, NBC], BF16, name="pt", bufs=3, align_bytes=64)
+            pts[t] = p_t
+            view = p_t[:].rearrange("p (g u n w) -> p g u n w", g=2, u=2, n=4)
+            for n in range(NB):
                 col = t * NB + n
                 nc.vector.scalar_tensor_tensor(
                     out=view[:, n // 4, :, n % 4, :], in0=xs[t], scalar=sbf_cols[:, col:col + 1],
@@ -220,70 +228,89 @@ def tile_dimenettripletbilinear_kernel(tc, m_kj_bytes, m_kj_scale, m_ji, sbf, w_
             b_t = bank()
             for a in range(2 * g0, 2 * g1):
                 nc.tensor.transpose(b_t[:, a * P:(a + 1) * P], words[:, a * P:(a + 1) * P], ident[:])
-            ptr[t] = b_t
             ptr[t, g0] = b_t
 
-        def p_copy(t):
-            c, a = t // 2, t % 2
-            if a == 0:
+        groups = [(0,)] + [(2 * c - 1, 2 * c) for c in range(1, PAIRS - 1)] + [(t,) for t in range(TILES - 3, TILES)]
+
+        def p_copy(engine, t, g0, g1):
+            c = [t in grp for grp in groups].index(True)
+            a, width = groups[c].index(t), len(groups[c])
+            if a == 0 and g0 == 0:
                 pq_t = work.tile([P, 2 * NBC], BF16, name="pq", bufs=3, align_bytes=64)
                 pqs[c] = pq_t
-            dst = pqs[c][:].bitcast(F32).rearrange("p (g a r u) -> p g a r u", g=2, a=2, u=2)[:, :, a]
-            nc.scalar.copy(out=dst, in_=ptr[t][:].rearrange("p (g u r) -> p g r u", g=2, u=2))
+            dst = pqs[c][:, 0:width * NBC].bitcast(F32).rearrange("p (g a r u) -> p g a r u", g=2, a=width, u=2)[:, g0:g1, a]
+            engine(out=dst, in_=ptr[t, g0][:].rearrange("p (g u r) -> p g r u", g=2, u=2)[:, g0:g1])
+            free.append(ptr[t, g0])
 
-        def p_quant(c):
-            pc_t = work.tile([P, 4 * P], U32, name="pc", bufs=3, align_bytes=64)
-            ps_t = work.tile([P, 4 * P], U8, name="ps", bufs=3, align_bytes=64)
-            nc.vector.quantize_mx(out=pc_t[:].bitcast(FP8X4), scales=ps_t[:], in_=pqs[c][:])
-            pcode[c] = (pc_t, ps_t)
+        def p_quant(c, g0, g1):
+            if g0 == 0:
+                pc_t = work.tile([P, 4 * P], U32, name="pc", bufs=3, align_bytes=64)
+                ps_t = work.tile([P, 4 * P], U8, name="ps", bufs=3, align_bytes=64)
+                pcode[c] = (pc_t, ps_t)
+            n = len(groups[c]) * P
+            cols = slice(g0 * n, g1 * n)
+            nc.vector.quantize_mx(out=pcode[c][0][:, cols].bitcast(FP8X4), scales=pcode[c][1][:, cols], in_=pqs[c][:, 4 * g0 * n:4 * g1 * n])
 
-        def stage2(c, b):
+        def stage2(c, d0, d1):
             mm_t = bank()
             pc_t, ps_t = pcode[c]
-            for i in range(2):
-                cols = slice(i * P, (i + 1) * P)
+            n = len(groups[c]) * P
+            for d in range(d0, d1):
+                cols = slice(d * P, (d + 1) * P)
                 for g in range(2):
-                    toks = slice(g * 256, (g + 1) * 256)
+                    toks = slice(g * n, (g + 1) * n)
                     nc.tensor.matmul_mx(
-                        out=mm_t[:, i * 256:(i + 1) * 256], lhsT=wb_codes[g, b][:, cols].bitcast(FP8X4), lhsT_scale=wb_sc[g, b][:, cols],
+                        out=mm_t[:, (d - d0) * n:(d - d0 + 1) * n], lhsT=wb_codes[g][:, cols].bitcast(FP8X4), lhsT_scale=wb_sc[g][:, cols],
                         rhs=pc_t[:, toks].bitcast(FP8X4), rhs_scale=ps_t[:, toks], start=(g == 0), stop=(g == 1),
                     )
-            mm[c, b] = mm_t
+            mm[c, d0] = mm_t
 
-        def silu2(key, width):
+        def stage2_turned(c, d0, d1, g):
+            if g == 0:
+                mm[c, d0] = bank()
+            toks, cols = slice(g * P, (g + 1) * P), slice(d0 * P, d1 * P)
+            nc.tensor.matmul_mx(
+                out=mm[c, d0][:, 0:(d1 - d0) * P], lhsT=pcode[c][0][:, toks].bitcast(FP8X4), lhsT_scale=pcode[c][1][:, toks],
+                rhs=wb_codes[g][:, cols].bitcast(FP8X4), rhs_scale=wb_sc[g][:, cols], start=(g == 0), stop=(g == 1),
+            )
+
+        def silu2(c, d0, width):
             t_t = work.tile([P, 4 * P], F32, name="tt", bufs=8, align_bytes=64)
-            nc.scalar.activation(out=t_t[:, 0:width], in_=mm[key][:, 0:width], func=SILU)
-            tts[key] = t_t
+            nc.scalar.activation(out=t_t[:, 0:width], in_=mm[c, d0][:, 0:width], func=SILU)
+            free.append(mm[c, d0])
+            tts[c, d0] = t_t
 
-        def agg_open(h, d0, d1):
-            agg_t = psum.tile([P, D], F32, name="agg", bufs=3)
-            nc.tensor.matmul(out=agg_t[:, d0 * P:d1 * P], lhsT=ident4[:], rhs=mji[:, h, d0 * P:d1 * P], start=True, stop=False)
+        def agg_open(h):
+            agg_t = bank()
+            nc.tensor.matmul(out=agg_t[:], lhsT=ident4[:], rhs=mji[:, h, :], start=True, stop=False)
+            aggs[h] = agg_t
+
+        last_summed = (HALF - 1, TILES - 4)
+
+        def k_sum(c, d0, d1):
+            width = len(groups[c])
             for d in range(d0, d1):
-                aggs[h, d] = agg_t
+                for a, t in enumerate(groups[c]):
+                    i = (d - d0) * width + a
+                    nc.tensor.matmul(
+                        out=aggs[t // HALF][:, d * P:(d + 1) * P], lhsT=tts[c, d0][:, i * P:(i + 1) * P], rhs=ident[:],
+                        is_transpose=True, start=False, stop=(t in last_summed and d == 3),
+                    )
 
-        def k_sum(key, h, dims, last):
-            for i, d in enumerate(dims):
-                nc.tensor.matmul(
-                    out=aggs[h, d][:, d * P:(d + 1) * P], lhsT=tts[key][:, i * P:(i + 1) * P], rhs=ident[:],
-                    is_transpose=True, start=False, stop=(last and i == len(dims) - 1),
-                )
+        sums = []
+        for h in range(2):
+            sum_t = const.tile([P, D], F32, name="sum%d" % h, align_bytes=64)
+            sums.append(sum_t)
 
-        def k_sum_pair(c, b):
-            k_sum((c, b), c // 8, [2 * b, 2 * b, 2 * b + 1, 2 * b + 1], c == 7 and b == 1)
-
-        def finish_scalar(h, d0, d1):
+        def agg_close(h, d0, d1):
             cols = slice(d0 * P, d1 * P)
-            o_t = const.tile([P, D], F32, name="o%d%d" % (h, d0), align_bytes=64)
-            nc.scalar.activation(out=o_t[:, cols], in_=aggs[h, d0][:, cols], func=COPY, scale=0.25)
-            nc.sync.dma_start(out=out[h * P:(h + 1) * P, cols], in_=o_t[:, cols])
+            nc.scalar.activation(out=sums[h][:, cols], in_=aggs[h][:, cols], func=COPY, scale=0.25)
+            if d1 == 4:
+                free.append(aggs[h])
 
-        def finish_vector(h, d0, d1):
+        def add_turned(dst, c, first, d0, d1, src):
             cols = slice(d0 * P, d1 * P)
-            o_t = const.tile([P, D], F32, name="o%d%d" % (h, d0), align_bytes=64)
-            nc.vector.tensor_scalar(out=o_t[:, cols], in0=aggs[h, d0][:, cols], scalar1=0.25, scalar2=None, op0=MULT)
-            nc.sync.dma_start(out=out[h * P:(h + 1) * P, cols], in_=o_t[:, cols])
-
-        head = {}
+            nc.vector.scalar_tensor_tensor(out=dst[:, cols], in0=tts[c, first][:, (d0 - first) * P:(d1 - first) * P], scalar=0.25, in1=src[:, cols], op0=MULT, op1=ADD)
 
         def head_transpose(t):
             b_t = bank()
@@ -294,14 +321,12 @@ def tile_dimenettripletbilinear_kernel(tc, m_kj_bytes, m_kj_scale, m_ji, sbf, w_
             head[t] = b_t
 
         def head_product(t):
-            if t % 2 == 0:
-                mq_t = work.tile([P, 2 * D], BF16, name="mq", bufs=3, align_bytes=64)
-                mq[t // 2] = mq_t
             nc.vector.tensor_tensor(
-                out=mq[t // 2][:, t % 2 * D:(t % 2 + 1) * D].rearrange("p (r u e) -> p r u e", u=2, e=2),
+                out=ring[t // 2][:, t % 2 * D:(t % 2 + 1) * D].rearrange("p (r u e) -> p r u e", u=2, e=2),
                 in0=head[t][:, 0:256].bitcast(BF16).rearrange("p (u r e) -> p r u e", u=2, e=2),
                 in1=scale4[:].rearrange("p (u e) -> p u e", u=2).unsqueeze(1).to_broadcast([P, P, 2, 2]), op=MULT,
             )
+            free.append(head[t])
 
         cast_split(0)
         head_transpose(0)
@@ -309,9 +334,9 @@ def tile_dimenettripletbilinear_kernel(tc, m_kj_bytes, m_kj_scale, m_ji, sbf, w_
         cast_split(1)
         head_transpose(1)
         wd_interleave()
-        cast_scalar(1, 2 * D)
+        cast_columns(1024, 2048)
         scale_copy_split(scale_bank)
-        cast_scalar(2, SCALAR_CAST)
+        cast_columns(2048, 3072)
         head_product(0)
         wd_quantise()
         m_quant(0, 0, 1)
@@ -321,138 +346,149 @@ def tile_dimenettripletbilinear_kernel(tc, m_kj_bytes, m_kj_scale, m_ji, sbf, w_
         head_product(1)
         head_transpose(2)
         wb_interleave(nc.vector.tensor_copy, 0, 0)
-        cast_vector(2)
-        product_gpsimd(2)
         m_quant(0, 1, 2)
+        product_gpsimd(2)
         head_transpose(3)
         stage1(0, 1, 2)
+        cast_columns(3072, 4096)
         wb_interleave(nc.scalar.copy, 1, 0)
         silu1(0, 1, 2)
-        p_ops(0, 0, NB)
+        p_ops(0)
         head_product(2)
         head_product(3)
+        cast_columns(4096, 5120)
+        p_transpose(0, 0, 2)
+        p_copy(nc.scalar.copy, 0, 0, 2)
         wb_interleave(nc.scalar.copy, 0, 1)
-        cast_scalar(3, SCALAR_CAST)
+        agg_open(0)
 
-        def single_copy(engine, t, g0, g1):
-            if g0 == 0:
-                pq_t = work.tile([P, 2 * NBC], BF16, name="pq", bufs=3, align_bytes=64)
-                pqs[t] = pq_t
-            dst = pqs[t][:, 0:NBC].bitcast(F32).rearrange("p (g r u) -> p g r u", g=2, u=2)[:, g0:g1]
-            engine(out=dst, in_=ptr[t, g0][:].rearrange("p (g u r) -> p g r u", g=2, u=2)[:, g0:g1])
-
-        def single_quant(t, g0, g1):
-            if g0 == 0:
-                pc_t = work.tile([P, 4 * P], U32, name="pc", bufs=3, align_bytes=64)
-                ps_t = work.tile([P, 4 * P], U8, name="ps", bufs=3, align_bytes=64)
-                pcode[t] = (pc_t, ps_t)
-            cols = slice(g0 * P, g1 * P)
-            nc.vector.quantize_mx(out=pcode[t][0][:, cols].bitcast(FP8X4), scales=pcode[t][1][:, cols], in_=pqs[t][:, g0 * D:g1 * D])
-
-        def single_pass(t, key, slot, d, g, start, stop):
-            b, cols, toks = d // 2, slice(d % 2 * P, (d % 2 + 1) * P), slice(g * P, (g + 1) * P)
-            nc.tensor.matmul_mx(
-                out=mm[key][:, slot * P:(slot + 1) * P], lhsT=wb_codes[g, b][:, cols].bitcast(FP8X4), lhsT_scale=wb_sc[g, b][:, cols],
-                rhs=pcode[t][0][:, toks].bitcast(FP8X4), rhs_scale=pcode[t][1][:, toks], start=start, stop=stop,
-            )
-
-        def single_stage2(t):
-            mm[t] = bank()
-            for d in range(4):
-                for g in range(2):
-                    single_pass(t, t, d, d, g, g == 0, g == 1)
-            silu2(t, 512)
-
-        for j in range(1, PAIRS - 1):
+        for j in range(1, PAIRS - 2):
             if j == 1:
                 wb_quantise(0, 0)
-            if 2 <= j < PAIRS - 2:
-                cast_scalar(j + 2, SCALAR_CAST)
-            m_quant(j, 0, 2)
+                wb_interleave(nc.vector.tensor_copy, 1, 1)
             if j == 2:
                 wb_quantise(0, 1)
                 wb_quantise(1, 1)
-            if j + 2 < PAIRS:
-                cast_vector(j + 2)
-                product_gpsimd(j + 2)
+            m_quant(j, 0, 2)
+            product_gpsimd(j + 2)
             if j == 1:
                 wb_quantise(1, 0)
             if j >= 2:
-                p_quant(j - 2)
+                p_quant(j - 2, 0, 2)
+                p_copy(nc.scalar.copy, 2 * j - 3, 0, 2)
             if j >= 3:
-                k_sum_pair(j - 3, 0)
-                silu2((j - 3, 1), 512)
-            p_transpose(2 * j - 2, 0, 2)
-            p_copy(2 * j - 2)
+                cast_columns(CAST_HEAD + (j - 3) * CAST_STEP, CAST_HEAD + (j - 2) * CAST_STEP)
+            if j == 1:
+                cast_columns(5120, 6144)
+            if j == 2:
+                cast_columns(8192, 10240)
             m_transpose(j + 1)
+            if j >= 2:
+                p_transpose(2 * j - 2, 0, 2)
             stage1(j, 0, 2)
             silu1(j, 0, 2)
+            if j >= 2:
+                p_copy(nc.scalar.copy, 2 * j - 2, 0, 2)
             m_copy(j + 1)
             if j == 1:
-                wb_interleave(nc.scalar.copy, 1, 1)
-            if j >= 2:
-                stage2(j - 2, 0)
-                silu2((j - 2, 0), 512)
-            p_ops(2 * j - 1, 0, NB)
+                cast_columns(6144, 8192)
+            if j == 2:
+                stage2(0, 0, 4)
+                silu2(0, 0, 512)
+                cast_columns(10240, CAST_HEAD)
             if j >= 3:
-                k_sum_pair(j - 3, 1)
+                stage2(j - 2, 0, 2)
+                stage2(j - 2, 2, 4)
+                silu2(j - 2, 0, 512)
+                silu2(j - 2, 2, 512)
+            if j == 9:
+                agg_open(1)
+            p_ops(2 * j - 1)
+            if j == 3:
+                k_sum(0, 0, 4)
+            if j >= 4:
+                k_sum(j - 3, 0, 2)
+                k_sum(j - 3, 2, 4)
             p_transpose(2 * j - 1, 0, 2)
-            p_copy(2 * j - 1)
-            if j == 1:
-                agg_open(0, 0, 4)
-                agg_open(1, 0, 2)
-                agg_open(1, 2, 4)
-            if j >= 2:
-                stage2(j - 2, 1)
-            p_ops(2 * j, 0, NB)
+            p_ops(2 * j)
 
+        m_quant(14, 0, 2)
+        p_quant(12, 0, 2)
+        m_transpose(15)
+        p_transpose(26, 0, 2)
+        p_copy(nc.scalar.copy, 25, 0, 2)
+        stage1(14, 0, 2)
+        p_copy(nc.scalar.copy, 26, 0, 2)
+        silu1(14, 0, 2)
+        m_copy(15)
+        stage2(12, 0, 2)
+        stage2(12, 2, 4)
+        silu2(12, 0, 512)
+        p_ops(27)
+        p_quant(13, 0, 2)
         m_quant(15, 0, 2)
-        p_quant(13)
-        k_sum_pair(12, 0)
-        silu2((12, 1), 512)
-        p_transpose(28, 0, 2)
-        single_copy(nc.scalar.copy, 28, 0, 2)
+        k_sum(11, 0, 2)
+        p_transpose(27, 0, 2)
+        silu2(12, 2, 512)
+        p_copy(nc.scalar.copy, 27, 0, 2)
+        p_ops(28)
+        stage2(13, 0, 2)
         stage1(15, 0, 2)
+        stage2(13, 2, 4)
+        silu2(13, 0, 512)
         silu1(15, 0, 2)
-        stage2(13, 0)
-        stage2(13, 1)
-        silu2((13, 0), 512)
-        p_ops(29, 0, NB)
+        p_transpose(28, 0, 1)
+        p_transpose(28, 1, 2)
+        p_copy(nc.scalar.copy, 28, 0, 1)
+        p_copy(nc.scalar.copy, 28, 1, 2)
+        silu2(13, 2, 512)
+        k_sum(11, 2, 4)
+        k_sum(12, 0, 2)
+        k_sum(12, 2, 4)
+        p_ops(29)
+        p_quant(14, 0, 2)
         p_transpose(29, 0, 2)
-        k_sum_pair(12, 1)
-        single_copy(nc.scalar.copy, 29, 0, 2)
-        silu2((13, 1), 512)
-        single_quant(28, 0, 2)
-        single_stage2(28)
-        p_ops(30, 0, NB)
-        k_sum_pair(13, 0)
+        k_sum(13, 0, 2)
+        k_sum(13, 2, 4)
+        p_copy(nc.scalar.copy, 29, 0, 2)
+        stage2(14, 0, 2)
+        stage2(14, 2, 4)
+        silu2(14, 0, 512)
+        p_ops(30)
+        p_quant(15, 0, 2)
         p_transpose(30, 0, 2)
-        single_copy(nc.scalar.copy, 30, 0, 2)
-        single_quant(29, 0, 2)
-        single_stage2(29)
-        finish_scalar(0, 0, 4)
-        p_ops(31, 0, NB)
-        p_transpose(31, 0, 1)
-        p_transpose(31, 1, 2)
-        k_sum_pair(13, 1)
-        single_quant(30, 0, 2)
-        single_copy(nc.vector.tensor_copy, 31, 0, 1)
-        single_copy(nc.vector.tensor_copy, 31, 1, 2)
-        single_quant(31, 0, 1)
-        single_quant(31, 1, 2)
-        single_stage2(30)
-        for b in range(2):
-            mm[31, b] = bank()
+        silu2(14, 2, 512)
+        p_copy(nc.scalar.copy, 30, 0, 2)
         for g in range(2):
-            for b in range(2):
-                for i in range(2):
-                    single_pass(31, (31, b), i, 2 * b + i, g, g == 0 and i == 0, g == 1 and i == 1)
-        for b in range(2):
-            silu2((31, b), 256)
-        nc.vector.tensor_tensor(out=tts[29][:], in0=tts[28][:], in1=tts[29][:], op=ADD)
-        k_sum(29, 1, [0, 1, 2, 3], False)
-        k_sum(30, 1, [0, 1, 2, 3], False)
-        k_sum((31, 0), 1, [0, 1], True)
-        finish_vector(1, 0, 2)
-        k_sum((31, 1), 1, [2, 3], True)
-        finish_scalar(1, 2, 4)
+            stage2_turned(15, 0, 4, g)
+        p_ops(31)
+        p_quant(16, 0, 2)
+        p_transpose(31, 0, 1)
+        k_sum(14, 0, 2)
+        p_transpose(31, 1, 2)
+        k_sum(14, 2, 4)
+        silu2(15, 0, 512)
+        p_copy(nc.vector.tensor_copy, 31, 0, 1)
+        p_copy(nc.vector.tensor_copy, 31, 1, 2)
+        for g in range(2):
+            stage2_turned(16, 0, 4, g)
+        p_quant(17, 0, 1)
+        p_quant(17, 1, 2)
+        agg_close(0, 0, 4)
+        nc.sync.dma_start(out=out[0:P, :], in_=sums[0][:])
+        agg_close(1, 0, 4)
+        silu2(16, 0, 512)
+        for g in range(2):
+            for d0 in (0, 2):
+                stage2_turned(17, d0, d0 + 2, g)
+        with29 = const.tile([P, D], F32, name="with29", align_bytes=64)
+        with30 = const.tile([P, D], F32, name="with30", align_bytes=64)
+        for d0 in (0, 2):
+            add_turned(with29, 15, 0, d0, d0 + 2, sums[1])
+        for d0 in (0, 2):
+            add_turned(with30, 16, 0, d0, d0 + 2, with29)
+        for d0 in (0, 2):
+            silu2(17, d0, 256)
+            o_t = const.tile([P, D], F32, name="o%d" % d0, align_bytes=64)
+            add_turned(o_t, 17, d0, d0, d0 + 2, with30)
+            nc.sync.dma_start(out=out[P:2 * P, d0 * P:(d0 + 2) * P], in_=o_t[:, d0 * P:(d0 + 2) * P])

@@ -22,9 +22,6 @@ COPY = mybir.ActivationFunctionType.Copy
 TILES = 32
 PAIRS = 16
 HALF = 16
-CAST_HEAD = 11264
-CAST_STEP = 512
-LOADS = [(0, 2), (2, 6), (6, 10), (10, 16), (16, 24), (24, 32)]
 
 
 def tile_dimenettripletbilinear_kernel(tc, m_kj_bytes, m_kj_scale, m_ji, sbf, w_down, gain, w_bil, out):
@@ -46,11 +43,9 @@ def tile_dimenettripletbilinear_kernel(tc, m_kj_bytes, m_kj_scale, m_ji, sbf, w_
             for t in range(t0, t1, 2):
                 mbytes[t // 2] = t_t[:, (t - t0) * D:(t - t0 + 2) * D].bitcast(FP8)
 
-        load_bytes(*LOADS[0])
+        load_bytes(0, 2)
         scale4 = const.tile([P, 4], F32, name="scale4", align_bytes=64)
         nc.scalar.dma_start(out=scale4[:], in_=m_kj_scale.rearrange("a b (p j) -> p (a b j)", j=4))
-        wd_raw = const.tile([P, 4, C], BF16, name="wd_raw", align_bytes=64)
-        nc.sync.dma_start(out=wd_raw[:], in_=w_down.rearrange("(p j) c -> p j c", j=4))
         gain8 = const.tile([P, 2, 4], BF16, name="gain8", align_bytes=64)
         nc.scalar.dma_start(out=gain8[:], in_=gain.rearrange("(g p j) -> p g j", g=2, j=4))
         sbf_sb = const.tile([P, 2, K * NB], BF16, name="sbf_sb", align_bytes=64)
@@ -63,17 +58,20 @@ def tile_dimenettripletbilinear_kernel(tc, m_kj_bytes, m_kj_scale, m_ji, sbf, w_
             nc.sync.dma_start(out=wb_t[:], in_=wb_hbm[g][:, :, b * 256:(b + 1) * 256])
             wb_raw[g, b] = wb_t
 
-        load_bytes(*LOADS[1])
+        load_bytes(2, 4)
+        wd_raw = const.tile([P, 4, C], BF16, name="wd_raw", align_bytes=64)
+        nc.sync.dma_start(out=wd_raw[:], in_=w_down.rearrange("(p j) c -> p j c", j=4))
+        load_bytes(4, 8)
         load_wb(0, 0)
-        load_bytes(*LOADS[2])
+        load_bytes(8, 12)
         load_wb(1, 0)
         load_wb(0, 1)
         load_wb(1, 1)
-        load_bytes(*LOADS[3])
+        load_bytes(12, 16)
         mji = const.tile([P, 2, D], BF16, name="mji", align_bytes=64)
         nc.sync.dma_start(out=mji[:], in_=m_ji.rearrange("(h e) d -> e h d", e=P))
-        for t0, t1 in LOADS[4:]:
-            load_bytes(t0, t1)
+        load_bytes(16, 24)
+        load_bytes(24, 32)
 
         ident = const.tile([P, P], F32, name="ident", align_bytes=64)
         make_identity(nc, ident[:])
@@ -132,10 +130,11 @@ def tile_dimenettripletbilinear_kernel(tc, m_kj_bytes, m_kj_scale, m_ji, sbf, w_
             wb_codes.append(codes_t)
             wb_sc.append(sc_t)
 
-        def wb_interleave(engine, g, b):
-            grp_t = const.tile([P, 256, 4], BF16, name="wb_grp%d%d" % (g, b), align_bytes=64)
-            engine(out=grp_t[:], in_=wb_raw[g, b][:].rearrange("p j d -> p d j"))
-            wb_grp[g, b] = grp_t
+        def wb_interleave(engine, g, b, d0, d1):
+            if d0 == 0:
+                grp_t = const.tile([P, 256, 4], BF16, name="wb_grp%d%d" % (g, b), align_bytes=64)
+                wb_grp[g, b] = grp_t
+            engine(out=wb_grp[g, b][:, d0:d1], in_=wb_raw[g, b][:].rearrange("p j d -> p d j")[:, d0:d1])
 
         def wb_quantise(g, b):
             cols = slice(b * 256, (b + 1) * 256)
@@ -158,11 +157,9 @@ def tile_dimenettripletbilinear_kernel(tc, m_kj_bytes, m_kj_scale, m_ji, sbf, w_
                 in0=mbytes[t // 2][:, cols].rearrange("p (w u e) -> p w u e", u=2, e=2), scalar1=one[:], scalar2=None, op0=MULT,
             )
 
-        def cast_columns(c0, c1):
-            for j in range(c0 // (2 * D), PAIRS):
-                lo, hi = max(c0 - j * 2 * D, 0), min(c1 - j * 2 * D, 2 * D)
-                if lo < hi:
-                    nc.scalar.copy(out=casts[j][:, lo:hi], in_=mbytes[j][:, lo:hi])
+        def cast(t0, t1):
+            cols = slice(t0 % 2 * D, (t0 % 2 + t1 - t0) * D)
+            nc.scalar.copy(out=casts[t0 // 2][:, cols], in_=mbytes[t0 // 2][:, cols])
 
         def product_gpsimd(j):
             nc.gpsimd.tensor_tensor(
@@ -328,85 +325,107 @@ def tile_dimenettripletbilinear_kernel(tc, m_kj_bytes, m_kj_scale, m_ji, sbf, w_
             )
             free.append(head[t])
 
+        with29 = const.tile([P, D], F32, name="with29", align_bytes=64)
+        with30 = const.tile([P, D], F32, name="with30", align_bytes=64)
+        o_last = []
+        for i in range(2):
+            o_t = const.tile([P, D], F32, name="o%d" % i, align_bytes=64)
+            o_last.append(o_t)
+
+        scale_bank = scale_spread()
+        scale_copy_split(scale_bank)
+        gain_spread()
         cast_split(0)
         head_transpose(0)
-        scale_bank = scale_spread()
         cast_split(1)
         head_transpose(1)
         wd_interleave()
-        cast_columns(1024, 2048)
-        scale_copy_split(scale_bank)
-        cast_columns(2048, 3072)
+        cast(2, 4)
+        cast(4, 6)
+        cast(6, 8)
         head_product(0)
         wd_quantise()
         m_quant(0, 0, 1)
         stage1(0, 0, 1)
-        gain_spread()
         silu1(0, 0, 1)
         head_product(1)
         head_transpose(2)
-        wb_interleave(nc.vector.tensor_copy, 0, 0)
+        wb_interleave(nc.vector.tensor_copy, 0, 0, 0, 128)
         m_quant(0, 1, 2)
         product_gpsimd(2)
+        wb_interleave(nc.vector.tensor_copy, 0, 0, 128, 256)
         head_transpose(3)
         stage1(0, 1, 2)
-        cast_columns(3072, 4096)
-        wb_interleave(nc.scalar.copy, 1, 0)
+        cast(8, 10)
+        wb_interleave(nc.scalar.copy, 1, 0, 0, 256)
         silu1(0, 1, 2)
         p_ops(0)
         head_product(2)
         head_product(3)
-        cast_columns(4096, 5120)
         p_transpose(0, 0, 2)
+        wb_interleave(nc.scalar.copy, 0, 1, 0, 256)
         p_copy(nc.scalar.copy, 0, 0, 2)
-        wb_interleave(nc.scalar.copy, 0, 1)
+        wb_quantise(0, 0)
+        m_quant(1, 0, 2)
+        product_gpsimd(3)
+        wb_quantise(1, 0)
+        cast(10, 12)
+        m_transpose(2)
+        stage1(1, 0, 2)
+        silu1(1, 0, 2)
+        m_copy(2)
+        wb_interleave(nc.scalar.copy, 1, 1, 0, 256)
+        p_ops(1)
+        p_transpose(1, 0, 2)
+        p_ops(2)
+        wb_quantise(0, 1)
+        m_quant(2, 0, 2)
+        product_gpsimd(4)
+        wb_quantise(1, 1)
+        p_quant(0, 0, 2)
+        p_copy(nc.scalar.copy, 1, 0, 2)
+        cast(12, 14)
+        cast(14, 16)
+        m_transpose(3)
+        stage1(2, 0, 2)
+        p_transpose(2, 0, 2)
+        silu1(2, 0, 2)
+        p_copy(nc.scalar.copy, 2, 0, 2)
+        m_copy(3)
+        stage2(0, 0, 4)
         agg_open(0)
+        silu2(0, 0, 512)
+        cast(16, 18)
+        p_ops(3)
+        p_transpose(3, 0, 2)
+        p_ops(4)
 
-        for j in range(1, PAIRS - 2):
-            if j == 1:
-                wb_quantise(0, 0)
-                wb_interleave(nc.vector.tensor_copy, 1, 1)
-            if j == 2:
-                wb_quantise(0, 1)
-                wb_quantise(1, 1)
+        to_cast = 18
+        for j in range(3, PAIRS - 2):
             m_quant(j, 0, 2)
             product_gpsimd(j + 2)
-            if j == 1:
-                wb_quantise(1, 0)
-            if j >= 2:
-                p_quant(j - 2, 0, 2)
-                p_copy(nc.scalar.copy, 2 * j - 3, 0, 2)
-            if j >= 3:
-                cast_columns(CAST_HEAD + (j - 3) * CAST_STEP, CAST_HEAD + (j - 2) * CAST_STEP)
-            if j == 1:
-                cast_columns(5120, 6144)
-            if j == 2:
-                cast_columns(8192, 10240)
+            p_quant(j - 2, 0, 2)
+            p_copy(nc.scalar.copy, 2 * j - 3, 0, 2)
             m_transpose(j + 1)
-            if j >= 2:
-                p_transpose(2 * j - 2, 0, 2)
+            p_transpose(2 * j - 2, 0, 2)
             stage1(j, 0, 2)
             silu1(j, 0, 2)
-            if j >= 2:
-                p_copy(nc.scalar.copy, 2 * j - 2, 0, 2)
+            p_copy(nc.scalar.copy, 2 * j - 2, 0, 2)
             m_copy(j + 1)
-            if j == 1:
-                cast_columns(6144, 8192)
-            if j == 2:
-                stage2(0, 0, 4)
-                silu2(0, 0, 512)
-                cast_columns(10240, CAST_HEAD)
-            if j >= 3:
-                stage2(j - 2, 0, 2)
-                stage2(j - 2, 2, 4)
-                silu2(j - 2, 0, 512)
-                silu2(j - 2, 2, 512)
+            if to_cast < TILES:
+                count = 2 if j % 3 == 0 else 1
+                cast(to_cast, to_cast + count)
+                to_cast = to_cast + count
+            stage2(j - 2, 0, 2)
+            stage2(j - 2, 2, 4)
+            silu2(j - 2, 0, 512)
+            silu2(j - 2, 2, 512)
             if j == 9:
                 agg_open(1)
             p_ops(2 * j - 1)
             if j == 3:
                 k_sum(0, 0, 4)
-            if j >= 4:
+            else:
                 k_sum(j - 3, 0, 2)
                 k_sum(j - 3, 2, 4)
             p_transpose(2 * j - 1, 0, 2)
@@ -436,11 +455,11 @@ def tile_dimenettripletbilinear_kernel(tc, m_kj_bytes, m_kj_scale, m_ji, sbf, w_
         stage1(15, 0, 2)
         stage2(13, 2, 4)
         silu2(13, 0, 512)
-        silu1(15, 0, 2)
         p_transpose(28, 0, 1)
         p_transpose(28, 1, 2)
         p_copy(nc.scalar.copy, 28, 0, 1)
         p_copy(nc.scalar.copy, 28, 1, 2)
+        silu1(15, 0, 2)
         silu2(13, 2, 512)
         k_sum(11, 2, 4)
         k_sum(12, 0, 2)
@@ -449,18 +468,20 @@ def tile_dimenettripletbilinear_kernel(tc, m_kj_bytes, m_kj_scale, m_ji, sbf, w_
         p_quant(14, 0, 2)
         p_transpose(29, 0, 2)
         k_sum(13, 0, 2)
-        k_sum(13, 2, 4)
         p_copy(nc.scalar.copy, 29, 0, 2)
         stage2(14, 0, 2)
         stage2(14, 2, 4)
+        agg_close(0, 0, 4)
+        nc.sync.dma_start(out=out[0:P, :], in_=sums[0][:])
         silu2(14, 0, 512)
         p_ops(30)
         p_quant(15, 0, 2)
+        k_sum(13, 2, 4)
         p_transpose(30, 0, 2)
         silu2(14, 2, 512)
         p_copy(nc.scalar.copy, 30, 0, 2)
-        for g in range(2):
-            stage2_turned(15, 0, 4, g)
+        stage2_turned(15, 0, 4, 0)
+        stage2_turned(15, 0, 4, 1)
         p_ops(31)
         p_quant(16, 0, 2)
         p_transpose(31, 0, 1)
@@ -470,25 +491,23 @@ def tile_dimenettripletbilinear_kernel(tc, m_kj_bytes, m_kj_scale, m_ji, sbf, w_
         silu2(15, 0, 512)
         p_copy(nc.vector.tensor_copy, 31, 0, 1)
         p_copy(nc.vector.tensor_copy, 31, 1, 2)
-        for g in range(2):
-            stage2_turned(16, 0, 4, g)
+        stage2_turned(16, 0, 4, 0)
+        stage2_turned(16, 0, 4, 1)
         p_quant(17, 0, 1)
         p_quant(17, 1, 2)
-        agg_close(0, 0, 4)
-        nc.sync.dma_start(out=out[0:P, :], in_=sums[0][:])
         agg_close(1, 0, 4)
         silu2(16, 0, 512)
-        for g in range(2):
-            for d0 in (0, 2):
-                stage2_turned(17, d0, d0 + 2, g)
-        with29 = const.tile([P, D], F32, name="with29", align_bytes=64)
-        with30 = const.tile([P, D], F32, name="with30", align_bytes=64)
-        for d0 in (0, 2):
-            add_turned(with29, 15, 0, d0, d0 + 2, sums[1])
-        for d0 in (0, 2):
-            add_turned(with30, 16, 0, d0, d0 + 2, with29)
-        for d0 in (0, 2):
-            silu2(17, d0, 256)
-            o_t = const.tile([P, D], F32, name="o%d" % d0, align_bytes=64)
-            add_turned(o_t, 17, d0, d0, d0 + 2, with30)
-            nc.sync.dma_start(out=out[P:2 * P, d0 * P:(d0 + 2) * P], in_=o_t[:, d0 * P:(d0 + 2) * P])
+        stage2_turned(17, 0, 2, 0)
+        stage2_turned(17, 2, 4, 0)
+        stage2_turned(17, 0, 2, 1)
+        stage2_turned(17, 2, 4, 1)
+        add_turned(with29, 15, 0, 0, 2, sums[1])
+        add_turned(with29, 15, 0, 2, 4, sums[1])
+        add_turned(with30, 16, 0, 0, 2, with29)
+        add_turned(with30, 16, 0, 2, 4, with29)
+        silu2(17, 0, 256)
+        add_turned(o_last[0], 17, 0, 0, 2, with30)
+        nc.sync.dma_start(out=out[P:2 * P, 0 * P:2 * P], in_=o_last[0][:, 0 * P:2 * P])
+        silu2(17, 2, 256)
+        add_turned(o_last[1], 17, 2, 2, 4, with30)
+        nc.sync.dma_start(out=out[P:2 * P, 2 * P:4 * P], in_=o_last[1][:, 2 * P:4 * P])

@@ -43,9 +43,9 @@ def tile_dimenettripletbilinear_kernel(tc, m_kj_bytes, m_kj_scale, m_ji, sbf, w_
             for t in range(t0, t1, 2):
                 mbytes[t // 2] = t_t[:, (t - t0) * D:(t - t0 + 2) * D].bitcast(FP8)
 
-        load_bytes(0, 2)
         scale4 = const.tile([P, 4], F32, name="scale4", align_bytes=64)
-        nc.scalar.dma_start(out=scale4[:], in_=m_kj_scale.rearrange("a b (p j) -> p (a b j)", j=4))
+        nc.sync.dma_start(out=scale4[:], in_=m_kj_scale.rearrange("a b (p j) -> p (a b j)", j=4))
+        load_bytes(0, 2)
         gain8 = const.tile([P, 2, 4], BF16, name="gain8", align_bytes=64)
         nc.scalar.dma_start(out=gain8[:], in_=gain.rearrange("(g p j) -> p g j", g=2, j=4))
         sbf_sb = const.tile([P, 2, K * NB], BF16, name="sbf_sb", align_bytes=64)
@@ -134,7 +134,10 @@ def tile_dimenettripletbilinear_kernel(tc, m_kj_bytes, m_kj_scale, m_ji, sbf, w_
             if d0 == 0:
                 grp_t = const.tile([P, 256, 4], BF16, name="wb_grp%d%d" % (g, b), align_bytes=64)
                 wb_grp[g, b] = grp_t
-            engine(out=wb_grp[g, b][:, d0:d1], in_=wb_raw[g, b][:].rearrange("p j d -> p d j")[:, d0:d1])
+            engine(
+                out=wb_grp[g, b][:, d0:d1].rearrange("p (c i) j -> p c j i", i=4),
+                in_=wb_raw[g, b][:, :, d0:d1].rearrange("p j (c i) -> p c j i", i=4),
+            )
 
         def wb_quantise(g, b):
             cols = slice(b * 256, (b + 1) * 256)
@@ -333,20 +336,20 @@ def tile_dimenettripletbilinear_kernel(tc, m_kj_bytes, m_kj_scale, m_ji, sbf, w_
             o_last.append(o_t)
 
         scale_bank = scale_spread()
-        scale_copy_split(scale_bank)
-        gain_spread()
         cast_split(0)
         head_transpose(0)
         cast_split(1)
         head_transpose(1)
         wd_interleave()
         cast(2, 4)
+        scale_copy_split(scale_bank)
         cast(4, 6)
         cast(6, 8)
         head_product(0)
         wd_quantise()
         m_quant(0, 0, 1)
         stage1(0, 0, 1)
+        gain_spread()
         silu1(0, 0, 1)
         head_product(1)
         head_transpose(2)

@@ -79,6 +79,8 @@ def tile_dimenettripletbilinear_kernel(tc, m_kj_bytes, m_kj_scale, m_ji, sbf, w_
         nc.vector.memset(one[:], 1.0)
         warm = const.tile([P, 1], F32, name="warm")
         nc.scalar.activation(out=warm[:], in_=one[:], func=SILU)
+        ident_bf = const.tile([P, P], BF16, name="ident_bf", align_bytes=64)
+        nc.vector.tensor_copy(out=ident_bf[:], in_=ident[:])
         ident4 = const.tile([P, P], BF16, name="ident4", align_bytes=64)
         nc.vector.tensor_scalar(out=ident4[:], in0=ident[:], scalar1=4.0, scalar2=None, op0=MULT)
 
@@ -123,25 +125,29 @@ def tile_dimenettripletbilinear_kernel(tc, m_kj_bytes, m_kj_scale, m_ji, sbf, w_
         def wd_quantise():
             nc.vector.quantize_mx(out=wd_codes[:].bitcast(FP8X4), scales=wd_sc[:], in_=wd_grp[:].rearrange("p c j -> p (c j)"))
 
-        wb_grp, wb_codes, wb_sc = {}, [], []
+        wb_ps, wb_grp, wb_codes, wb_sc = {}, {}, [], []
         for g in range(2):
             codes_t = const.tile([P, D], U32, name="wb_codes%d" % g, align_bytes=64)
             sc_t = const.tile([P, D], U8, name="wb_sc%d" % g, align_bytes=64)
             wb_codes.append(codes_t)
             wb_sc.append(sc_t)
 
-        def wb_interleave(engine, g, b, d0, d1):
-            if d0 == 0:
-                grp_t = const.tile([P, 256, 4], BF16, name="wb_grp%d%d" % (g, b), align_bytes=64)
-                wb_grp[g, b] = grp_t
-            engine(
-                out=wb_grp[g, b][:, d0:d1].rearrange("p (c i) j -> p c j i", i=4),
-                in_=wb_raw[g, b][:, :, d0:d1].rearrange("p j (c i) -> p c j i", i=4),
-            )
+        def wb_interleave(g, b):
+            b_t = bank()
+            rows = wb_raw[g, b][:].rearrange("p j d -> p d j")
+            for i in range(2):
+                nc.tensor.matmul(out=b_t[:].bitcast(BF16)[:, i * 512:(i + 1) * 512], lhsT=ident_bf[:], rhs=rows[:, i * P:(i + 1) * P], start=True, stop=True)
+            wb_ps[g, b] = b_t
+
+        def wb_copy(engine, g, b):
+            grp_t = const.tile([P, NBC], BF16, name="wb_grp%d%d" % (g, b), align_bytes=64)
+            engine(out=grp_t[:], in_=wb_ps[g, b][:].bitcast(BF16))
+            free.append(wb_ps[g, b])
+            wb_grp[g, b] = grp_t
 
         def wb_quantise(g, b):
             cols = slice(b * 256, (b + 1) * 256)
-            nc.vector.quantize_mx(out=wb_codes[g][:, cols].bitcast(FP8X4), scales=wb_sc[g][:, cols], in_=wb_grp[g, b][:].rearrange("p d j -> p (d j)"))
+            nc.vector.quantize_mx(out=wb_codes[g][:, cols].bitcast(FP8X4), scales=wb_sc[g][:, cols], in_=wb_grp[g, b][:])
 
         mtr, mcode, yps, xs, pts, ptr, pqs, pcode, mm, tts, aggs, head = ({} for a in range(12))
         casts = []
@@ -340,6 +346,7 @@ def tile_dimenettripletbilinear_kernel(tc, m_kj_bytes, m_kj_scale, m_ji, sbf, w_
         head_transpose(0)
         cast_split(1)
         head_transpose(1)
+        gain_spread()
         wd_interleave()
         cast(2, 4)
         scale_copy_split(scale_bank)
@@ -349,61 +356,68 @@ def tile_dimenettripletbilinear_kernel(tc, m_kj_bytes, m_kj_scale, m_ji, sbf, w_
         wd_quantise()
         m_quant(0, 0, 1)
         stage1(0, 0, 1)
-        gain_spread()
         silu1(0, 0, 1)
         head_product(1)
-        head_transpose(2)
-        wb_interleave(nc.vector.tensor_copy, 0, 0, 0, 128)
         m_quant(0, 1, 2)
         product_gpsimd(2)
-        wb_interleave(nc.vector.tensor_copy, 0, 0, 128, 256)
+        wb_interleave(0, 0)
+        cast(8, 10)
+        wb_copy(nc.scalar.copy, 0, 0)
+        head_transpose(2)
         head_transpose(3)
         stage1(0, 1, 2)
-        cast(8, 10)
-        wb_interleave(nc.scalar.copy, 1, 0, 0, 256)
+        wb_interleave(1, 0)
         silu1(0, 1, 2)
+        cast(10, 11)
+        wb_copy(nc.scalar.copy, 1, 0)
         p_ops(0)
         head_product(2)
         head_product(3)
         p_transpose(0, 0, 2)
-        wb_interleave(nc.scalar.copy, 0, 1, 0, 256)
+        cast(11, 12)
+        cast(12, 13)
         p_copy(nc.scalar.copy, 0, 0, 2)
         wb_quantise(0, 0)
         m_quant(1, 0, 2)
         product_gpsimd(3)
         wb_quantise(1, 0)
-        cast(10, 12)
+        wb_interleave(0, 1)
         m_transpose(2)
         stage1(1, 0, 2)
+        wb_interleave(1, 1)
+        wb_copy(nc.scalar.copy, 0, 1)
         silu1(1, 0, 2)
         m_copy(2)
-        wb_interleave(nc.scalar.copy, 1, 1, 0, 256)
+        wb_copy(nc.scalar.copy, 1, 1)
+        cast(13, 14)
+        cast(14, 16)
         p_ops(1)
         p_transpose(1, 0, 2)
         p_ops(2)
         wb_quantise(0, 1)
+        wb_quantise(1, 1)
         m_quant(2, 0, 2)
         product_gpsimd(4)
-        wb_quantise(1, 1)
         p_quant(0, 0, 2)
         p_copy(nc.scalar.copy, 1, 0, 2)
-        cast(12, 14)
-        cast(14, 16)
+        cast(16, 18)
         m_transpose(3)
-        stage1(2, 0, 2)
         p_transpose(2, 0, 2)
+        stage1(2, 0, 2)
+        cast(18, 19)
         silu1(2, 0, 2)
         p_copy(nc.scalar.copy, 2, 0, 2)
         m_copy(3)
         stage2(0, 0, 4)
         agg_open(0)
         silu2(0, 0, 512)
-        cast(16, 18)
+        cast(19, 20)
+        cast(20, 22)
         p_ops(3)
         p_transpose(3, 0, 2)
         p_ops(4)
 
-        to_cast = 18
+        to_cast = 22
         for j in range(3, PAIRS - 2):
             m_quant(j, 0, 2)
             product_gpsimd(j + 2)
@@ -416,9 +430,8 @@ def tile_dimenettripletbilinear_kernel(tc, m_kj_bytes, m_kj_scale, m_ji, sbf, w_
             p_copy(nc.scalar.copy, 2 * j - 2, 0, 2)
             m_copy(j + 1)
             if to_cast < TILES:
-                count = 2 if j % 3 == 0 else 1
-                cast(to_cast, to_cast + count)
-                to_cast = to_cast + count
+                cast(to_cast, to_cast + 1)
+                to_cast = to_cast + 1
             stage2(j - 2, 0, 2)
             stage2(j - 2, 2, 4)
             silu2(j - 2, 0, 512)

@@ -34,14 +34,15 @@ def tile_dimenettripletbilinear_kernel(tc, m_kj_bytes, m_kj_scale, m_ji, sbf, w_
 
         mbytes = {}
 
-        def load_bytes(t0, t1):
-            t_t = const.tile([P, (t1 - t0) * D], U8, name="mbytes%d" % t0, align_bytes=64)
+        def load_bytes(t0, t1, step=1):
+            tiles = range(t0, t1, step)
+            t_t = const.tile([P, len(tiles) * D], U8, name="mbytes%d" % t0, align_bytes=64)
             h = t0 // HALF
             nc.sync.dma_start(
-                out=t_t[:], in_=m_kj_bytes[h * P:(h + 1) * P, t0 - h * HALF:t1 - h * HALF, :].rearrange("e k d -> e (k d)")
+                out=t_t[:].rearrange("e (k d) -> e k d", d=D), in_=m_kj_bytes[h * P:(h + 1) * P, t0 - h * HALF:t1 - h * HALF:step, :]
             )
-            for t in range(t0, t1, 2):
-                mbytes[t // 2] = t_t[:, (t - t0) * D:(t - t0 + 2) * D].bitcast(FP8)
+            for i, t in enumerate(tiles):
+                mbytes[t] = t_t[:, i * D:]
 
         scale4 = const.tile([P, 4], F32, name="scale4", align_bytes=64)
         nc.sync.dma_start(out=scale4[:], in_=m_kj_scale.rearrange("a b (p j) -> p (a b j)", j=4))
@@ -65,13 +66,15 @@ def tile_dimenettripletbilinear_kernel(tc, m_kj_bytes, m_kj_scale, m_ji, sbf, w_
         load_wb(0, 0)
         load_bytes(8, 12)
         load_wb(1, 0)
+        load_bytes(12, 16, 2)
         load_wb(0, 1)
+        load_bytes(16, 24, 2)
         load_wb(1, 1)
-        load_bytes(12, 16)
+        load_bytes(24, 32, 2)
         mji = const.tile([P, 2, D], BF16, name="mji", align_bytes=64)
         nc.sync.dma_start(out=mji[:], in_=m_ji.rearrange("(h e) d -> e h d", e=P))
-        load_bytes(16, 24)
-        load_bytes(24, 32)
+        load_bytes(13, 16, 2)
+        load_bytes(17, 32, 2)
 
         ident = const.tile([P, P], F32, name="ident", align_bytes=64)
         make_identity(nc, ident[:])
@@ -134,10 +137,18 @@ def tile_dimenettripletbilinear_kernel(tc, m_kj_bytes, m_kj_scale, m_ji, sbf, w_
 
         def wb_interleave(g, b):
             b_t = bank()
-            rows = wb_raw[g, b][:].rearrange("p j d -> p d j")
             for i in range(2):
-                nc.tensor.matmul(out=b_t[:].bitcast(BF16)[:, i * 512:(i + 1) * 512], lhsT=ident_bf[:], rhs=rows[:, i * P:(i + 1) * P], start=True, stop=True)
+                nc.tensor.matmul(
+                    out=b_t[:].bitcast(BF16)[:, i * 512:(i + 1) * 512].rearrange("p (c i j) -> p c j i", i=8, j=4), lhsT=ident_bf[:],
+                    rhs=wb_raw[g, b][:, :, i * P:(i + 1) * P].rearrange("p j (c i) -> p c j i", i=8), start=True, stop=True,
+                )
             wb_ps[g, b] = b_t
+
+        def wb_interleave_vector(g, b, d0, d1):
+            if d0 == 0:
+                grp_t = const.tile([P, NBC], BF16, name="wb_grp%d%d" % (g, b), align_bytes=64)
+                wb_grp[g, b] = grp_t
+            nc.vector.tensor_copy(out=wb_grp[g, b][:].rearrange("p (d j) -> p d j", j=4)[:, d0:d1], in_=wb_raw[g, b][:].rearrange("p j d -> p d j")[:, d0:d1])
 
         def wb_copy(engine, g, b):
             grp_t = const.tile([P, NBC], BF16, name="wb_grp%d%d" % (g, b), align_bytes=64)
@@ -163,12 +174,12 @@ def tile_dimenettripletbilinear_kernel(tc, m_kj_bytes, m_kj_scale, m_ji, sbf, w_
             cols = slice(t % 2 * D, (t % 2 + 1) * D)
             nc.vector.tensor_scalar(
                 out=casts[t // 2][:, cols].rearrange("p (u w e) -> p w u e", u=2, e=2),
-                in0=mbytes[t // 2][:, cols].rearrange("p (w u e) -> p w u e", u=2, e=2), scalar1=one[:], scalar2=None, op0=MULT,
+                in0=mbytes[t][:, 0:D].bitcast(FP8).rearrange("p (w u e) -> p w u e", u=2, e=2), scalar1=one[:], scalar2=None, op0=MULT,
             )
 
         def cast(t0, t1):
             cols = slice(t0 % 2 * D, (t0 % 2 + t1 - t0) * D)
-            nc.scalar.copy(out=casts[t0 // 2][:, cols], in_=mbytes[t0 // 2][:, cols])
+            nc.scalar.copy(out=casts[t0 // 2][:, cols], in_=mbytes[t0][:, 0:(t1 - t0) * D].bitcast(FP8))
 
         def product_gpsimd(j):
             nc.gpsimd.tensor_tensor(
@@ -218,11 +229,12 @@ def tile_dimenettripletbilinear_kernel(tc, m_kj_bytes, m_kj_scale, m_ji, sbf, w_
         gain_bf = gain_ps[:].bitcast(BF16).rearrange("p (g u n w) -> p g u n w", g=2, u=2, n=4)
         sbf_cols = sbf_sb[:].rearrange("p h k -> p (h k)")
 
-        def p_ops(t):
-            p_t = work.tile([P, NBC], BF16, name="pt", bufs=3, align_bytes=64)
-            pts[t] = p_t
-            view = p_t[:].rearrange("p (g u n w) -> p g u n w", g=2, u=2, n=4)
-            for n in range(NB):
+        def p_ops(t, n0=0, n1=NB):
+            if n0 == 0:
+                p_t = work.tile([P, NBC], BF16, name="pt", bufs=3, align_bytes=64)
+                pts[t] = p_t
+            view = pts[t][:].rearrange("p (g u n w) -> p g u n w", g=2, u=2, n=4)
+            for n in range(n0, n1):
                 col = t * NB + n
                 nc.vector.scalar_tensor_tensor(
                     out=view[:, n // 4, :, n % 4, :], in0=xs[t], scalar=sbf_cols[:, col:col + 1],
@@ -318,6 +330,10 @@ def tile_dimenettripletbilinear_kernel(tc, m_kj_bytes, m_kj_scale, m_ji, sbf, w_
             cols = slice(d0 * P, d1 * P)
             nc.vector.scalar_tensor_tensor(out=dst[:, cols], in0=tts[c, first][:, (d0 - first) * P:(d1 - first) * P], scalar=0.25, in1=src[:, cols], op0=MULT, op1=ADD)
 
+        def close_vector(h):
+            nc.vector.tensor_scalar(out=sums[h][:], in0=aggs[h][:], scalar1=0.25, scalar2=None, op0=MULT)
+            nc.sync.dma_start(out=out[h * P:(h + 1) * P, :], in_=sums[h][:])
+
         def head_transpose(t):
             b_t = bank()
             words = casts[t // 2][:, t % 2 * D:(t % 2 + 1) * D].bitcast(F32)
@@ -358,67 +374,90 @@ def tile_dimenettripletbilinear_kernel(tc, m_kj_bytes, m_kj_scale, m_ji, sbf, w_
         stage1(0, 0, 1)
         silu1(0, 0, 1)
         head_product(1)
+        wb_interleave_vector(0, 0, 0, 128)
         m_quant(0, 1, 2)
         product_gpsimd(2)
-        wb_interleave(0, 0)
-        cast(8, 10)
-        wb_copy(nc.scalar.copy, 0, 0)
+        wb_interleave_vector(0, 0, 128, 256)
         head_transpose(2)
         head_transpose(3)
         stage1(0, 1, 2)
         wb_interleave(1, 0)
-        silu1(0, 1, 2)
+        cast(8, 9)
         cast(10, 11)
-        wb_copy(nc.scalar.copy, 1, 0)
-        p_ops(0)
+        silu1(0, 1, 2)
+        cast(12, 13)
+        cast(14, 15)
+        p_ops(0, 0, 4)
         head_product(2)
         head_product(3)
-        p_transpose(0, 0, 2)
-        cast(11, 12)
-        cast(12, 13)
-        p_copy(nc.scalar.copy, 0, 0, 2)
-        wb_quantise(0, 0)
+        p_ops(0, 4, 8)
+        wb_interleave(0, 1)
+        wb_copy(nc.scalar.copy, 1, 0)
+        cast(16, 17)
+        cast(18, 19)
+        wb_copy(nc.scalar.copy, 0, 1)
         m_quant(1, 0, 2)
         product_gpsimd(3)
-        wb_quantise(1, 0)
-        wb_interleave(0, 1)
-        m_transpose(2)
         stage1(1, 0, 2)
         wb_interleave(1, 1)
-        wb_copy(nc.scalar.copy, 0, 1)
+        m_transpose(2)
+        p_transpose(0, 0, 2)
+        cast(20, 21)
         silu1(1, 0, 2)
-        m_copy(2)
+        cast(22, 23)
+        cast(24, 25)
         wb_copy(nc.scalar.copy, 1, 1)
-        cast(13, 14)
-        cast(14, 16)
+        m_copy(2)
+        p_copy(nc.scalar.copy, 0, 0, 2)
+        cast(9, 10)
         p_ops(1)
         p_transpose(1, 0, 2)
         p_ops(2)
+        wb_quantise(0, 0)
+        wb_quantise(1, 0)
         wb_quantise(0, 1)
         wb_quantise(1, 1)
         m_quant(2, 0, 2)
         product_gpsimd(4)
         p_quant(0, 0, 2)
         p_copy(nc.scalar.copy, 1, 0, 2)
-        cast(16, 18)
+        cast(26, 27)
         m_transpose(3)
         p_transpose(2, 0, 2)
         stage1(2, 0, 2)
-        cast(18, 19)
+        cast(28, 29)
         silu1(2, 0, 2)
         p_copy(nc.scalar.copy, 2, 0, 2)
         m_copy(3)
+        cast(11, 12)
         stage2(0, 0, 4)
         agg_open(0)
         silu2(0, 0, 512)
-        cast(19, 20)
-        cast(20, 22)
+        cast(30, 31)
         p_ops(3)
         p_transpose(3, 0, 2)
         p_ops(4)
+        m_quant(3, 0, 2)
+        product_gpsimd(5)
+        p_quant(1, 0, 2)
+        p_copy(nc.scalar.copy, 3, 0, 2)
+        m_transpose(4)
+        p_transpose(4, 0, 2)
+        stage1(3, 0, 2)
+        silu1(3, 0, 2)
+        p_copy(nc.scalar.copy, 4, 0, 2)
+        m_copy(4)
+        cast(13, 14)
+        stage2(1, 0, 2)
+        stage2(1, 2, 4)
+        silu2(1, 0, 512)
+        silu2(1, 2, 512)
+        p_ops(5)
+        k_sum(0, 0, 4)
+        p_transpose(5, 0, 2)
+        p_ops(6)
 
-        to_cast = 22
-        for j in range(3, PAIRS - 2):
+        for j in range(4, PAIRS - 2):
             m_quant(j, 0, 2)
             product_gpsimd(j + 2)
             p_quant(j - 2, 0, 2)
@@ -429,9 +468,8 @@ def tile_dimenettripletbilinear_kernel(tc, m_kj_bytes, m_kj_scale, m_ji, sbf, w_
             silu1(j, 0, 2)
             p_copy(nc.scalar.copy, 2 * j - 2, 0, 2)
             m_copy(j + 1)
-            if to_cast < TILES:
-                cast(to_cast, to_cast + 1)
-                to_cast = to_cast + 1
+            if j + 3 < PAIRS:
+                cast(2 * j + 7, 2 * j + 8)
             stage2(j - 2, 0, 2)
             stage2(j - 2, 2, 4)
             silu2(j - 2, 0, 512)
@@ -439,11 +477,8 @@ def tile_dimenettripletbilinear_kernel(tc, m_kj_bytes, m_kj_scale, m_ji, sbf, w_
             if j == 9:
                 agg_open(1)
             p_ops(2 * j - 1)
-            if j == 3:
-                k_sum(0, 0, 4)
-            else:
-                k_sum(j - 3, 0, 2)
-                k_sum(j - 3, 2, 4)
+            k_sum(j - 3, 0, 2)
+            k_sum(j - 3, 2, 4)
             p_transpose(2 * j - 1, 0, 2)
             p_ops(2 * j)
 
@@ -487,8 +522,6 @@ def tile_dimenettripletbilinear_kernel(tc, m_kj_bytes, m_kj_scale, m_ji, sbf, w_
         p_copy(nc.scalar.copy, 29, 0, 2)
         stage2(14, 0, 2)
         stage2(14, 2, 4)
-        agg_close(0, 0, 4)
-        nc.sync.dma_start(out=out[0:P, :], in_=sums[0][:])
         silu2(14, 0, 512)
         p_ops(30)
         p_quant(15, 0, 2)
@@ -517,6 +550,7 @@ def tile_dimenettripletbilinear_kernel(tc, m_kj_bytes, m_kj_scale, m_ji, sbf, w_
         stage2_turned(17, 2, 4, 0)
         stage2_turned(17, 0, 2, 1)
         stage2_turned(17, 2, 4, 1)
+        close_vector(0)
         add_turned(with29, 15, 0, 0, 2, sums[1])
         add_turned(with29, 15, 0, 2, 4, sums[1])
         add_turned(with30, 16, 0, 0, 2, with29)

@@ -22,6 +22,7 @@ COPY = mybir.ActivationFunctionType.Copy
 TILES = 32
 PAIRS = 16
 HALF = 16
+WARM = 4
 
 
 def tile_dimenettripletbilinear_kernel(tc, m_kj_bytes, m_kj_scale, m_ji, sbf, w_down, gain, w_bil, out):
@@ -94,6 +95,10 @@ def tile_dimenettripletbilinear_kernel(tc, m_kj_bytes, m_kj_scale, m_ji, sbf, w_
 
         def bank():
             return free.pop(0)
+
+        def warm_tensor():
+            for i in range(WARM):
+                nc.tensor.matmul(out=free[-1][:].rearrange("p (r c) -> p r c", r=4), lhsT=ident_bf[:], rhs=ident_bf[:].unsqueeze(1).to_broadcast([P, 4, P]), start=True, stop=True)
 
         scale_split = const.tile([P, D], F32, name="scale_split", align_bytes=64)
 
@@ -357,9 +362,10 @@ def tile_dimenettripletbilinear_kernel(tc, m_kj_bytes, m_kj_scale, m_ji, sbf, w_
             o_t = const.tile([P, D], F32, name="o%d" % i, align_bytes=64)
             o_last.append(o_t)
 
-        scale_bank = scale_spread()
+        warm_tensor()
         cast_split(0)
         head_transpose(0)
+        scale_bank = scale_spread()
         cast_split(1)
         head_transpose(1)
         gain_spread()

@@ -22,7 +22,7 @@ COPY = mybir.ActivationFunctionType.Copy
 TILES = 32
 PAIRS = 16
 HALF = 16
-WARM = 4
+WARM = 3
 
 
 def tile_dimenettripletbilinear_kernel(tc, m_kj_bytes, m_kj_scale, m_ji, sbf, w_down, gain, w_bil, out):
@@ -47,7 +47,7 @@ def tile_dimenettripletbilinear_kernel(tc, m_kj_bytes, m_kj_scale, m_ji, sbf, w_
 
         scale4 = const.tile([P, 4], F32, name="scale4", align_bytes=64)
         nc.sync.dma_start(out=scale4[:], in_=m_kj_scale.rearrange("a b (p j) -> p (a b j)", j=4))
-        load_bytes(0, 2)
+        load_bytes(0, 1)
         gain8 = const.tile([P, 2, 4], BF16, name="gain8", align_bytes=64)
         nc.scalar.dma_start(out=gain8[:], in_=gain.rearrange("(g p j) -> p g j", g=2, j=4))
         sbf_sb = const.tile([P, 2, K * NB], BF16, name="sbf_sb", align_bytes=64)
@@ -60,9 +60,9 @@ def tile_dimenettripletbilinear_kernel(tc, m_kj_bytes, m_kj_scale, m_ji, sbf, w_
             nc.sync.dma_start(out=wb_t[:], in_=wb_hbm[g][:, :, b * 256:(b + 1) * 256])
             wb_raw[g, b] = wb_t
 
-        load_bytes(2, 4)
         wd_raw = const.tile([P, 4, C], BF16, name="wd_raw", align_bytes=64)
         nc.sync.dma_start(out=wd_raw[:], in_=w_down.rearrange("(p j) c -> p j c", j=4))
+        load_bytes(1, 4)
         load_bytes(4, 8)
         load_wb(0, 0)
         load_bytes(8, 12)
@@ -297,11 +297,12 @@ def tile_dimenettripletbilinear_kernel(tc, m_kj_bytes, m_kj_scale, m_ji, sbf, w_
                 rhs=wb_codes[g][:, cols].bitcast(FP8X4), rhs_scale=wb_sc[g][:, cols], start=(g == 0), stop=(g == 1),
             )
 
-        def silu2(c, d0, width):
-            t_t = work.tile([P, 4 * P], F32, name="tt", bufs=8, align_bytes=64)
-            nc.scalar.activation(out=t_t[:, 0:width], in_=mm[c, d0][:, 0:width], func=SILU)
-            free.append(mm[c, d0])
-            tts[c, d0] = t_t
+        def silu2(c, d0, width, first=0):
+            if first == 0:
+                t_t = work.tile([P, 4 * P], F32, name="tt", bufs=8, align_bytes=64)
+                tts[c, d0] = t_t
+                free.append(mm[c, d0])
+            nc.scalar.activation(out=tts[c, d0][:, first:width], in_=mm[c, d0][:, first:width], func=SILU)
 
         def agg_open(h):
             agg_t = bank()
@@ -335,15 +336,18 @@ def tile_dimenettripletbilinear_kernel(tc, m_kj_bytes, m_kj_scale, m_ji, sbf, w_
             cols = slice(d0 * P, d1 * P)
             nc.vector.scalar_tensor_tensor(out=dst[:, cols], in0=tts[c, first][:, (d0 - first) * P:(d1 - first) * P], scalar=0.25, in1=src[:, cols], op0=MULT, op1=ADD)
 
-        def close_vector(h):
-            nc.vector.tensor_scalar(out=sums[h][:], in0=aggs[h][:], scalar1=0.25, scalar2=None, op0=MULT)
-            nc.sync.dma_start(out=out[h * P:(h + 1) * P, :], in_=sums[h][:])
+        def scale_turned(dst, c):
+            nc.vector.tensor_scalar(out=dst[:], in0=tts[c, 0][:], scalar1=0.25, scalar2=None, op0=MULT)
+
+        def add_sum(dst, h, d0, d1, src):
+            cols = slice(d0 * P, d1 * P)
+            nc.vector.scalar_tensor_tensor(out=dst[:, cols], in0=aggs[h][:, cols], scalar=0.25, in1=src[:, cols], op0=MULT, op1=ADD)
 
         def head_transpose(t):
             b_t = bank()
             words = casts[t // 2][:, t % 2 * D:(t % 2 + 1) * D].bitcast(F32)
             for u in range(2):
-                half = words[:, u * P:(u + 1) * P] if t < 2 else words[:, u:256:2]
+                half = words[:, u * P:(u + 1) * P] if t == 0 else words[:, u:256:2]
                 nc.tensor.transpose(b_t[:, u * P:(u + 1) * P], half, ident[:])
             head[t] = b_t
 
@@ -366,19 +370,19 @@ def tile_dimenettripletbilinear_kernel(tc, m_kj_bytes, m_kj_scale, m_ji, sbf, w_
         cast_split(0)
         head_transpose(0)
         scale_bank = scale_spread()
-        cast_split(1)
+        cast(1, 2)
         head_transpose(1)
         gain_spread()
         wd_interleave()
         cast(2, 4)
         scale_copy_split(scale_bank)
         cast(4, 6)
-        cast(6, 8)
         head_product(0)
         wd_quantise()
         m_quant(0, 0, 1)
         stage1(0, 0, 1)
         silu1(0, 0, 1)
+        cast(6, 8)
         head_product(1)
         wb_interleave_vector(0, 0, 0, 128)
         m_quant(0, 1, 2)
@@ -389,8 +393,8 @@ def tile_dimenettripletbilinear_kernel(tc, m_kj_bytes, m_kj_scale, m_ji, sbf, w_
         stage1(0, 1, 2)
         wb_interleave(1, 0)
         cast(8, 9)
-        cast(10, 11)
         silu1(0, 1, 2)
+        cast(10, 11)
         cast(12, 13)
         cast(14, 15)
         p_ops(0, 0, 4)
@@ -398,22 +402,21 @@ def tile_dimenettripletbilinear_kernel(tc, m_kj_bytes, m_kj_scale, m_ji, sbf, w_
         head_product(3)
         p_ops(0, 4, 8)
         wb_interleave(0, 1)
-        wb_copy(nc.scalar.copy, 1, 0)
         cast(16, 17)
+        wb_copy(nc.scalar.copy, 1, 0)
         cast(18, 19)
-        wb_copy(nc.scalar.copy, 0, 1)
+        cast(20, 21)
         m_quant(1, 0, 2)
         product_gpsimd(3)
         stage1(1, 0, 2)
-        wb_interleave(1, 1)
         m_transpose(2)
+        wb_interleave(1, 1)
         p_transpose(0, 0, 2)
-        cast(20, 21)
         silu1(1, 0, 2)
-        cast(22, 23)
-        cast(24, 25)
-        wb_copy(nc.scalar.copy, 1, 1)
+        wb_copy(nc.scalar.copy, 0, 1)
         m_copy(2)
+        cast(22, 23)
+        wb_copy(nc.scalar.copy, 1, 1)
         p_copy(nc.scalar.copy, 0, 0, 2)
         cast(9, 10)
         p_ops(1)
@@ -427,19 +430,19 @@ def tile_dimenettripletbilinear_kernel(tc, m_kj_bytes, m_kj_scale, m_ji, sbf, w_
         product_gpsimd(4)
         p_quant(0, 0, 2)
         p_copy(nc.scalar.copy, 1, 0, 2)
-        cast(26, 27)
         m_transpose(3)
         p_transpose(2, 0, 2)
         stage1(2, 0, 2)
-        cast(28, 29)
         silu1(2, 0, 2)
+        cast(24, 25)
         p_copy(nc.scalar.copy, 2, 0, 2)
         m_copy(3)
         cast(11, 12)
         stage2(0, 0, 4)
         agg_open(0)
+        cast(26, 27)
         silu2(0, 0, 512)
-        cast(30, 31)
+        cast(28, 29)
         p_ops(3)
         p_transpose(3, 0, 2)
         p_ops(4)
@@ -456,6 +459,7 @@ def tile_dimenettripletbilinear_kernel(tc, m_kj_bytes, m_kj_scale, m_ji, sbf, w_
         cast(13, 14)
         stage2(1, 0, 2)
         stage2(1, 2, 4)
+        cast(30, 31)
         silu2(1, 0, 512)
         silu2(1, 2, 512)
         p_ops(5)
@@ -512,11 +516,11 @@ def tile_dimenettripletbilinear_kernel(tc, m_kj_bytes, m_kj_scale, m_ji, sbf, w_
         stage1(15, 0, 2)
         stage2(13, 2, 4)
         silu2(13, 0, 512)
+        silu1(15, 0, 2)
         p_transpose(28, 0, 1)
         p_transpose(28, 1, 2)
         p_copy(nc.scalar.copy, 28, 0, 1)
         p_copy(nc.scalar.copy, 28, 1, 2)
-        silu1(15, 0, 2)
         silu2(13, 2, 512)
         k_sum(11, 2, 4)
         k_sum(12, 0, 2)
@@ -531,8 +535,8 @@ def tile_dimenettripletbilinear_kernel(tc, m_kj_bytes, m_kj_scale, m_ji, sbf, w_
         silu2(14, 0, 512)
         p_ops(30)
         p_quant(15, 0, 2)
-        k_sum(13, 2, 4)
         p_transpose(30, 0, 2)
+        k_sum(13, 2, 4)
         silu2(14, 2, 512)
         p_copy(nc.scalar.copy, 30, 0, 2)
         stage2_turned(15, 0, 4, 0)
@@ -540,27 +544,31 @@ def tile_dimenettripletbilinear_kernel(tc, m_kj_bytes, m_kj_scale, m_ji, sbf, w_
         p_ops(31)
         p_quant(16, 0, 2)
         p_transpose(31, 0, 1)
-        k_sum(14, 0, 2)
         p_transpose(31, 1, 2)
+        k_sum(14, 0, 2)
         k_sum(14, 2, 4)
         silu2(15, 0, 512)
         p_copy(nc.vector.tensor_copy, 31, 0, 1)
         p_copy(nc.vector.tensor_copy, 31, 1, 2)
-        stage2_turned(16, 0, 4, 0)
-        stage2_turned(16, 0, 4, 1)
+        stage2_turned(16, 0, 2, 0)
+        stage2_turned(16, 0, 2, 1)
+        stage2_turned(16, 2, 4, 0)
+        stage2_turned(16, 2, 4, 1)
         p_quant(17, 0, 1)
+        scale_turned(sums[1], 15)
         p_quant(17, 1, 2)
-        agg_close(1, 0, 4)
-        silu2(16, 0, 512)
+        agg_close(0, 0, 4)
+        nc.sync.dma_start(out=out[0:P, :], in_=sums[0][:])
+        silu2(16, 0, 256)
+        silu2(16, 2, 256)
         stage2_turned(17, 0, 2, 0)
         stage2_turned(17, 2, 4, 0)
         stage2_turned(17, 0, 2, 1)
         stage2_turned(17, 2, 4, 1)
-        close_vector(0)
-        add_turned(with29, 15, 0, 0, 2, sums[1])
-        add_turned(with29, 15, 0, 2, 4, sums[1])
+        add_sum(with29, 1, 0, 2, sums[1])
+        add_sum(with29, 1, 2, 4, sums[1])
         add_turned(with30, 16, 0, 0, 2, with29)
-        add_turned(with30, 16, 0, 2, 4, with29)
+        add_turned(with30, 16, 2, 2, 4, with29)
         silu2(17, 0, 256)
         add_turned(o_last[0], 17, 0, 0, 2, with30)
         nc.sync.dma_start(out=out[P:2 * P, 0 * P:2 * P], in_=o_last[0][:, 0 * P:2 * P])

@@ -83,6 +83,8 @@ def tile_dimenettripletbilinear_kernel(tc, m_kj_bytes, m_kj_scale, m_ji, sbf, w_
         nc.vector.memset(one[:], 1.0)
         warm = const.tile([P, 1], F32, name="warm")
         nc.scalar.activation(out=warm[:], in_=one[:], func=SILU)
+        sbf32 = const.tile([P, 2 * K * NB], F32, name="sbf32", align_bytes=64)
+        nc.scalar.copy(out=sbf32[:], in_=sbf_sb[:].rearrange("p h k -> p (h k)"))
         ident_bf = const.tile([P, P], BF16, name="ident_bf", align_bytes=64)
         nc.vector.tensor_copy(out=ident_bf[:], in_=ident[:])
         ident4 = const.tile([P, P], BF16, name="ident4", align_bytes=64)
@@ -232,7 +234,7 @@ def tile_dimenettripletbilinear_kernel(tc, m_kj_bytes, m_kj_scale, m_ji, sbf, w_
                 xs[2 * j + a] = x_t[:, a * P:(a + 1) * P].rearrange("p (u w) -> p u w", u=2)
 
         gain_bf = gain_ps[:].bitcast(BF16).rearrange("p (g u n w) -> p g u n w", g=2, u=2, n=4)
-        sbf_cols = sbf_sb[:].rearrange("p h k -> p (h k)")
+        sbf_cols = sbf32[:]
 
         def p_ops(t, n0=0, n1=NB):
             if n0 == 0:
@@ -430,19 +432,20 @@ def tile_dimenettripletbilinear_kernel(tc, m_kj_bytes, m_kj_scale, m_ji, sbf, w_
         product_gpsimd(4)
         p_quant(0, 0, 2)
         p_copy(nc.scalar.copy, 1, 0, 2)
+        cast(24, 25)
         m_transpose(3)
         p_transpose(2, 0, 2)
         stage1(2, 0, 2)
         silu1(2, 0, 2)
-        cast(24, 25)
+        cast(26, 27)
         p_copy(nc.scalar.copy, 2, 0, 2)
         m_copy(3)
         cast(11, 12)
         stage2(0, 0, 4)
         agg_open(0)
-        cast(26, 27)
         silu2(0, 0, 512)
         cast(28, 29)
+        cast(30, 31)
         p_ops(3)
         p_transpose(3, 0, 2)
         p_ops(4)
@@ -459,7 +462,6 @@ def tile_dimenettripletbilinear_kernel(tc, m_kj_bytes, m_kj_scale, m_ji, sbf, w_
         cast(13, 14)
         stage2(1, 0, 2)
         stage2(1, 2, 4)
-        cast(30, 31)
         silu2(1, 0, 512)
         silu2(1, 2, 512)
         p_ops(5)
@@ -516,11 +518,11 @@ def tile_dimenettripletbilinear_kernel(tc, m_kj_bytes, m_kj_scale, m_ji, sbf, w_
         stage1(15, 0, 2)
         stage2(13, 2, 4)
         silu2(13, 0, 512)
-        silu1(15, 0, 2)
         p_transpose(28, 0, 1)
         p_transpose(28, 1, 2)
         p_copy(nc.scalar.copy, 28, 0, 1)
         p_copy(nc.scalar.copy, 28, 1, 2)
+        silu1(15, 0, 2)
         silu2(13, 2, 512)
         k_sum(11, 2, 4)
         k_sum(12, 0, 2)

@@ -46,8 +46,10 @@ def tile_dimenettripletbilinear_kernel(tc, m_kj_bytes, m_kj_scale, m_ji, sbf, w_
                 mbytes[t] = t_t[:, i * D:]
 
         scale4 = const.tile([P, 4], F32, name="scale4", align_bytes=64)
-        nc.sync.dma_start(out=scale4[:], in_=m_kj_scale.rearrange("a b (p j) -> p (a b j)", j=4))
+        nc.scalar.dma_start(out=scale4[:], in_=m_kj_scale.rearrange("a b (p j) -> p (a b j)", j=4))
         load_bytes(0, 1)
+        wd_raw = const.tile([P, 4, C], BF16, name="wd_raw", align_bytes=64)
+        nc.scalar.dma_start(out=wd_raw[:], in_=w_down.rearrange("(p j) c -> p j c", j=4))
         gain8 = const.tile([P, 2, 4], BF16, name="gain8", align_bytes=64)
         nc.scalar.dma_start(out=gain8[:], in_=gain.rearrange("(g p j) -> p g j", g=2, j=4))
         sbf_sb = const.tile([P, 2, K * NB], BF16, name="sbf_sb", align_bytes=64)
@@ -60,8 +62,6 @@ def tile_dimenettripletbilinear_kernel(tc, m_kj_bytes, m_kj_scale, m_ji, sbf, w_
             nc.sync.dma_start(out=wb_t[:], in_=wb_hbm[g][:, :, b * 256:(b + 1) * 256])
             wb_raw[g, b] = wb_t
 
-        wd_raw = const.tile([P, 4, C], BF16, name="wd_raw", align_bytes=64)
-        nc.sync.dma_start(out=wd_raw[:], in_=w_down.rearrange("(p j) c -> p j c", j=4))
         load_bytes(1, 4)
         load_bytes(4, 8)
         load_wb(0, 0)
@@ -83,8 +83,6 @@ def tile_dimenettripletbilinear_kernel(tc, m_kj_bytes, m_kj_scale, m_ji, sbf, w_
         nc.vector.memset(one[:], 1.0)
         warm = const.tile([P, 1], F32, name="warm")
         nc.scalar.activation(out=warm[:], in_=one[:], func=SILU)
-        sbf32 = const.tile([P, 2 * K * NB], F32, name="sbf32", align_bytes=64)
-        nc.scalar.copy(out=sbf32[:], in_=sbf_sb[:].rearrange("p h k -> p (h k)"))
         ident_bf = const.tile([P, P], BF16, name="ident_bf", align_bytes=64)
         nc.vector.tensor_copy(out=ident_bf[:], in_=ident[:])
         ident4 = const.tile([P, P], BF16, name="ident4", align_bytes=64)
@@ -234,7 +232,7 @@ def tile_dimenettripletbilinear_kernel(tc, m_kj_bytes, m_kj_scale, m_ji, sbf, w_
                 xs[2 * j + a] = x_t[:, a * P:(a + 1) * P].rearrange("p (u w) -> p u w", u=2)
 
         gain_bf = gain_ps[:].bitcast(BF16).rearrange("p (g u n w) -> p g u n w", g=2, u=2, n=4)
-        sbf_cols = sbf32[:]
+        sbf_cols = sbf_sb[:].rearrange("p h k -> p (h k)")
 
         def p_ops(t, n0=0, n1=NB):
             if n0 == 0:

@@ -22,7 +22,6 @@ COPY = mybir.ActivationFunctionType.Copy
 TILES = 32
 PAIRS = 16
 HALF = 16
-WARM = 3
 
 
 def tile_dimenettripletbilinear_kernel(tc, m_kj_bytes, m_kj_scale, m_ji, sbf, w_down, gain, w_bil, out):
@@ -33,52 +32,52 @@ def tile_dimenettripletbilinear_kernel(tc, m_kj_bytes, m_kj_scale, m_ji, sbf, w_
         psum = ctx.enter_context(tc.psum_pool(name="psum", bufs=1))
         ctx.enter_context(tc.manual_schedule())
 
-        mbytes = {}
+        mbytes, load_end = {}, {}
 
-        def load_bytes(t0, t1, step=1):
-            tiles = range(t0, t1, step)
+        def load_bytes(t0, t1):
+            tiles = range(t0, t1)
             t_t = const.tile([P, len(tiles) * D], U8, name="mbytes%d" % t0, align_bytes=64)
             h = t0 // HALF
             nc.sync.dma_start(
-                out=t_t[:].rearrange("e (k d) -> e k d", d=D), in_=m_kj_bytes[h * P:(h + 1) * P, t0 - h * HALF:t1 - h * HALF:step, :]
+                out=t_t[:].rearrange("e (k d) -> e k d", d=D), in_=m_kj_bytes[h * P:(h + 1) * P, t0 - h * HALF:t1 - h * HALF, :]
             )
             for i, t in enumerate(tiles):
                 mbytes[t] = t_t[:, i * D:]
+                load_end[t] = t1
 
-        scale4 = const.tile([P, 4], F32, name="scale4", align_bytes=64)
-        nc.scalar.dma_start(out=scale4[:], in_=m_kj_scale.rearrange("a b (p j) -> p (a b j)", j=4))
-        load_bytes(0, 1)
-        wd_raw = const.tile([P, 4, C], BF16, name="wd_raw", align_bytes=64)
-        nc.scalar.dma_start(out=wd_raw[:], in_=w_down.rearrange("(p j) c -> p j c", j=4))
-        gain8 = const.tile([P, 2, 4], BF16, name="gain8", align_bytes=64)
-        nc.scalar.dma_start(out=gain8[:], in_=gain.rearrange("(g p j) -> p g j", g=2, j=4))
-        sbf_sb = const.tile([P, 2, K * NB], BF16, name="sbf_sb", align_bytes=64)
-        nc.scalar.dma_start(out=sbf_sb[:], in_=sbf.rearrange("(h e) k n -> e h (k n)", e=P))
         wb_hbm = w_bil.rearrange("(g p j) d -> g p j d", g=2, j=4)
         wb_raw = {}
 
-        def load_wb(g, b):
-            wb_t = const.tile([P, 4, 256], BF16, name="wb_raw%d%d" % (g, b), align_bytes=64)
-            nc.sync.dma_start(out=wb_t[:], in_=wb_hbm[g][:, :, b * 256:(b + 1) * 256])
-            wb_raw[g, b] = wb_t
+        def load_wb(g, b0, b1):
+            wb_t = const.tile([P, 4, (b1 - b0) * 256], BF16, name="wb_raw%d%d" % (g, b0), align_bytes=64)
+            nc.sync.dma_start(out=wb_t[:], in_=wb_hbm[g][:, :, b0 * 256:b1 * 256])
+            for b in range(b0, b1):
+                wb_raw[g, b] = wb_t[:, :, (b - b0) * 256:(b - b0 + 1) * 256]
 
-        load_bytes(1, 4)
-        load_bytes(4, 8)
-        load_wb(0, 0)
-        load_bytes(8, 12)
-        load_wb(1, 0)
-        load_bytes(12, 16, 2)
-        load_wb(0, 1)
-        load_bytes(16, 24, 2)
-        load_wb(1, 1)
-        load_bytes(24, 32, 2)
+        scale4 = const.tile([P, 4], F32, name="scale4", align_bytes=64)
+        wd_raw = const.tile([P, 4, C], BF16, name="wd_raw", align_bytes=64)
+        gain8 = const.tile([P, 2, 4], BF16, name="gain8", align_bytes=64)
+        sbf_sb = const.tile([P, 2, K * NB], BF16, name="sbf_sb", align_bytes=64)
         mji = const.tile([P, 2, D], BF16, name="mji", align_bytes=64)
+        load_bytes(0, 2)
+        nc.scalar.dma_start(out=scale4[:], in_=m_kj_scale.rearrange("a b (p j) -> p (a b j)", j=4))
+        load_bytes(2, 4)
+        nc.scalar.dma_start(out=wd_raw[:], in_=w_down.rearrange("(p j) c -> p j c", j=4))
+        nc.scalar.dma_start(out=gain8[:], in_=gain.rearrange("(g p j) -> p g j", g=2, j=4))
+        load_bytes(4, 8)
+        nc.scalar.dma_start(out=sbf_sb[:], in_=sbf.rearrange("(h e) k n -> e h (k n)", e=P))
+        load_bytes(8, 12)
+        load_wb(0, 0, 2)
+        load_wb(1, 0, 2)
+        load_bytes(12, 16)
+        load_bytes(16, 24)
+        load_bytes(24, 32)
         nc.sync.dma_start(out=mji[:], in_=m_ji.rearrange("(h e) d -> e h d", e=P))
-        load_bytes(13, 16, 2)
-        load_bytes(17, 32, 2)
 
         ident = const.tile([P, P], F32, name="ident", align_bytes=64)
         make_identity(nc, ident[:])
+        zeros = const.tile([P, P], BF16, name="zeros", align_bytes=64)
+        nc.vector.memset(zeros[:], 0.0)
         one = const.tile([P, 1], F32, name="one")
         nc.vector.memset(one[:], 1.0)
         warm = const.tile([P, 1], F32, name="warm")
@@ -95,10 +94,6 @@ def tile_dimenettripletbilinear_kernel(tc, m_kj_bytes, m_kj_scale, m_ji, sbf, w_
 
         def bank():
             return free.pop(0)
-
-        def warm_tensor():
-            for i in range(WARM):
-                nc.tensor.matmul(out=free[-1][:].rearrange("p (r c) -> p r c", r=4), lhsT=ident_bf[:], rhs=ident_bf[:].unsqueeze(1).to_broadcast([P, 4, P]), start=True, stop=True)
 
         scale_split = const.tile([P, D], F32, name="scale_split", align_bytes=64)
 
@@ -140,20 +135,14 @@ def tile_dimenettripletbilinear_kernel(tc, m_kj_bytes, m_kj_scale, m_ji, sbf, w_
             wb_codes.append(codes_t)
             wb_sc.append(sc_t)
 
-        def wb_interleave(g, b):
-            b_t = bank()
-            for i in range(2):
+        def wb_interleave(g, b, i0=0, i1=2):
+            b_t = bank() if i0 == 0 else wb_ps[g, b]
+            for i in range(i0, i1):
                 nc.tensor.matmul(
                     out=b_t[:].bitcast(BF16)[:, i * 512:(i + 1) * 512].rearrange("p (c i j) -> p c j i", i=8, j=4), lhsT=ident_bf[:],
                     rhs=wb_raw[g, b][:, :, i * P:(i + 1) * P].rearrange("p j (c i) -> p c j i", i=8), start=True, stop=True,
                 )
             wb_ps[g, b] = b_t
-
-        def wb_interleave_vector(g, b, d0, d1):
-            if d0 == 0:
-                grp_t = const.tile([P, NBC], BF16, name="wb_grp%d%d" % (g, b), align_bytes=64)
-                wb_grp[g, b] = grp_t
-            nc.vector.tensor_copy(out=wb_grp[g, b][:].rearrange("p (d j) -> p d j", j=4)[:, d0:d1], in_=wb_raw[g, b][:].rearrange("p j d -> p d j")[:, d0:d1])
 
         def wb_copy(engine, g, b):
             grp_t = const.tile([P, NBC], BF16, name="wb_grp%d%d" % (g, b), align_bytes=64)
@@ -165,15 +154,26 @@ def tile_dimenettripletbilinear_kernel(tc, m_kj_bytes, m_kj_scale, m_ji, sbf, w_
             cols = slice(b * 256, (b + 1) * 256)
             nc.vector.quantize_mx(out=wb_codes[g][:, cols].bitcast(FP8X4), scales=wb_sc[g][:, cols], in_=wb_grp[g, b][:])
 
+        def wb_interleave_vector(g, b, d0, d1):
+            if d0 == 0:
+                grp_t = const.tile([P, NBC], BF16, name="wb_grp%d%d" % (g, b), align_bytes=64)
+                wb_grp[g, b] = grp_t
+            nc.vector.tensor_copy(out=wb_grp[g, b][:].rearrange("p (d j) -> p d j", j=4)[:, d0:d1], in_=wb_raw[g, b].rearrange("p j d -> p d j")[:, d0:d1])
+
+        def warm_tensor(n):
+            for i in range(n):
+                nc.tensor.matmul(out=free[-1][:].rearrange("p (r c) -> p r c", r=4), lhsT=zeros[:], rhs=zeros[:].unsqueeze(1).to_broadcast([P, 4, P]), start=True, stop=True)
+
         mtr, mcode, yps, xs, pts, ptr, pqs, pcode, mm, tts, aggs, head = ({} for a in range(12))
-        casts = []
-        for j in range(PAIRS):
-            cast_t = const.tile([P, 2 * D], BF16, name="cast%d" % j, align_bytes=64)
-            casts.append(cast_t)
+        widened = const.tile([P, TILES * D], BF16, name="widened", align_bytes=64)
+        casts = [widened[:, j * 2 * D:(j + 1) * 2 * D] for j in range(PAIRS)]
         ring = []
         for i in range(3):
             ring_t = const.tile([P, 2 * D], BF16, name="ring%d" % i, align_bytes=64)
             ring.append(ring_t)
+
+        scaled1 = const.tile([P, D], BF16, name="scaled1", align_bytes=64)
+        head_scaled = [ring[0][:, 0:D], scaled1[:], ring[1][:, 0:D], ring[1][:, D:2 * D]]
 
         def cast_split(t):
             cols = slice(t % 2 * D, (t % 2 + 1) * D)
@@ -182,14 +182,22 @@ def tile_dimenettripletbilinear_kernel(tc, m_kj_bytes, m_kj_scale, m_ji, sbf, w_
                 in0=mbytes[t][:, 0:D].bitcast(FP8).rearrange("p (w u e) -> p w u e", u=2, e=2), scalar1=one[:], scalar2=None, op0=MULT,
             )
 
-        def cast(t0, t1):
-            cols = slice(t0 % 2 * D, (t0 % 2 + t1 - t0) * D)
-            nc.scalar.copy(out=casts[t0 // 2][:, cols], in_=mbytes[t0][:, 0:(t1 - t0) * D].bitcast(FP8))
+        cast_done = [2 * D]
+
+        def cast(n):
+            c0 = cast_done[0]
+            t = c0 // D
+            c1 = min(c0 + n, load_end[t] * D)
+            nc.scalar.copy(out=widened[:, c0:c1], in_=mbytes[t][:, c0 - t * D:c1 - t * D].bitcast(FP8))
+            cast_done[0] = c1
+            if c1 < min(c0 + n, TILES * D):
+                cast(c0 + n - c1)
 
         def product_gpsimd(j):
+            assert cast_done[0] >= (j + 1) * 2 * D
             nc.gpsimd.tensor_tensor(
                 out=ring[(j + 1) % 3][:].rearrange("p (u a w e) -> p u a w e", u=2, a=2, e=2),
-                in0=casts[j][:].rearrange("p (a w u e) -> p u a w e", a=2, u=2, e=2),
+                in0=casts[j].rearrange("p (a w u e) -> p u a w e", a=2, u=2, e=2),
                 in1=scale_split[:].rearrange("p (u w e) -> p u w e", u=2, e=2).unsqueeze(2).to_broadcast([P, 2, 2, P, 2]), op=MULT,
             )
 
@@ -210,7 +218,7 @@ def tile_dimenettripletbilinear_kernel(tc, m_kj_bytes, m_kj_scale, m_ji, sbf, w_
                 ms_t = work.tile([P, 2 * P], U8, name="ms", bufs=2, align_bytes=64)
                 mcode[j] = (mc_t, ms_t)
             cols = slice(a0 * P, a1 * P)
-            nc.vector.quantize_mx(out=mcode[j][0][:, cols].bitcast(FP8X4), scales=mcode[j][1][:, cols], in_=ring[j % 3][:, a0 * D:a1 * D])
+            nc.vector.quantize_mx(out=mcode[j][0][:, cols].bitcast(FP8X4), scales=mcode[j][1][:, cols], in_=head_scaled[a0] if j == 0 else ring[j % 3][:])
 
         def stage1(j, a0, a1):
             y_t = bank()
@@ -267,8 +275,8 @@ def tile_dimenettripletbilinear_kernel(tc, m_kj_bytes, m_kj_scale, m_ji, sbf, w_
 
         def p_quant(c, g0, g1):
             if g0 == 0:
-                pc_t = work.tile([P, 4 * P], U32, name="pc", bufs=3, align_bytes=64)
-                ps_t = work.tile([P, 4 * P], U8, name="ps", bufs=3, align_bytes=64)
+                pc_t = work.tile([P, 4 * P], U32, name="pc", bufs=4, align_bytes=64)
+                ps_t = work.tile([P, 4 * P], U8, name="ps", bufs=4, align_bytes=64)
                 pcode[c] = (pc_t, ps_t)
             n = len(groups[c]) * P
             cols = slice(g0 * n, g1 * n)
@@ -347,13 +355,13 @@ def tile_dimenettripletbilinear_kernel(tc, m_kj_bytes, m_kj_scale, m_ji, sbf, w_
             b_t = bank()
             words = casts[t // 2][:, t % 2 * D:(t % 2 + 1) * D].bitcast(F32)
             for u in range(2):
-                half = words[:, u * P:(u + 1) * P] if t == 0 else words[:, u:256:2]
+                half = words[:, u * P:(u + 1) * P] if t < 2 else words[:, u:256:2]
                 nc.tensor.transpose(b_t[:, u * P:(u + 1) * P], half, ident[:])
             head[t] = b_t
 
         def head_product(t):
             nc.vector.tensor_tensor(
-                out=ring[t // 2][:, t % 2 * D:(t % 2 + 1) * D].rearrange("p (r u e) -> p r u e", u=2, e=2),
+                out=head_scaled[t].rearrange("p (r u e) -> p r u e", u=2, e=2),
                 in0=head[t][:, 0:256].bitcast(BF16).rearrange("p (u r e) -> p r u e", u=2, e=2),
                 in1=scale4[:].rearrange("p (u e) -> p u e", u=2).unsqueeze(1).to_broadcast([P, P, 2, 2]), op=MULT,
             )
@@ -366,104 +374,99 @@ def tile_dimenettripletbilinear_kernel(tc, m_kj_bytes, m_kj_scale, m_ji, sbf, w_
             o_t = const.tile([P, D], F32, name="o%d" % i, align_bytes=64)
             o_last.append(o_t)
 
-        warm_tensor()
-        cast_split(0)
-        head_transpose(0)
+        warm_tensor(3)
         scale_bank = scale_spread()
-        cast(1, 2)
+        cast_split(0)
+        cast_split(1)
+        head_transpose(0)
         head_transpose(1)
-        gain_spread()
-        wd_interleave()
-        cast(2, 4)
+        cast(1024)
         scale_copy_split(scale_bank)
-        cast(4, 6)
-        head_product(0)
-        wd_quantise()
-        m_quant(0, 0, 1)
-        stage1(0, 0, 1)
-        silu1(0, 0, 1)
-        cast(6, 8)
-        head_product(1)
-        wb_interleave_vector(0, 0, 0, 128)
-        m_quant(0, 1, 2)
-        product_gpsimd(2)
-        wb_interleave_vector(0, 0, 128, 256)
+        wd_interleave()
         head_transpose(2)
         head_transpose(3)
+        gain_spread()
+        cast(1024)
+        head_product(0)
+        head_product(1)
+        wd_quantise()
+        m_quant(0, 0, 1)
+        product_gpsimd(2)
+        m_quant(0, 1, 2)
+        cast(1024)
+        cast(512)
+        stage1(0, 0, 1)
+        silu1(0, 0, 1)
         stage1(0, 1, 2)
-        wb_interleave(1, 0)
-        cast(8, 9)
         silu1(0, 1, 2)
-        cast(10, 11)
-        cast(12, 13)
-        cast(14, 15)
-        p_ops(0, 0, 4)
+        cast(512)
         head_product(2)
         head_product(3)
-        p_ops(0, 4, 8)
-        wb_interleave(0, 1)
-        cast(16, 17)
-        wb_copy(nc.scalar.copy, 1, 0)
-        cast(18, 19)
-        cast(20, 21)
+        wb_interleave(0, 0)
+        wb_interleave(1, 0)
+        p_ops(0)
+        cast(1024)
+        wb_copy(nc.scalar.copy, 0, 0)
+        cast(1024)
         m_quant(1, 0, 2)
         product_gpsimd(3)
         stage1(1, 0, 2)
-        m_transpose(2)
-        wb_interleave(1, 1)
         p_transpose(0, 0, 2)
+        m_transpose(2)
         silu1(1, 0, 2)
-        wb_copy(nc.scalar.copy, 0, 1)
-        m_copy(2)
-        cast(22, 23)
-        wb_copy(nc.scalar.copy, 1, 1)
+        wb_copy(nc.scalar.copy, 1, 0)
+        wb_interleave(0, 1)
         p_copy(nc.scalar.copy, 0, 0, 2)
-        cast(9, 10)
+        m_copy(2)
+        wb_copy(nc.scalar.copy, 0, 1)
         p_ops(1)
         p_transpose(1, 0, 2)
         p_ops(2)
         wb_quantise(0, 0)
         wb_quantise(1, 0)
-        wb_quantise(0, 1)
-        wb_quantise(1, 1)
         m_quant(2, 0, 2)
         product_gpsimd(4)
         p_quant(0, 0, 2)
         p_copy(nc.scalar.copy, 1, 0, 2)
-        cast(24, 25)
+        cast(1024)
         m_transpose(3)
         p_transpose(2, 0, 2)
+        wb_interleave(1, 1, 0, 1)
         stage1(2, 0, 2)
+        stage2(0, 0, 2)
+        wb_interleave(1, 1, 1, 2)
         silu1(2, 0, 2)
-        cast(26, 27)
         p_copy(nc.scalar.copy, 2, 0, 2)
         m_copy(3)
-        cast(11, 12)
-        stage2(0, 0, 4)
-        agg_open(0)
-        silu2(0, 0, 512)
-        cast(28, 29)
-        cast(30, 31)
+        wb_copy(nc.scalar.copy, 1, 1)
+        cast(512)
+        silu2(0, 0, 256)
         p_ops(3)
         p_transpose(3, 0, 2)
+        agg_open(0)
         p_ops(4)
+        wb_quantise(0, 1)
+        wb_quantise(1, 1)
         m_quant(3, 0, 2)
         product_gpsimd(5)
         p_quant(1, 0, 2)
+        cast(768)
         p_copy(nc.scalar.copy, 3, 0, 2)
         m_transpose(4)
         p_transpose(4, 0, 2)
         stage1(3, 0, 2)
+        stage2(0, 2, 4)
         silu1(3, 0, 2)
         p_copy(nc.scalar.copy, 4, 0, 2)
         m_copy(4)
-        cast(13, 14)
         stage2(1, 0, 2)
         stage2(1, 2, 4)
+        silu2(0, 2, 256)
         silu2(1, 0, 512)
         silu2(1, 2, 512)
         p_ops(5)
-        k_sum(0, 0, 4)
+        k_sum(0, 0, 2)
+        k_sum(0, 2, 4)
         p_transpose(5, 0, 2)
         p_ops(6)
 
@@ -478,8 +481,8 @@ def tile_dimenettripletbilinear_kernel(tc, m_kj_bytes, m_kj_scale, m_ji, sbf, w_
             silu1(j, 0, 2)
             p_copy(nc.scalar.copy, 2 * j - 2, 0, 2)
             m_copy(j + 1)
-            if j + 3 < PAIRS:
-                cast(2 * j + 7, 2 * j + 8)
+            if cast_done[0] < TILES * D:
+                cast(768)
             stage2(j - 2, 0, 2)
             stage2(j - 2, 2, 4)
             silu2(j - 2, 0, 512)

@@ -66,13 +66,13 @@ def tile_dimenettripletbilinear_kernel(tc, m_kj_bytes, m_kj_scale, m_ji, sbf, w_
         nc.scalar.dma_start(out=gain8[:], in_=gain.rearrange("(g p j) -> p g j", g=2, j=4))
         load_bytes(4, 8)
         nc.scalar.dma_start(out=sbf_sb[:], in_=sbf.rearrange("(h e) k n -> e h (k n)", e=P))
-        load_bytes(8, 12)
         load_wb(0, 0, 2)
+        load_bytes(8, 12)
         load_wb(1, 0, 2)
         load_bytes(12, 16)
         load_bytes(16, 24)
-        load_bytes(24, 32)
         nc.sync.dma_start(out=mji[:], in_=m_ji.rearrange("(h e) d -> e h d", e=P))
+        load_bytes(24, 32)
 
         ident = const.tile([P, P], F32, name="ident", align_bytes=64)
         make_identity(nc, ident[:])
@@ -394,31 +394,33 @@ def tile_dimenettripletbilinear_kernel(tc, m_kj_bytes, m_kj_scale, m_ji, sbf, w_
         product_gpsimd(2)
         m_quant(0, 1, 2)
         cast(1024)
-        cast(512)
         stage1(0, 0, 1)
         silu1(0, 0, 1)
         stage1(0, 1, 2)
         silu1(0, 1, 2)
-        cast(512)
         head_product(2)
         head_product(3)
         wb_interleave(0, 0)
-        wb_interleave(1, 0)
+        wb_interleave(0, 1)
         p_ops(0)
+        cast(1024)
         cast(1024)
         wb_copy(nc.scalar.copy, 0, 0)
         cast(1024)
+        cast(1024)
+        wb_interleave_vector(1, 0, 0, 256)
         m_quant(1, 0, 2)
         product_gpsimd(3)
         stage1(1, 0, 2)
         p_transpose(0, 0, 2)
         m_transpose(2)
         silu1(1, 0, 2)
-        wb_copy(nc.scalar.copy, 1, 0)
-        wb_interleave(0, 1)
+        wb_copy(nc.scalar.copy, 0, 1)
+        wb_interleave(1, 1, 0, 1)
+        agg_open(0)
         p_copy(nc.scalar.copy, 0, 0, 2)
         m_copy(2)
-        wb_copy(nc.scalar.copy, 0, 1)
+        cast(1024)
         p_ops(1)
         p_transpose(1, 0, 2)
         p_ops(2)
@@ -431,7 +433,6 @@ def tile_dimenettripletbilinear_kernel(tc, m_kj_bytes, m_kj_scale, m_ji, sbf, w_
         cast(1024)
         m_transpose(3)
         p_transpose(2, 0, 2)
-        wb_interleave(1, 1, 0, 1)
         stage1(2, 0, 2)
         stage2(0, 0, 2)
         wb_interleave(1, 1, 1, 2)
@@ -439,18 +440,17 @@ def tile_dimenettripletbilinear_kernel(tc, m_kj_bytes, m_kj_scale, m_ji, sbf, w_
         p_copy(nc.scalar.copy, 2, 0, 2)
         m_copy(3)
         wb_copy(nc.scalar.copy, 1, 1)
-        cast(512)
         silu2(0, 0, 256)
+        cast(1024)
         p_ops(3)
         p_transpose(3, 0, 2)
-        agg_open(0)
+        agg_open(1)
         p_ops(4)
         wb_quantise(0, 1)
         wb_quantise(1, 1)
         m_quant(3, 0, 2)
         product_gpsimd(5)
         p_quant(1, 0, 2)
-        cast(768)
         p_copy(nc.scalar.copy, 3, 0, 2)
         m_transpose(4)
         p_transpose(4, 0, 2)
@@ -462,6 +462,7 @@ def tile_dimenettripletbilinear_kernel(tc, m_kj_bytes, m_kj_scale, m_ji, sbf, w_
         stage2(1, 0, 2)
         stage2(1, 2, 4)
         silu2(0, 2, 256)
+        cast(512)
         silu2(1, 0, 512)
         silu2(1, 2, 512)
         p_ops(5)
@@ -482,13 +483,11 @@ def tile_dimenettripletbilinear_kernel(tc, m_kj_bytes, m_kj_scale, m_ji, sbf, w_
             p_copy(nc.scalar.copy, 2 * j - 2, 0, 2)
             m_copy(j + 1)
             if cast_done[0] < TILES * D:
-                cast(768)
+                cast(512)
             stage2(j - 2, 0, 2)
             stage2(j - 2, 2, 4)
             silu2(j - 2, 0, 512)
             silu2(j - 2, 2, 512)
-            if j == 9:
-                agg_open(1)
             p_ops(2 * j - 1)
             k_sum(j - 3, 0, 2)
             k_sum(j - 3, 2, 4)

@@ -61,11 +61,11 @@ def tile_dimenettripletbilinear_kernel(tc, m_kj_bytes, m_kj_scale, m_ji, sbf, w_
         mji = const.tile([P, 2, D], BF16, name="mji", align_bytes=64)
         load_bytes(0, 2)
         nc.scalar.dma_start(out=scale4[:], in_=m_kj_scale.rearrange("a b (p j) -> p (a b j)", j=4))
+        nc.sync.dma_start(out=wd_raw[:], in_=w_down.rearrange("(p j) c -> p j c", j=4))
         load_bytes(2, 4)
-        nc.scalar.dma_start(out=wd_raw[:], in_=w_down.rearrange("(p j) c -> p j c", j=4))
-        nc.scalar.dma_start(out=gain8[:], in_=gain.rearrange("(g p j) -> p g j", g=2, j=4))
+        nc.sync.dma_start(out=gain8[:], in_=gain.rearrange("(g p j) -> p g j", g=2, j=4))
         load_bytes(4, 8)
-        nc.scalar.dma_start(out=sbf_sb[:], in_=sbf.rearrange("(h e) k n -> e h (k n)", e=P))
+        nc.sync.dma_start(out=sbf_sb[:], in_=sbf.rearrange("(h e) k n -> e h (k n)", e=P))
         load_wb(0, 0, 2)
         load_bytes(8, 12)
         load_wb(1, 0, 2)
@@ -114,19 +114,23 @@ def tile_dimenettripletbilinear_kernel(tc, m_kj_bytes, m_kj_scale, m_ji, sbf, w_
             for j in range(4):
                 nc.tensor.transpose(gain_ps[:, j * P:(j + 1) * P], words[:, j:j + 1].to_broadcast([P, P]), ident[:])
 
-        wd_grp = const.tile([P, C, 4], BF16, name="wd_grp", align_bytes=64)
+        ring = []
+        for i in range(3):
+            ring_t = const.tile([P, 2 * D], BF16, name="ring%d" % i, align_bytes=64)
+            ring.append(ring_t)
+        wd_grp = ring[0][:, 0:D].rearrange("p (c j) -> p c j", j=4)
         wd_codes = const.tile([P, C], U32, name="wd_codes", align_bytes=64)
         wd_sc = const.tile([P, C], U8, name="wd_sc", align_bytes=64)
 
         def wd_interleave():
             for u in range(2):
                 nc.vector.tensor_copy(
-                    out=wd_grp[:].rearrange("p (u i e) j -> p u i e j", u=2, e=2)[:, u],
+                    out=wd_grp.rearrange("p (u i e) j -> p u i e j", u=2, e=2)[:, u],
                     in_=wd_raw[:].rearrange("p j (i u e) -> p u i e j", u=2, e=2)[:, u],
                 )
 
         def wd_quantise():
-            nc.vector.quantize_mx(out=wd_codes[:].bitcast(FP8X4), scales=wd_sc[:], in_=wd_grp[:].rearrange("p c j -> p (c j)"))
+            nc.vector.quantize_mx(out=wd_codes[:].bitcast(FP8X4), scales=wd_sc[:], in_=ring[0][:, 0:D])
 
         wb_ps, wb_grp, wb_codes, wb_sc = {}, {}, [], []
         for g in range(2):
@@ -167,13 +171,8 @@ def tile_dimenettripletbilinear_kernel(tc, m_kj_bytes, m_kj_scale, m_ji, sbf, w_
         mtr, mcode, yps, xs, pts, ptr, pqs, pcode, mm, tts, aggs, head = ({} for a in range(12))
         widened = const.tile([P, TILES * D], BF16, name="widened", align_bytes=64)
         casts = [widened[:, j * 2 * D:(j + 1) * 2 * D] for j in range(PAIRS)]
-        ring = []
-        for i in range(3):
-            ring_t = const.tile([P, 2 * D], BF16, name="ring%d" % i, align_bytes=64)
-            ring.append(ring_t)
-
-        scaled1 = const.tile([P, D], BF16, name="scaled1", align_bytes=64)
-        head_scaled = [ring[0][:, 0:D], scaled1[:], ring[1][:, 0:D], ring[1][:, D:2 * D]]
+        scaled01 = const.tile([P, 2 * D], BF16, name="scaled01", align_bytes=64)
+        head_scaled = [scaled01[:, 0:D], scaled01[:, D:2 * D], ring[1][:, 0:D], ring[1][:, D:2 * D]]
 
         def cast_split(t):
             cols = slice(t % 2 * D, (t % 2 + 1) * D)
@@ -390,8 +389,8 @@ def tile_dimenettripletbilinear_kernel(tc, m_kj_bytes, m_kj_scale, m_ji, sbf, w_
         head_product(0)
         head_product(1)
         wd_quantise()
-        m_quant(0, 0, 1)
         product_gpsimd(2)
+        m_quant(0, 0, 1)
         m_quant(0, 1, 2)
         cast(1024)
         stage1(0, 0, 1)
@@ -401,21 +400,22 @@ def tile_dimenettripletbilinear_kernel(tc, m_kj_bytes, m_kj_scale, m_ji, sbf, w_
         head_product(2)
         head_product(3)
         wb_interleave(0, 0)
-        wb_interleave(0, 1)
+        wb_interleave(1, 0)
         p_ops(0)
         cast(1024)
         cast(1024)
         wb_copy(nc.scalar.copy, 0, 0)
         cast(1024)
         cast(1024)
-        wb_interleave_vector(1, 0, 0, 256)
+        wb_interleave_vector(0, 1, 0, 64)
         m_quant(1, 0, 2)
         product_gpsimd(3)
+        wb_interleave_vector(0, 1, 64, 256)
         stage1(1, 0, 2)
         p_transpose(0, 0, 2)
         m_transpose(2)
         silu1(1, 0, 2)
-        wb_copy(nc.scalar.copy, 0, 1)
+        wb_copy(nc.scalar.copy, 1, 0)
         wb_interleave(1, 1, 0, 1)
         agg_open(0)
         p_copy(nc.scalar.copy, 0, 0, 2)
@@ -425,9 +425,9 @@ def tile_dimenettripletbilinear_kernel(tc, m_kj_bytes, m_kj_scale, m_ji, sbf, w_
         p_transpose(1, 0, 2)
         p_ops(2)
         wb_quantise(0, 0)
-        wb_quantise(1, 0)
         m_quant(2, 0, 2)
         product_gpsimd(4)
+        wb_quantise(1, 0)
         p_quant(0, 0, 2)
         p_copy(nc.scalar.copy, 1, 0, 2)
         cast(1024)
@@ -457,11 +457,11 @@ def tile_dimenettripletbilinear_kernel(tc, m_kj_bytes, m_kj_scale, m_ji, sbf, w_
         stage1(3, 0, 2)
         stage2(0, 2, 4)
         silu1(3, 0, 2)
+        silu2(0, 2, 256)
         p_copy(nc.scalar.copy, 4, 0, 2)
         m_copy(4)
         stage2(1, 0, 2)
         stage2(1, 2, 4)
-        silu2(0, 2, 256)
         cast(512)
         silu2(1, 0, 512)
         silu2(1, 2, 512)

@@ -61,10 +61,10 @@ def tile_dimenettripletbilinear_kernel(tc, m_kj_bytes, m_kj_scale, m_ji, sbf, w_
         mji = const.tile([P, 2, D], BF16, name="mji", align_bytes=64)
         load_bytes(0, 2)
         nc.scalar.dma_start(out=scale4[:], in_=m_kj_scale.rearrange("a b (p j) -> p (a b j)", j=4))
-        nc.sync.dma_start(out=wd_raw[:], in_=w_down.rearrange("(p j) c -> p j c", j=4))
         load_bytes(2, 4)
-        nc.sync.dma_start(out=gain8[:], in_=gain.rearrange("(g p j) -> p g j", g=2, j=4))
+        nc.sync.dma_start(out=wd_raw[:], in_=w_down.rearrange("(p j) c -> p j c", j=4))
         load_bytes(4, 8)
+        nc.sync.dma_start(out=gain8[:], in_=gain.rearrange("(g p j) -> p g j", g=2, j=4))
         nc.sync.dma_start(out=sbf_sb[:], in_=sbf.rearrange("(h e) k n -> e h (k n)", e=P))
         load_wb(0, 0, 2)
         load_bytes(8, 12)
@@ -171,8 +171,8 @@ def tile_dimenettripletbilinear_kernel(tc, m_kj_bytes, m_kj_scale, m_ji, sbf, w_
         mtr, mcode, yps, xs, pts, ptr, pqs, pcode, mm, tts, aggs, head = ({} for a in range(12))
         widened = const.tile([P, TILES * D], BF16, name="widened", align_bytes=64)
         casts = [widened[:, j * 2 * D:(j + 1) * 2 * D] for j in range(PAIRS)]
-        scaled01 = const.tile([P, 2 * D], BF16, name="scaled01", align_bytes=64)
-        head_scaled = [scaled01[:, 0:D], scaled01[:, D:2 * D], ring[1][:, 0:D], ring[1][:, D:2 * D]]
+        scaled01 = const.tile([P, 3 * D], BF16, name="scaled01", align_bytes=64)
+        head_scaled = [scaled01[:, 0:D], scaled01[:, D:2 * D], ring[1][:, 0:D], scaled01[:, 2 * D:3 * D]]
 
         def cast_split(t):
             cols = slice(t % 2 * D, (t % 2 + 1) * D)
@@ -217,7 +217,7 @@ def tile_dimenettripletbilinear_kernel(tc, m_kj_bytes, m_kj_scale, m_ji, sbf, w_
                 ms_t = work.tile([P, 2 * P], U8, name="ms", bufs=2, align_bytes=64)
                 mcode[j] = (mc_t, ms_t)
             cols = slice(a0 * P, a1 * P)
-            nc.vector.quantize_mx(out=mcode[j][0][:, cols].bitcast(FP8X4), scales=mcode[j][1][:, cols], in_=head_scaled[a0] if j == 0 else ring[j % 3][:])
+            nc.vector.quantize_mx(out=mcode[j][0][:, cols].bitcast(FP8X4), scales=mcode[j][1][:, cols], in_=head_scaled[2 * j + a0] if j < 2 else ring[j % 3][:])
 
         def stage1(j, a0, a1):
             y_t = bank()
@@ -406,21 +406,20 @@ def tile_dimenettripletbilinear_kernel(tc, m_kj_bytes, m_kj_scale, m_ji, sbf, w_
         cast(1024)
         wb_copy(nc.scalar.copy, 0, 0)
         cast(1024)
-        cast(1024)
-        wb_interleave_vector(0, 1, 0, 64)
-        m_quant(1, 0, 2)
+        cast(512)
+        m_quant(1, 0, 1)
         product_gpsimd(3)
-        wb_interleave_vector(0, 1, 64, 256)
+        m_quant(1, 1, 2)
         stage1(1, 0, 2)
         p_transpose(0, 0, 2)
         m_transpose(2)
         silu1(1, 0, 2)
         wb_copy(nc.scalar.copy, 1, 0)
-        wb_interleave(1, 1, 0, 1)
-        agg_open(0)
+        wb_interleave(0, 1)
         p_copy(nc.scalar.copy, 0, 0, 2)
         m_copy(2)
-        cast(1024)
+        cast(512)
+        wb_copy(nc.scalar.copy, 0, 1)
         p_ops(1)
         p_transpose(1, 0, 2)
         p_ops(2)
@@ -430,12 +429,12 @@ def tile_dimenettripletbilinear_kernel(tc, m_kj_bytes, m_kj_scale, m_ji, sbf, w_
         wb_quantise(1, 0)
         p_quant(0, 0, 2)
         p_copy(nc.scalar.copy, 1, 0, 2)
-        cast(1024)
+        cast(512)
         m_transpose(3)
         p_transpose(2, 0, 2)
         stage1(2, 0, 2)
         stage2(0, 0, 2)
-        wb_interleave(1, 1, 1, 2)
+        wb_interleave(1, 1)
         silu1(2, 0, 2)
         p_copy(nc.scalar.copy, 2, 0, 2)
         m_copy(3)
@@ -444,7 +443,7 @@ def tile_dimenettripletbilinear_kernel(tc, m_kj_bytes, m_kj_scale, m_ji, sbf, w_
         cast(1024)
         p_ops(3)
         p_transpose(3, 0, 2)
-        agg_open(1)
+        agg_open(0)
         p_ops(4)
         wb_quantise(0, 1)
         wb_quantise(1, 1)
@@ -452,6 +451,7 @@ def tile_dimenettripletbilinear_kernel(tc, m_kj_bytes, m_kj_scale, m_ji, sbf, w_
         product_gpsimd(5)
         p_quant(1, 0, 2)
         p_copy(nc.scalar.copy, 3, 0, 2)
+        cast(448)
         m_transpose(4)
         p_transpose(4, 0, 2)
         stage1(3, 0, 2)
@@ -462,7 +462,7 @@ def tile_dimenettripletbilinear_kernel(tc, m_kj_bytes, m_kj_scale, m_ji, sbf, w_
         m_copy(4)
         stage2(1, 0, 2)
         stage2(1, 2, 4)
-        cast(512)
+        cast(1024)
         silu2(1, 0, 512)
         silu2(1, 2, 512)
         p_ops(5)
@@ -483,11 +483,13 @@ def tile_dimenettripletbilinear_kernel(tc, m_kj_bytes, m_kj_scale, m_ji, sbf, w_
             p_copy(nc.scalar.copy, 2 * j - 2, 0, 2)
             m_copy(j + 1)
             if cast_done[0] < TILES * D:
-                cast(512)
+                cast(576)
             stage2(j - 2, 0, 2)
             stage2(j - 2, 2, 4)
             silu2(j - 2, 0, 512)
             silu2(j - 2, 2, 512)
+            if j == 9:
+                agg_open(1)
             p_ops(2 * j - 1)
             k_sum(j - 3, 0, 2)
             k_sum(j - 3, 2, 4)

@@ -304,12 +304,13 @@ def tile_dimenettripletbilinear_kernel(tc, m_kj_bytes, m_kj_scale, m_ji, sbf, w_
                 rhs=wb_codes[g][:, cols].bitcast(FP8X4), rhs_scale=wb_sc[g][:, cols], start=(g == 0), stop=(g == 1),
             )
 
-        def silu2(c, d0, width, first=0):
-            if first == 0:
-                t_t = work.tile([P, 4 * P], F32, name="tt", bufs=8, align_bytes=64)
-                tts[c, d0] = t_t
-                free.append(mm[c, d0])
-            nc.scalar.activation(out=tts[c, d0][:, first:width], in_=mm[c, d0][:, first:width], func=SILU)
+        def silu2(c, d0, width):
+            if d0 == 0:
+                t_t = work.tile([P, 8 * P], F32, name="tt", bufs=4, align_bytes=64)
+                tts[c] = t_t
+            tts[c, d0] = tts[c][:, d0 * 2 * P:(d0 + 2) * 2 * P]
+            free.append(mm[c, d0])
+            nc.scalar.activation(out=tts[c, d0][:, 0:width], in_=mm[c, d0][:, 0:width], func=SILU)
 
         def agg_open(h):
             agg_t = bank()
@@ -328,6 +329,18 @@ def tile_dimenettripletbilinear_kernel(tc, m_kj_bytes, m_kj_scale, m_ji, sbf, w_
                         is_transpose=True, start=False, stop=(t in last_summed and d == 3),
                     )
 
+        pre = {}
+
+        def pair_add(c, dst):
+            both = tts[c][:].rearrange("p (d a e) -> p d a e", d=4, a=2)
+            nc.gpsimd.tensor_tensor(out=dst.rearrange("p (d e) -> p d e", d=4), in0=both[:, :, 0], in1=both[:, :, 1], op=ADD)
+            pre[c] = dst
+
+        def k_sum_added(c):
+            for d in range(4):
+                cols = slice(d * P, (d + 1) * P)
+                nc.tensor.matmul(out=aggs[1][:, cols], lhsT=pre[c][:, cols], rhs=ident[:], is_transpose=True, start=False, stop=False)
+
         sums = []
         for h in range(2):
             sum_t = const.tile([P, D], F32, name="sum%d" % h, align_bytes=64)
@@ -344,7 +357,7 @@ def tile_dimenettripletbilinear_kernel(tc, m_kj_bytes, m_kj_scale, m_ji, sbf, w_
             nc.vector.scalar_tensor_tensor(out=dst[:, cols], in0=tts[c, first][:, (d0 - first) * P:(d1 - first) * P], scalar=0.25, in1=src[:, cols], op0=MULT, op1=ADD)
 
         def scale_turned(dst, c):
-            nc.vector.tensor_scalar(out=dst[:], in0=tts[c, 0][:], scalar1=0.25, scalar2=None, op0=MULT)
+            nc.vector.tensor_scalar(out=dst[:], in0=tts[c, 0], scalar1=0.25, scalar2=None, op0=MULT)
 
         def add_sum(dst, h, d0, d1, src):
             cols = slice(d0 * P, d1 * P)
@@ -508,31 +521,32 @@ def tile_dimenettripletbilinear_kernel(tc, m_kj_bytes, m_kj_scale, m_ji, sbf, w_
         stage2(12, 0, 2)
         stage2(12, 2, 4)
         silu2(12, 0, 512)
+        pair_add(11, ring[2][:].bitcast(F32))
         p_ops(27)
         p_quant(13, 0, 2)
         m_quant(15, 0, 2)
-        k_sum(11, 0, 2)
         p_transpose(27, 0, 2)
         silu2(12, 2, 512)
+        pair_add(12, ring[0][:].bitcast(F32))
         p_copy(nc.scalar.copy, 27, 0, 2)
         p_ops(28)
         stage2(13, 0, 2)
         stage1(15, 0, 2)
         stage2(13, 2, 4)
         silu2(13, 0, 512)
+        silu1(15, 0, 2)
         p_transpose(28, 0, 1)
         p_transpose(28, 1, 2)
         p_copy(nc.scalar.copy, 28, 0, 1)
         p_copy(nc.scalar.copy, 28, 1, 2)
-        silu1(15, 0, 2)
         silu2(13, 2, 512)
-        k_sum(11, 2, 4)
-        k_sum(12, 0, 2)
-        k_sum(12, 2, 4)
+        k_sum_added(11)
+        k_sum(13, 0, 2)
+        k_sum_added(12)
         p_ops(29)
         p_quant(14, 0, 2)
         p_transpose(29, 0, 2)
-        k_sum(13, 0, 2)
+        k_sum(13, 2, 4)
         p_copy(nc.scalar.copy, 29, 0, 2)
         stage2(14, 0, 2)
         stage2(14, 2, 4)
@@ -540,7 +554,6 @@ def tile_dimenettripletbilinear_kernel(tc, m_kj_bytes, m_kj_scale, m_ji, sbf, w_
         p_ops(30)
         p_quant(15, 0, 2)
         p_transpose(30, 0, 2)
-        k_sum(13, 2, 4)
         silu2(14, 2, 512)
         p_copy(nc.scalar.copy, 30, 0, 2)
         stage2_turned(15, 0, 4, 0)

@@ -212,7 +212,7 @@ def tile_dimenettripletbilinear_kernel(tc, m_kj_bytes, m_kj_scale, m_ji, sbf, w_
             free.append(mtr[j])
 
         def m_quant(j, a0, a1):
-            if a0 == 0:
+            if j not in mcode:
                 mc_t = work.tile([P, 2 * P], U32, name="mc", bufs=2, align_bytes=64)
                 ms_t = work.tile([P, 2 * P], U8, name="ms", bufs=2, align_bytes=64)
                 mcode[j] = (mc_t, ms_t)
@@ -446,8 +446,8 @@ def tile_dimenettripletbilinear_kernel(tc, m_kj_bytes, m_kj_scale, m_ji, sbf, w_
         m_transpose(3)
         p_transpose(2, 0, 2)
         stage1(2, 0, 2)
-        stage2(0, 0, 2)
         wb_interleave(1, 1)
+        stage2(0, 0, 2)
         silu1(2, 0, 2)
         p_copy(nc.scalar.copy, 2, 0, 2)
         m_copy(3)

@@ -308,7 +308,8 @@ def tile_dimenettripletbilinear_kernel(tc, m_kj_bytes, m_kj_scale, m_ji, sbf, w_
             if d0 == 0:
                 t_t = work.tile([P, 8 * P], F32, name="tt", bufs=4, align_bytes=64)
                 tts[c] = t_t
-            tts[c, d0] = tts[c][:, d0 * 2 * P:(d0 + 2) * 2 * P]
+            first = d0 * len(groups[c]) * P
+            tts[c, d0] = tts[c][:, first:first + width]
             free.append(mm[c, d0])
             nc.scalar.activation(out=tts[c, d0][:, 0:width], in_=mm[c, d0][:, 0:width], func=SILU)
 
@@ -356,8 +357,8 @@ def tile_dimenettripletbilinear_kernel(tc, m_kj_bytes, m_kj_scale, m_ji, sbf, w_
             cols = slice(d0 * P, d1 * P)
             nc.vector.scalar_tensor_tensor(out=dst[:, cols], in0=tts[c, first][:, (d0 - first) * P:(d1 - first) * P], scalar=0.25, in1=src[:, cols], op0=MULT, op1=ADD)
 
-        def scale_turned(dst, c):
-            nc.vector.tensor_scalar(out=dst[:], in0=tts[c, 0], scalar1=0.25, scalar2=None, op0=MULT)
+        def scale_turned(dst, c, d0, d1):
+            nc.scalar.activation(out=dst[:, d0 * P:d1 * P], in_=tts[c, d0], func=COPY, scale=0.25)
 
         def add_sum(dst, h, d0, d1, src):
             cols = slice(d0 * P, d1 * P)
@@ -548,6 +549,8 @@ def tile_dimenettripletbilinear_kernel(tc, m_kj_bytes, m_kj_scale, m_ji, sbf, w_
         p_transpose(29, 0, 2)
         k_sum(13, 2, 4)
         p_copy(nc.scalar.copy, 29, 0, 2)
+        agg_close(0, 0, 4)
+        nc.sync.dma_start(out=out[0:P, :], in_=sums[0][:])
         stage2(14, 0, 2)
         stage2(14, 2, 4)
         silu2(14, 0, 512)
@@ -556,15 +559,20 @@ def tile_dimenettripletbilinear_kernel(tc, m_kj_bytes, m_kj_scale, m_ji, sbf, w_
         p_transpose(30, 0, 2)
         silu2(14, 2, 512)
         p_copy(nc.scalar.copy, 30, 0, 2)
-        stage2_turned(15, 0, 4, 0)
-        stage2_turned(15, 0, 4, 1)
+        stage2_turned(15, 0, 2, 0)
+        stage2_turned(15, 0, 2, 1)
+        stage2_turned(15, 2, 4, 0)
+        stage2_turned(15, 2, 4, 1)
         p_ops(31)
         p_quant(16, 0, 2)
         p_transpose(31, 0, 1)
-        p_transpose(31, 1, 2)
         k_sum(14, 0, 2)
+        p_transpose(31, 1, 2)
         k_sum(14, 2, 4)
-        silu2(15, 0, 512)
+        silu2(15, 0, 256)
+        silu2(15, 2, 256)
+        scale_turned(sums[1], 15, 0, 2)
+        scale_turned(sums[1], 15, 2, 4)
         p_copy(nc.vector.tensor_copy, 31, 0, 1)
         p_copy(nc.vector.tensor_copy, 31, 1, 2)
         stage2_turned(16, 0, 2, 0)
@@ -572,23 +580,30 @@ def tile_dimenettripletbilinear_kernel(tc, m_kj_bytes, m_kj_scale, m_ji, sbf, w_
         stage2_turned(16, 2, 4, 0)
         stage2_turned(16, 2, 4, 1)
         p_quant(17, 0, 1)
-        scale_turned(sums[1], 15)
         p_quant(17, 1, 2)
-        agg_close(0, 0, 4)
-        nc.sync.dma_start(out=out[0:P, :], in_=sums[0][:])
         silu2(16, 0, 256)
         silu2(16, 2, 256)
-        stage2_turned(17, 0, 2, 0)
-        stage2_turned(17, 2, 4, 0)
-        stage2_turned(17, 0, 2, 1)
-        stage2_turned(17, 2, 4, 1)
+        stage2_turned(17, 0, 1, 0)
+        stage2_turned(17, 1, 2, 0)
+        stage2_turned(17, 2, 3, 0)
+        stage2_turned(17, 3, 4, 0)
+        stage2_turned(17, 0, 1, 1)
+        stage2_turned(17, 1, 2, 1)
+        stage2_turned(17, 2, 3, 1)
+        stage2_turned(17, 3, 4, 1)
         add_sum(with29, 1, 0, 2, sums[1])
         add_sum(with29, 1, 2, 4, sums[1])
         add_turned(with30, 16, 0, 0, 2, with29)
         add_turned(with30, 16, 2, 2, 4, with29)
-        silu2(17, 0, 256)
-        add_turned(o_last[0], 17, 0, 0, 2, with30)
-        nc.sync.dma_start(out=out[P:2 * P, 0 * P:2 * P], in_=o_last[0][:, 0 * P:2 * P])
-        silu2(17, 2, 256)
-        add_turned(o_last[1], 17, 2, 2, 4, with30)
-        nc.sync.dma_start(out=out[P:2 * P, 2 * P:4 * P], in_=o_last[1][:, 2 * P:4 * P])
+        silu2(17, 0, 128)
+        add_turned(o_last[0], 17, 0, 0, 1, with30)
+        nc.sync.dma_start(out=out[P:2 * P, 0 * P:1 * P], in_=o_last[0][:, 0 * P:1 * P])
+        silu2(17, 1, 128)
+        add_turned(o_last[1], 17, 1, 1, 2, with30)
+        nc.sync.dma_start(out=out[P:2 * P, 1 * P:2 * P], in_=o_last[1][:, 1 * P:2 * P])
+        silu2(17, 2, 128)
+        add_turned(o_last[0], 17, 2, 2, 3, with30)
+        nc.sync.dma_start(out=out[P:2 * P, 2 * P:3 * P], in_=o_last[0][:, 2 * P:3 * P])
+        silu2(17, 3, 128)
+        add_turned(o_last[1], 17, 3, 3, 4, with30)
+        nc.sync.dma_start(out=out[P:2 * P, 3 * P:4 * P], in_=o_last[1][:, 3 * P:4 * P])

@@ -76,8 +76,6 @@ def tile_dimenettripletbilinear_kernel(tc, m_kj_bytes, m_kj_scale, m_ji, sbf, w_
 
         ident = const.tile([P, P], F32, name="ident", align_bytes=64)
         make_identity(nc, ident[:])
-        zeros = const.tile([P, P], BF16, name="zeros", align_bytes=64)
-        nc.vector.memset(zeros[:], 0.0)
         one = const.tile([P, 1], F32, name="one")
         nc.vector.memset(one[:], 1.0)
         warm = const.tile([P, 1], F32, name="warm")
@@ -163,10 +161,6 @@ def tile_dimenettripletbilinear_kernel(tc, m_kj_bytes, m_kj_scale, m_ji, sbf, w_
                 grp_t = const.tile([P, NBC], BF16, name="wb_grp%d%d" % (g, b), align_bytes=64)
                 wb_grp[g, b] = grp_t
             nc.vector.tensor_copy(out=wb_grp[g, b][:].rearrange("p (d j) -> p d j", j=4)[:, d0:d1], in_=wb_raw[g, b].rearrange("p j d -> p d j")[:, d0:d1])
-
-        def warm_tensor(n):
-            for i in range(n):
-                nc.tensor.matmul(out=free[-1][:].rearrange("p (r c) -> p r c", r=4), lhsT=zeros[:], rhs=zeros[:].unsqueeze(1).to_broadcast([P, 4, P]), start=True, stop=True)
 
         mtr, mcode, yps, xs, pts, ptr, pqs, pcode, mm, tts, aggs, head = ({} for a in range(12))
         widened = const.tile([P, TILES * D], BF16, name="widened", align_bytes=64)
@@ -387,7 +381,6 @@ def tile_dimenettripletbilinear_kernel(tc, m_kj_bytes, m_kj_scale, m_ji, sbf, w_
             o_t = const.tile([P, D], F32, name="o%d" % i, align_bytes=64)
             o_last.append(o_t)
 
-        warm_tensor(3)
         scale_bank = scale_spread()
         cast_split(0)
         cast_split(1)

@@ -56,7 +56,7 @@ def tile_dimenettripletbilinear_kernel(tc, m_kj_bytes, m_kj_scale, m_ji, sbf, w_
 
         scale4 = const.tile([P, 4], F32, name="scale4", align_bytes=64)
         wd_raw = const.tile([P, 4, C], BF16, name="wd_raw", align_bytes=64)
-        gain8 = const.tile([P, 2, 4], BF16, name="gain8", align_bytes=64)
+        gain8 = const.tile([P, 8], BF16, name="gain8", align_bytes=64)
         sbf_sb = const.tile([P, 2, K * NB], BF16, name="sbf_sb", align_bytes=64)
         mji = const.tile([P, 2, D], BF16, name="mji", align_bytes=64)
         load_bytes(0, 2)
@@ -64,7 +64,7 @@ def tile_dimenettripletbilinear_kernel(tc, m_kj_bytes, m_kj_scale, m_ji, sbf, w_
         load_bytes(2, 4)
         nc.sync.dma_start(out=wd_raw[:], in_=w_down.rearrange("(p j) c -> p j c", j=4))
         load_bytes(4, 8)
-        nc.sync.dma_start(out=gain8[:], in_=gain.rearrange("(g p j) -> p g j", g=2, j=4))
+        nc.sync.dma_start(out=gain8[:], in_=gain.rearrange("(p j) -> p j", j=8))
         nc.sync.dma_start(out=sbf_sb[:], in_=sbf.rearrange("(h e) k n -> e h (k n)", e=P))
         load_wb(0, 0, 2)
         load_bytes(8, 12)
@@ -108,9 +108,10 @@ def tile_dimenettripletbilinear_kernel(tc, m_kj_bytes, m_kj_scale, m_ji, sbf, w_
         gain_ps = psum.tile([P, 512], F32, name="gain_ps")
 
         def gain_spread():
-            words = gain8[:].rearrange("p g j -> p (g j)").bitcast(F32)
+            words = gain8[:].bitcast(F32)
+            spread = gain_ps[:].rearrange("q (g u i o) -> q o u g i", g=2, u=2, o=2)
             for j in range(4):
-                nc.tensor.transpose(gain_ps[:, j * P:(j + 1) * P], words[:, j:j + 1].to_broadcast([P, P]), ident[:])
+                nc.tensor.transpose(spread[:, j // 2, j % 2], words[:, j:j + 1].to_broadcast([P, P]), ident[:])
 
         ring = []
         for i in range(3):
@@ -407,7 +408,7 @@ def tile_dimenettripletbilinear_kernel(tc, m_kj_bytes, m_kj_scale, m_ji, sbf, w_
         head_product(2)
         head_product(3)
         wb_interleave(0, 0)
-        wb_interleave(1, 0)
+        wb_interleave(0, 1)
         p_ops(0)
         cast(1024)
         cast(1024)
@@ -421,19 +422,19 @@ def tile_dimenettripletbilinear_kernel(tc, m_kj_bytes, m_kj_scale, m_ji, sbf, w_
         p_transpose(0, 0, 2)
         m_transpose(2)
         silu1(1, 0, 2)
-        wb_copy(nc.scalar.copy, 1, 0)
-        wb_interleave(0, 1)
+        wb_copy(nc.scalar.copy, 0, 1)
+        wb_interleave(1, 0)
         p_copy(nc.scalar.copy, 0, 0, 2)
         m_copy(2)
         cast(512)
-        wb_copy(nc.scalar.copy, 0, 1)
+        wb_copy(nc.scalar.copy, 1, 0)
         p_ops(1)
         p_transpose(1, 0, 2)
         p_ops(2)
         wb_quantise(0, 0)
         m_quant(2, 0, 2)
         product_gpsimd(4)
-        wb_quantise(1, 0)
+        wb_quantise(0, 1)
         p_quant(0, 0, 2)
         p_copy(nc.scalar.copy, 1, 0, 2)
         cast(512)
@@ -441,40 +442,37 @@ def tile_dimenettripletbilinear_kernel(tc, m_kj_bytes, m_kj_scale, m_ji, sbf, w_
         p_transpose(2, 0, 2)
         stage1(2, 0, 2)
         wb_interleave(1, 1)
-        stage2(0, 0, 2)
         silu1(2, 0, 2)
         p_copy(nc.scalar.copy, 2, 0, 2)
         m_copy(3)
         wb_copy(nc.scalar.copy, 1, 1)
-        silu2(0, 0, 256)
         cast(1024)
         p_ops(3)
         p_transpose(3, 0, 2)
         agg_open(0)
         p_ops(4)
-        wb_quantise(0, 1)
+        wb_quantise(1, 0)
         wb_quantise(1, 1)
         m_quant(3, 0, 2)
         product_gpsimd(5)
         p_quant(1, 0, 2)
         p_copy(nc.scalar.copy, 3, 0, 2)
-        cast(448)
+        cast(704)
         m_transpose(4)
         p_transpose(4, 0, 2)
         stage1(3, 0, 2)
-        stage2(0, 2, 4)
+        stage2(0, 0, 4)
         silu1(3, 0, 2)
-        silu2(0, 2, 256)
         p_copy(nc.scalar.copy, 4, 0, 2)
         m_copy(4)
+        silu2(0, 0, 512)
         stage2(1, 0, 2)
         stage2(1, 2, 4)
-        cast(1024)
+        cast(768)
         silu2(1, 0, 512)
         silu2(1, 2, 512)
         p_ops(5)
-        k_sum(0, 0, 2)
-        k_sum(0, 2, 4)
+        k_sum(0, 0, 4)
         p_transpose(5, 0, 2)
         p_ops(6)
 
@@ -549,15 +547,18 @@ def tile_dimenettripletbilinear_kernel(tc, m_kj_bytes, m_kj_scale, m_ji, sbf, w_
         silu2(14, 0, 512)
         p_ops(30)
         p_quant(15, 0, 2)
-        p_transpose(30, 0, 2)
+        p_transpose(30, 0, 1)
+        p_transpose(30, 1, 2)
         silu2(14, 2, 512)
-        p_copy(nc.scalar.copy, 30, 0, 2)
+        p_copy(nc.scalar.copy, 30, 0, 1)
+        p_copy(nc.scalar.copy, 30, 1, 2)
         stage2_turned(15, 0, 2, 0)
         stage2_turned(15, 0, 2, 1)
         stage2_turned(15, 2, 4, 0)
         stage2_turned(15, 2, 4, 1)
         p_ops(31)
-        p_quant(16, 0, 2)
+        p_quant(16, 0, 1)
+        p_quant(16, 1, 2)
         p_transpose(31, 0, 1)
         k_sum(14, 0, 2)
         p_transpose(31, 1, 2)

from contextlib import ExitStack

import concourse.mybir as mybir
from concourse.masks import make_identity

E, K, D, C, NB = 256, 16, 512, 128, 8
NBC = NB * C
P = 128
FLOPS = 2 * E * K * D * C + 2 * E * K * NBC * D

F32 = mybir.dt.float32
BF16 = mybir.dt.bfloat16
U32 = mybir.dt.uint32
U8 = mybir.dt.uint8
FP8 = mybir.dt.float8_e4m3fn
FP8X4 = mybir.dt.float8_e4m3fn_x4
MULT = mybir.AluOpType.mult
ADD = mybir.AluOpType.add
SILU = mybir.ActivationFunctionType.Silu
COPY = mybir.ActivationFunctionType.Copy

TILES = 32
PAIRS = 16
HALF = 16


def tile_dimenettripletbilinear_kernel(tc, m_kj_bytes, m_kj_scale, m_ji, sbf, w_down, gain, w_bil, out):
    nc = tc.nc
    with ExitStack() as ctx:
        const = ctx.enter_context(tc.tile_pool(name="const", bufs=1))
        work = ctx.enter_context(tc.tile_pool(name="work", bufs=2))
        psum = ctx.enter_context(tc.psum_pool(name="psum", bufs=1))
        ctx.enter_context(tc.manual_schedule())

        mbytes, load_end = {}, {}

        def load_bytes(t0, t1):
            tiles = range(t0, t1)
            t_t = const.tile([P, len(tiles) * D], U8, name="mbytes%d" % t0, align_bytes=64)
            h = t0 // HALF
            nc.sync.dma_start(
                out=t_t[:].rearrange("e (k d) -> e k d", d=D), in_=m_kj_bytes[h * P:(h + 1) * P, t0 - h * HALF:t1 - h * HALF, :]
            )
            for i, t in enumerate(tiles):
                mbytes[t] = t_t[:, i * D:]
                load_end[t] = t1

        wb_hbm = w_bil.rearrange("(g p j) d -> g p j d", g=2, j=4)
        wb_raw = {}

        def load_wb(g, b0, b1):
            wb_t = const.tile([P, 4, (b1 - b0) * 256], BF16, name="wb_raw%d%d" % (g, b0), align_bytes=64)
            nc.sync.dma_start(out=wb_t[:], in_=wb_hbm[g][:, :, b0 * 256:b1 * 256])
            for b in range(b0, b1):
                wb_raw[g, b] = wb_t[:, :, (b - b0) * 256:(b - b0 + 1) * 256]

        scale4 = const.tile([P, 4], F32, name="scale4", align_bytes=64)
        wd_raw = const.tile([P, 4, C], BF16, name="wd_raw", align_bytes=64)
        gain8 = const.tile([P, 8], BF16, name="gain8", align_bytes=64)
        sbf_sb = const.tile([P, 2, K * NB], BF16, name="sbf_sb", align_bytes=64)
        mji = const.tile([P, 2, D], BF16, name="mji", align_bytes=64)
        load_bytes(0, 2)
        nc.scalar.dma_start(out=scale4[:], in_=m_kj_scale.rearrange("a b (p j) -> p (a b j)", j=4))
        load_bytes(2, 4)
        nc.sync.dma_start(out=wd_raw[:], in_=w_down.rearrange("(p j) c -> p j c", j=4))
        load_bytes(4, 8)
        nc.sync.dma_start(out=gain8[:], in_=gain.rearrange("(p j) -> p j", j=8))
        nc.sync.dma_start(out=sbf_sb[:], in_=sbf.rearrange("(h e) k n -> e h (k n)", e=P))
        load_wb(0, 0, 2)
        load_bytes(8, 12)
        load_wb(1, 0, 2)
        load_bytes(12, 16)
        load_bytes(16, 24)
        nc.sync.dma_start(out=mji[:], in_=m_ji.rearrange("(h e) d -> e h d", e=P))
        load_bytes(24, 32)

        ident = const.tile([P, P], F32, name="ident", align_bytes=64)
        make_identity(nc, ident[:])
        one = const.tile([P, 1], F32, name="one")
        nc.vector.memset(one[:], 1.0)
        warm = const.tile([P, 1], F32, name="warm")
        nc.scalar.activation(out=warm[:], in_=one[:], func=SILU)
        ident_bf = const.tile([P, P], BF16, name="ident_bf", align_bytes=64)
        nc.vector.tensor_copy(out=ident_bf[:], in_=ident[:])
        ident4 = const.tile([P, P], BF16, name="ident4", align_bytes=64)
        nc.vector.tensor_scalar(out=ident4[:], in0=ident[:], scalar1=4.0, scalar2=None, op0=MULT)

        free = []
        for i in range(7):
            bank_t = psum.tile([P, 512], F32, name="bank%d" % i)
            free.append(bank_t)

        def bank():
            return free.pop(0)

        scale_split = const.tile([P, D], F32, name="scale_split", align_bytes=64)

        def scale_spread():
            b_t = bank()
            for j in range(4):
                nc.tensor.transpose(b_t[:, j * P:(j + 1) * P], scale4[:, j:j + 1].to_broadcast([P, P]), ident[:])
            return b_t

        def scale_copy_split(b_t):
            nc.scalar.copy(out=scale_split[:].rearrange("q (u p e) -> q u p e", u=2, e=2), in_=b_t[:].rearrange("q (u e p) -> q u p e", u=2, e=2))
            free.append(b_t)

        gain_ps = psum.tile([P, 512], F32, name="gain_ps")

        def gain_spread():
            words = gain8[:].bitcast(F32)
            spread = gain_ps[:].rearrange("q (g u i o) -> q o u g i", g=2, u=2, o=2)
            for j in range(4):
                nc.tensor.transpose(spread[:, j // 2, j % 2], words[:, j:j + 1].to_broadcast([P, P]), ident[:])

        ring = []
        for i in range(3):
            ring_t = const.tile([P, 2 * D], BF16, name="ring%d" % i, align_bytes=64)
            ring.append(ring_t)
        wd_grp = ring[0][:, 0:D].rearrange("p (c j) -> p c j", j=4)
        wd_codes = const.tile([P, C], U32, name="wd_codes", align_bytes=64)
        wd_sc = const.tile([P, C], U8, name="wd_sc", align_bytes=64)

        def wd_interleave():
            for u in range(2):
                nc.vector.tensor_copy(
                    out=wd_grp.rearrange("p (u i e) j -> p u i e j", u=2, e=2)[:, u],
                    in_=wd_raw[:].rearrange("p j (i u e) -> p u i e j", u=2, e=2)[:, u],
                )

        def wd_quantise():
            nc.vector.quantize_mx(out=wd_codes[:].bitcast(FP8X4), scales=wd_sc[:], in_=ring[0][:, 0:D])

        wb_ps, wb_grp, wb_codes, wb_sc = {}, {}, [], []
        for g in range(2):
            codes_t = const.tile([P, D], U32, name="wb_codes%d" % g, align_bytes=64)
            sc_t = const.tile([P, D], U8, name="wb_sc%d" % g, align_bytes=64)
            wb_codes.append(codes_t)
            wb_sc.append(sc_t)

        def wb_interleave(g, b, i0=0, i1=2):
            b_t = bank() if i0 == 0 else wb_ps[g, b]
            for i in range(i0, i1):
                nc.tensor.matmul(
                    out=b_t[:].bitcast(BF16)[:, i * 512:(i + 1) * 512].rearrange("p (c i j) -> p c j i", i=8, j=4), lhsT=ident_bf[:],
                    rhs=wb_raw[g, b][:, :, i * P:(i + 1) * P].rearrange("p j (c i) -> p c j i", i=8), start=True, stop=True,
                )
            wb_ps[g, b] = b_t

        def wb_copy(engine, g, b):
            grp_t = const.tile([P, NBC], BF16, name="wb_grp%d%d" % (g, b), align_bytes=64)
            engine(out=grp_t[:], in_=wb_ps[g, b][:].bitcast(BF16))
            free.append(wb_ps[g, b])
            wb_grp[g, b] = grp_t

        def wb_quantise(g, b):
            cols = slice(b * 256, (b + 1) * 256)
            nc.vector.quantize_mx(out=wb_codes[g][:, cols].bitcast(FP8X4), scales=wb_sc[g][:, cols], in_=wb_grp[g, b][:])

        def wb_interleave_vector(g, b, d0, d1):
            if d0 == 0:
                grp_t = const.tile([P, NBC], BF16, name="wb_grp%d%d" % (g, b), align_bytes=64)
                wb_grp[g, b] = grp_t
            nc.vector.tensor_copy(out=wb_grp[g, b][:].rearrange("p (d j) -> p d j", j=4)[:, d0:d1], in_=wb_raw[g, b].rearrange("p j d -> p d j")[:, d0:d1])

        mtr, mcode, yps, xs, pts, ptr, pqs, pcode, mm, tts, aggs, head = ({} for a in range(12))
        widened = const.tile([P, TILES * D], BF16, name="widened", align_bytes=64)
        casts = [widened[:, j * 2 * D:(j + 1) * 2 * D] for j in range(PAIRS)]
        scaled01 = const.tile([P, 3 * D], BF16, name="scaled01", align_bytes=64)
        head_scaled = [scaled01[:, 0:D], scaled01[:, D:2 * D], ring[1][:, 0:D], scaled01[:, 2 * D:3 * D]]

        def cast_split(t):
            cols = slice(t % 2 * D, (t % 2 + 1) * D)
            nc.vector.tensor_scalar(
                out=casts[t // 2][:, cols].rearrange("p (u w e) -> p w u e", u=2, e=2),
                in0=mbytes[t][:, 0:D].bitcast(FP8).rearrange("p (w u e) -> p w u e", u=2, e=2), scalar1=one[:], scalar2=None, op0=MULT,
            )

        cast_done = [2 * D]

        def cast(n):
            c0 = cast_done[0]
            t = c0 // D
            c1 = min(c0 + n, load_end[t] * D)
            nc.scalar.copy(out=widened[:, c0:c1], in_=mbytes[t][:, c0 - t * D:c1 - t * D].bitcast(FP8))
            cast_done[0] = c1
            if c1 < min(c0 + n, TILES * D):
                cast(c0 + n - c1)

        def product_gpsimd(j):
            assert cast_done[0] >= (j + 1) * 2 * D
            nc.gpsimd.tensor_tensor(
                out=ring[(j + 1) % 3][:].rearrange("p (u a w e) -> p u a w e", u=2, a=2, e=2),
                in0=casts[j].rearrange("p (a w u e) -> p u a w e", a=2, u=2, e=2),
                in1=scale_split[:].rearrange("p (u w e) -> p u w e", u=2, e=2).unsqueeze(2).to_broadcast([P, 2, 2, P, 2]), op=MULT,
            )

        def m_transpose(j):
            b_t = bank()
            words = ring[(j + 1) % 3][:].bitcast(F32)
            for i in range(4):
                nc.tensor.transpose(b_t[:, i * P:(i + 1) * P], words[:, i * P:(i + 1) * P], ident[:])
            mtr[j] = b_t

        def m_copy(j):
            nc.scalar.copy(out=ring[j % 3][:].bitcast(F32).rearrange("p (r u) -> p r u", u=2), in_=mtr[j][:].rearrange("p (u r) -> p r u", u=2))
            free.append(mtr[j])

        def m_quant(j, a0, a1):
            if j not in mcode:
                mc_t = work.tile([P, 2 * P], U32, name="mc", bufs=2, align_bytes=64)
                ms_t = work.tile([P, 2 * P], U8, name="ms", bufs=2, align_bytes=64)
                mcode[j] = (mc_t, ms_t)
            cols = slice(a0 * P, a1 * P)
            nc.vector.quantize_mx(out=mcode[j][0][:, cols].bitcast(FP8X4), scales=mcode[j][1][:, cols], in_=head_scaled[2 * j + a0] if j < 2 else ring[j % 3][:])

        def stage1(j, a0, a1):
            y_t = bank()
            mc_t, ms_t = mcode[j]
            for a in range(a0, a1):
                cols = slice(a * P, (a + 1) * P)
                nc.tensor.matmul_mx(
                    out=y_t[:, cols], lhsT=mc_t[:, cols].bitcast(FP8X4), lhsT_scale=ms_t[:, cols],
                    rhs=wd_codes[:].bitcast(FP8X4), rhs_scale=wd_sc[:], start=True, stop=True,
                )
            yps[j] = y_t

        def silu1(j, a0, a1):
            x_t = work.tile([P, 2 * C], F32, name="x", bufs=3, align_bytes=64)
            cols = slice(a0 * P, a1 * P)
            nc.scalar.activation(out=x_t[:, cols], in_=yps[j][:, cols], func=SILU)
            free.append(yps[j])
            for a in range(a0, a1):
                xs[2 * j + a] = x_t[:, a * P:(a + 1) * P].rearrange("p (u w) -> p u w", u=2)

        gain_bf = gain_ps[:].bitcast(BF16).rearrange("p (g u n w) -> p g u n w", g=2, u=2, n=4)
        sbf_cols = sbf_sb[:].rearrange("p h k -> p (h k)")

        def p_ops(t, n0=0, n1=NB):
            if n0 == 0:
                p_t = work.tile([P, NBC], BF16, name="pt", bufs=3, align_bytes=64)
                pts[t] = p_t
            view = pts[t][:].rearrange("p (g u n w) -> p g u n w", g=2, u=2, n=4)
            for n in range(n0, n1):
                col = t * NB + n
                nc.vector.scalar_tensor_tensor(
                    out=view[:, n // 4, :, n % 4, :], in0=xs[t], scalar=sbf_cols[:, col:col + 1],
                    in1=gain_bf[:, n // 4, :, n % 4, :], op0=MULT, op1=MULT,
                )

        def p_transpose(t, g0, g1):
            words = pts[t][:].bitcast(F32)
            b_t = bank()
            for a in range(2 * g0, 2 * g1):
                nc.tensor.transpose(b_t[:, a * P:(a + 1) * P], words[:, a * P:(a + 1) * P], ident[:])
            ptr[t, g0] = b_t

        groups = [(0,)] + [(2 * c - 1, 2 * c) for c in range(1, PAIRS - 1)] + [(t,) for t in range(TILES - 3, TILES)]

        def p_copy(engine, t, g0, g1):
            c = [t in grp for grp in groups].index(True)
            a, width = groups[c].index(t), len(groups[c])
            if a == 0 and g0 == 0:
                pq_t = work.tile([P, 2 * NBC], BF16, name="pq", bufs=3, align_bytes=64)
                pqs[c] = pq_t
            dst = pqs[c][:, 0:width * NBC].bitcast(F32).rearrange("p (g a r u) -> p g a r u", g=2, a=width, u=2)[:, g0:g1, a]
            engine(out=dst, in_=ptr[t, g0][:].rearrange("p (g u r) -> p g r u", g=2, u=2)[:, g0:g1])
            free.append(ptr[t, g0])

        def p_quant(c, g0, g1):
            if g0 == 0:
                pc_t = work.tile([P, 4 * P], U32, name="pc", bufs=4, align_bytes=64)
                ps_t = work.tile([P, 4 * P], U8, name="ps", bufs=4, align_bytes=64)
                pcode[c] = (pc_t, ps_t)
            n = len(groups[c]) * P
            cols = slice(g0 * n, g1 * n)
            nc.vector.quantize_mx(out=pcode[c][0][:, cols].bitcast(FP8X4), scales=pcode[c][1][:, cols], in_=pqs[c][:, 4 * g0 * n:4 * g1 * n])

        def stage2(c, d0, d1):
            mm_t = bank()
            pc_t, ps_t = pcode[c]
            n = len(groups[c]) * P
            for d in range(d0, d1):
                cols = slice(d * P, (d + 1) * P)
                for g in range(2):
                    toks = slice(g * n, (g + 1) * n)
                    nc.tensor.matmul_mx(
                        out=mm_t[:, (d - d0) * n:(d - d0 + 1) * n], lhsT=wb_codes[g][:, cols].bitcast(FP8X4), lhsT_scale=wb_sc[g][:, cols],
                        rhs=pc_t[:, toks].bitcast(FP8X4), rhs_scale=ps_t[:, toks], start=(g == 0), stop=(g == 1),
                    )
            mm[c, d0] = mm_t

        def stage2_turned(c, d0, d1, g):
            if g == 0:
                mm[c, d0] = bank()
            toks, cols = slice(g * P, (g + 1) * P), slice(d0 * P, d1 * P)
            nc.tensor.matmul_mx(
                out=mm[c, d0][:, 0:(d1 - d0) * P], lhsT=pcode[c][0][:, toks].bitcast(FP8X4), lhsT_scale=pcode[c][1][:, toks],
                rhs=wb_codes[g][:, cols].bitcast(FP8X4), rhs_scale=wb_sc[g][:, cols], start=(g == 0), stop=(g == 1),
            )

        def silu2(c, d0, width):
            if d0 == 0:
                t_t = work.tile([P, 8 * P], F32, name="tt", bufs=4, align_bytes=64)
                tts[c] = t_t
            first = d0 * len(groups[c]) * P
            tts[c, d0] = tts[c][:, first:first + width]
            free.append(mm[c, d0])
            nc.scalar.activation(out=tts[c, d0][:, 0:width], in_=mm[c, d0][:, 0:width], func=SILU)

        def agg_open(h):
            agg_t = bank()
            nc.tensor.matmul(out=agg_t[:], lhsT=ident4[:], rhs=mji[:, h, :], start=True, stop=False)
            aggs[h] = agg_t

        last_summed = (HALF - 1, TILES - 4)

        def k_sum(c, d0, d1):
            width = len(groups[c])
            for d in range(d0, d1):
                for a, t in enumerate(groups[c]):
                    i = (d - d0) * width + a
                    nc.tensor.matmul(
                        out=aggs[t // HALF][:, d * P:(d + 1) * P], lhsT=tts[c, d0][:, i * P:(i + 1) * P], rhs=ident[:],
                        is_transpose=True, start=False, stop=(t in last_summed and d == 3),
                    )

        pre = {}

        def pair_add(c, dst):
            both = tts[c][:].rearrange("p (d a e) -> p d a e", d=4, a=2)
            nc.gpsimd.tensor_tensor(out=dst.rearrange("p (d e) -> p d e", d=4), in0=both[:, :, 0], in1=both[:, :, 1], op=ADD)
            pre[c] = dst

        def k_sum_added(c):
            for d in range(4):
                cols = slice(d * P, (d + 1) * P)
                nc.tensor.matmul(out=aggs[1][:, cols], lhsT=pre[c][:, cols], rhs=ident[:], is_transpose=True, start=False, stop=False)

        sums = []
        for h in range(2):
            sum_t = const.tile([P, D], F32, name="sum%d" % h, align_bytes=64)
            sums.append(sum_t)

        def agg_close(h, d0, d1):
            cols = slice(d0 * P, d1 * P)
            nc.scalar.activation(out=sums[h][:, cols], in_=aggs[h][:, cols], func=COPY, scale=0.25)
            if d1 == 4:
                free.append(aggs[h])

        def add_turned(dst, c, first, d0, d1, src):
            cols = slice(d0 * P, d1 * P)
            nc.vector.scalar_tensor_tensor(out=dst[:, cols], in0=tts[c, first][:, (d0 - first) * P:(d1 - first) * P], scalar=0.25, in1=src[:, cols], op0=MULT, op1=ADD)

        def scale_turned(dst, c, d0, d1):
            nc.scalar.activation(out=dst[:, d0 * P:d1 * P], in_=tts[c, d0], func=COPY, scale=0.25)

        def add_sum(dst, h, d0, d1, src):
            cols = slice(d0 * P, d1 * P)
            nc.vector.scalar_tensor_tensor(out=dst[:, cols], in0=aggs[h][:, cols], scalar=0.25, in1=src[:, cols], op0=MULT, op1=ADD)

        def head_transpose(t):
            b_t = bank()
            words = casts[t // 2][:, t % 2 * D:(t % 2 + 1) * D].bitcast(F32)
            for u in range(2):
                half = words[:, u * P:(u + 1) * P] if t < 2 else words[:, u:256:2]
                nc.tensor.transpose(b_t[:, u * P:(u + 1) * P], half, ident[:])
            head[t] = b_t

        def head_product(t):
            nc.vector.tensor_tensor(
                out=head_scaled[t].rearrange("p (r u e) -> p r u e", u=2, e=2),
                in0=head[t][:, 0:256].bitcast(BF16).rearrange("p (u r e) -> p r u e", u=2, e=2),
                in1=scale4[:].rearrange("p (u e) -> p u e", u=2).unsqueeze(1).to_broadcast([P, P, 2, 2]), op=MULT,
            )
            free.append(head[t])

        with29 = const.tile([P, D], F32, name="with29", align_bytes=64)
        with30 = const.tile([P, D], F32, name="with30", align_bytes=64)
        o_last = []
        for i in range(2):
            o_t = const.tile([P, D], F32, name="o%d" % i, align_bytes=64)
            o_last.append(o_t)

        scale_bank = scale_spread()
        cast_split(0)
        cast_split(1)
        head_transpose(0)
        head_transpose(1)
        cast(1024)
        scale_copy_split(scale_bank)
        wd_interleave()
        head_transpose(2)
        head_transpose(3)
        gain_spread()
        cast(1024)
        head_product(0)
        head_product(1)
        wd_quantise()
        product_gpsimd(2)
        m_quant(0, 0, 1)
        m_quant(0, 1, 2)
        cast(1024)
        stage1(0, 0, 1)
        silu1(0, 0, 1)
        stage1(0, 1, 2)
        silu1(0, 1, 2)
        head_product(2)
        head_product(3)
        wb_interleave(0, 0)
        wb_interleave(0, 1)
        p_ops(0)
        cast(1024)
        cast(1024)
        wb_copy(nc.scalar.copy, 0, 0)
        cast(1024)
        cast(512)
        m_quant(1, 0, 1)
        product_gpsimd(3)
        m_quant(1, 1, 2)
        stage1(1, 0, 2)
        p_transpose(0, 0, 2)
        m_transpose(2)
        silu1(1, 0, 2)
        wb_copy(nc.scalar.copy, 0, 1)
        wb_interleave(1, 0)
        p_copy(nc.scalar.copy, 0, 0, 2)
        m_copy(2)
        cast(512)
        wb_copy(nc.scalar.copy, 1, 0)
        p_ops(1)
        p_transpose(1, 0, 2)
        p_ops(2)
        wb_quantise(0, 0)
        m_quant(2, 0, 2)
        product_gpsimd(4)
        wb_quantise(0, 1)
        p_quant(0, 0, 2)
        p_copy(nc.scalar.copy, 1, 0, 2)
        cast(512)
        m_transpose(3)
        p_transpose(2, 0, 2)
        stage1(2, 0, 2)
        wb_interleave(1, 1)
        silu1(2, 0, 2)
        p_copy(nc.scalar.copy, 2, 0, 2)
        m_copy(3)
        wb_copy(nc.scalar.copy, 1, 1)
        cast(1024)
        p_ops(3)
        p_transpose(3, 0, 2)
        agg_open(0)
        p_ops(4)
        wb_quantise(1, 0)
        wb_quantise(1, 1)
        m_quant(3, 0, 2)
        product_gpsimd(5)
        p_quant(1, 0, 2)
        p_copy(nc.scalar.copy, 3, 0, 2)
        cast(704)
        m_transpose(4)
        p_transpose(4, 0, 2)
        stage1(3, 0, 2)
        stage2(0, 0, 4)
        silu1(3, 0, 2)
        p_copy(nc.scalar.copy, 4, 0, 2)
        m_copy(4)
        silu2(0, 0, 512)
        stage2(1, 0, 2)
        stage2(1, 2, 4)
        cast(768)
        silu2(1, 0, 512)
        silu2(1, 2, 512)
        p_ops(5)
        k_sum(0, 0, 4)
        p_transpose(5, 0, 2)
        p_ops(6)

        for j in range(4, PAIRS - 2):
            m_quant(j, 0, 2)
            product_gpsimd(j + 2)
            p_quant(j - 2, 0, 2)
            p_copy(nc.scalar.copy, 2 * j - 3, 0, 2)
            m_transpose(j + 1)
            p_transpose(2 * j - 2, 0, 2)
            stage1(j, 0, 2)
            silu1(j, 0, 2)
            p_copy(nc.scalar.copy, 2 * j - 2, 0, 2)
            m_copy(j + 1)
            if cast_done[0] < TILES * D:
                cast(576)
            stage2(j - 2, 0, 2)
            stage2(j - 2, 2, 4)
            silu2(j - 2, 0, 512)
            silu2(j - 2, 2, 512)
            if j == 9:
                agg_open(1)
            p_ops(2 * j - 1)
            k_sum(j - 3, 0, 2)
            k_sum(j - 3, 2, 4)
            p_transpose(2 * j - 1, 0, 2)
            p_ops(2 * j)

        m_quant(14, 0, 2)
        p_quant(12, 0, 2)
        m_transpose(15)
        p_transpose(26, 0, 2)
        p_copy(nc.scalar.copy, 25, 0, 2)
        stage1(14, 0, 2)
        p_copy(nc.scalar.copy, 26, 0, 2)
        silu1(14, 0, 2)
        m_copy(15)
        stage2(12, 0, 2)
        stage2(12, 2, 4)
        silu2(12, 0, 512)
        pair_add(11, ring[2][:].bitcast(F32))
        p_ops(27)
        p_quant(13, 0, 2)
        m_quant(15, 0, 2)
        p_transpose(27, 0, 2)
        silu2(12, 2, 512)
        pair_add(12, ring[0][:].bitcast(F32))
        p_copy(nc.scalar.copy, 27, 0, 2)
        p_ops(28)
        stage2(13, 0, 2)
        stage1(15, 0, 2)
        stage2(13, 2, 4)
        silu2(13, 0, 512)
        silu1(15, 0, 2)
        p_transpose(28, 0, 1)
        p_transpose(28, 1, 2)
        p_copy(nc.scalar.copy, 28, 0, 1)
        p_copy(nc.scalar.copy, 28, 1, 2)
        silu2(13, 2, 512)
        k_sum_added(11)
        k_sum(13, 0, 2)
        k_sum_added(12)
        p_ops(29)
        p_quant(14, 0, 2)
        p_transpose(29, 0, 2)
        k_sum(13, 2, 4)
        p_copy(nc.scalar.copy, 29, 0, 2)
        agg_close(0, 0, 4)
        nc.sync.dma_start(out=out[0:P, :], in_=sums[0][:])
        stage2(14, 0, 2)
        stage2(14, 2, 4)
        silu2(14, 0, 512)
        p_ops(30)
        p_quant(15, 0, 2)
        p_transpose(30, 0, 1)
        p_transpose(30, 1, 2)
        silu2(14, 2, 512)
        p_copy(nc.scalar.copy, 30, 0, 1)
        p_copy(nc.scalar.copy, 30, 1, 2)
        stage2_turned(15, 0, 2, 0)
        stage2_turned(15, 0, 2, 1)
        stage2_turned(15, 2, 4, 0)
        stage2_turned(15, 2, 4, 1)
        p_ops(31)
        p_quant(16, 0, 1)
        p_quant(16, 1, 2)
        p_transpose(31, 0, 1)
        k_sum(14, 0, 2)
        p_transpose(31, 1, 2)
        k_sum(14, 2, 4)
        silu2(15, 0, 256)
        silu2(15, 2, 256)
        scale_turned(sums[1], 15, 0, 2)
        scale_turned(sums[1], 15, 2, 4)
        p_copy(nc.vector.tensor_copy, 31, 0, 1)
        p_copy(nc.vector.tensor_copy, 31, 1, 2)
        stage2_turned(16, 0, 2, 0)
        stage2_turned(16, 0, 2, 1)
        stage2_turned(16, 2, 4, 0)
        stage2_turned(16, 2, 4, 1)
        p_quant(17, 0, 1)
        p_quant(17, 1, 2)
        silu2(16, 0, 256)
        silu2(16, 2, 256)
        stage2_turned(17, 0, 1, 0)
        stage2_turned(17, 1, 2, 0)
        stage2_turned(17, 2, 3, 0)
        stage2_turned(17, 3, 4, 0)
        stage2_turned(17, 0, 1, 1)
        stage2_turned(17, 1, 2, 1)
        stage2_turned(17, 2, 3, 1)
        stage2_turned(17, 3, 4, 1)
        add_sum(with29, 1, 0, 2, sums[1])
        add_sum(with29, 1, 2, 4, sums[1])
        add_turned(with30, 16, 0, 0, 2, with29)
        add_turned(with30, 16, 2, 2, 4, with29)
        silu2(17, 0, 128)
        add_turned(o_last[0], 17, 0, 0, 1, with30)
        nc.sync.dma_start(out=out[P:2 * P, 0 * P:1 * P], in_=o_last[0][:, 0 * P:1 * P])
        silu2(17, 1, 128)
        add_turned(o_last[1], 17, 1, 1, 2, with30)
        nc.sync.dma_start(out=out[P:2 * P, 1 * P:2 * P], in_=o_last[1][:, 1 * P:2 * P])
        silu2(17, 2, 128)
        add_turned(o_last[0], 17, 2, 2, 3, with30)
        nc.sync.dma_start(out=out[P:2 * P, 2 * P:3 * P], in_=o_last[0][:, 2 * P:3 * P])
        silu2(17, 3, 128)
        add_turned(o_last[1], 17, 3, 3, 4, with30)
        nc.sync.dma_start(out=out[P:2 * P, 3 * P:4 * P], in_=o_last[1][:, 3 * P:4 * P])
